import numpy as np, ml_dtypes
CORES = [242,247,114,119]
N = 4
BF = ml_dtypes.bfloat16
def gentries(a):
    return np.ascontiguousarray(a.reshape(8, 16, -1).transpose(0, 2, 1)).reshape(8, -1)
def gtable(e):
    e = np.asarray(e); return np.ascontiguousarray(e.reshape(8, -1, 16).transpose(0, 2, 1)).reshape(128, -1).astype(np.int32)
P, BS, T, CAP, G = 2368, 256, 4, 160, 128
S, SB, NEED, KILL = 2, 1, 8, 3
W = P + (N - 1) * G
def clans(rng, kk):
    sc = rng.choice(np.array([191.0, 120.0, 60.0], np.float32), (8, 1, 1)); cen = (sc * rng.random((8, 16, 4))).astype(np.float32); cen[:, :, 0] *= np.float32(0.1)
    t = np.maximum(1, (sc * (0.06 + 0.08 * rng.random((N, 8, 16, 1)))).astype(np.int32)); off = rng.integers(0, 4, (8, 1))
    def near():
        who = ((rng.random((N, 8, P)) * kk[:, None]).astype(np.int64) + off) & 3
        w = sc * (np.float32(0.05) + np.float32(0.15) * rng.random((N, 8, 1, P), dtype=np.float32))
        v = np.take_along_axis(np.broadcast_to(cen, (N, 8, 16, 4)), who[:, :, None, :], 3) + w * (2 * rng.random((N, 8, 16, P), dtype=np.float32) - 1)
        return np.clip(np.rint(v), 0, 191).astype(np.int32)
    x = near(); share = KILL * kk[:, None, None] * rng.choice(np.array([0.03, 0.06, 0.09]), (N, 8, 1, 1))
    y = np.where(rng.random((N, 8, 1, P)) < 0.1, 255, rng.integers(0, 192, (N, 8, 16, P), dtype=np.int32))
    return x, np.where(rng.random((N, 8, 1, P)) < share, near(), y), t
def chosen(key):
    return np.ascontiguousarray(np.argsort(key, axis=-1)[..., :16 * BS])
def deal(pts, num):
    a = np.empty((16, BS), np.int64); a[:, pts] = num.reshape(BS, 16).T
    return a.reshape(-1)
def parts(rng):
    x, y, t = clans(rng, rng.permutation(np.array([1, 1, 2, 2, 2, 3, 3, 4])))
    sd = rng.random((N, 8, BS)) < rng.choice(np.array([0.2, 0.4, 0.6, 0.9]), (N, 8, 1))
    c = chosen(rng.random((N, 8, T, S * W), dtype=np.float32))
    b = np.argsort(rng.random((N, 8, P)) * np.where(np.arange(P) < T * BS, 0.6, 1.0), axis=-1)[..., :(N - 1) * G]
    return x, y, t, sd, c, np.ascontiguousarray(b)
def pack(x, y, t, sd, c, b):
    c = c.reshape(N, 8, T, 16, BS).transpose(0, 1, 3, 2, 4).reshape(N, 128, T * BS)
    return {"x": x.reshape(N, 128, P).astype(np.float32).astype(BF), "y0": y.reshape(N, 128, P).astype(np.float32).astype(BF),
            "tl": t.reshape(N, 128, 1).astype(np.float32).astype(BF), "sd": sd.astype(np.float32).astype(BF),
            "cd": np.ascontiguousarray(c).astype(np.int32), "snd": np.stack([gtable(a) for a in b])}
def setup_inputs(rng):
    return pack(*parts(rng))
def setup_inputs_room(rng):
    x, y, t, sd, c, b = parts(rng)
    o = np.argsort(np.argsort(rng.random((N, 8, BS)), axis=-1), axis=-1); n = rng.choice(np.array([0, 1, CAP - 1, CAP, CAP + 1, BS]), (N, 8))
    n[0] = (CAP, CAP + 1, BS, CAP - 1, 1, 0, CAP, BS); n[1] = (BS, CAP, CAP + 1, CAP, CAP - 1, CAP, 0, 1)
    return pack(x, y, t, o < n[..., None], c, b)
def setup_inputs_ties(rng):
    x, y, t, sd, c, b = parts(rng)
    t = np.tile(rng.integers(0, 21, (1, 8, 16, 1)), (N, 1, 1, 1)); base = rng.integers(10, 121, (8, 16, 1))
    def step():
        return base + t * rng.integers(0, 3, (N, 8, 16, P), dtype=np.int32) + (rng.random((N, 8, 16, P), dtype=np.float32) < 0.3)
    x = step(); y = np.where(rng.random((N, 8, 1, P)) < 0.1 * KILL, step(), 255)
    t[:, 0] = 63; x[:, 0] = rng.choice(np.array([127, 128, 191]), (N, 16, P)); y[:, 0] = rng.choice(np.array([255, 255, 255, 191, 128, 64]), (N, 16, P))
    return pack(x, y, t, sd, c, b)
def setup_inputs_ends(rng):
    x, y, t, sd, c, b = parts(rng); a = np.arange(S * W); n = np.arange(BS); k = np.arange((N - 1) * G)
    key = rng.random((N, 8, T, S * W), dtype=np.float32)
    key[:, 1::2, :, S * P:] -= 1; key[:, 1::2, :, :S] -= 1; key[:, 1::2, :, S * (P - 1):S * P] -= 1
    key[:, 2] += (a >= 16 * BS).astype(np.float32); key[:, 4] += (a < S * W - 16 * BS).astype(np.float32)
    c = rng.permuted(chosen(key), axis=-1); c[:, 6] = np.arange(16 * BS)
    b[:, 1] = k; b[:, 3] = P - 1 - k; b[:, 7] = T * BS - (N - 1) * G + k
    sd[:, ::2] = n >= BS - CAP; sd[:, 1::2] = (n & 1) == 0; sd[:, 5] = (n == 0) | (n == BS - 1)
    return pack(x, y, t, sd, c, b)
def setup_inputs_dark(rng):
    x, y, t, sd, c, b = parts(rng); q = rng.permutation(N); g = rng.permutation(8)
    y[:, g[1]] = 255; t[:, g[2]] = 0
    for j in g[3:7]:
        x[:, j] = x[:, j] & 31; t[:, j] = 63
    y[:, g[3]] = y[:, g[3]] & 31; y[:, g[4]] = 128 + (y[:, g[4]] & 63)
    for r in range(N):
        m = np.isin(np.arange(BS) & 15, rng.permutation(16)[:16 * CAP // BS]); sd[r, g[4]] = m
        num = np.concatenate([rng.permutation(np.arange(S * P, S * W)), np.arange(16 * BS - S * (W - P))])
        c[r, g[4], 0] = deal(np.argsort(rng.random(BS) - m), num)
        m = rng.permutation(BS) < CAP; sd[r, g[5]] = m; o = rng.permutation(16)
        pl = np.argsort(o[np.arange(W) & 15] + rng.random(W))[:16 * CAP]; num = rng.permutation(S * pl + rng.integers(0, S, 16 * CAP))
        num = np.concatenate([num, rng.permutation(np.setdiff1d(np.arange(S * W), num))])[:16 * BS]
        c[r, g[5], 0] = deal(np.argsort(rng.random(BS) - m), num)
    c[:, g[4], 1:] = rng.permuted(np.tile(np.arange(16 * BS), (N, T - 1, 1)), axis=-1)
    key = rng.random((N, S * W)); key[:, S * BS:2 * S * BS] += 1; c[:, g[6], 0] = chosen(key)
    b[:, g[6]] = np.argsort(rng.random((N, P)) + (np.arange(P) // BS == 1), axis=-1)[:, :(N - 1) * G]
    sd[:, g[0]] = False; sd[q[0]] = False; sd[q[1], g[3]] = True
    return pack(x, y, t, sd, c, b)
def setup_inputs_spread(rng):
    x, y, t, sd, c, b = parts(rng)
    x = np.minimum((np.exp2(7.59 * rng.random((N, 8, 1, P))) * rng.random((N, 8, 16, P))).astype(np.int32), 191)
    y = np.minimum((np.exp2(7.59 * rng.random((N, 8, 1, P))) * rng.random((N, 8, 16, P))).astype(np.int32), 191)
    y = np.where(rng.random((N, 8, 1, P)) < rng.choice(np.array([0.1, 0.5, 0.9]), (N, 8, 1, 1)), 255, y)
    low = np.arange(16)[:, None] == rng.integers(0, 16, (N, 8, 1, P))
    y = np.where(rng.random((N, 8, 1, P)) < 0.15, np.where(low, y >> 3, 255), y)
    t = np.rint(np.exp2(6 * rng.random((N, 8, 16, 1)))).astype(np.int32) - 1
    return pack(x, y, np.minimum(t, 63), rng.random((N, 8, BS)) < rng.random((N, 8, 1)), c, b)
def check_inputs(d):
    bad = []
    for k, hi in (("x", 191), ("y0", 191), ("tl", 63), ("sd", 1)):
        v = np.asarray(d[k]).astype(np.float32); ok = (v >= 0) & (v <= hi) & (v == np.floor(v))
        if k == "y0": ok = ok | (v == 255)
        if not np.all(ok): bad.append("range of " + k)
    for k, hi in (("cd", S * W - 1), ("snd", P - 1)):
        if np.min(d[k]) < 0 or np.max(d[k]) > hi: bad.append("range of " + k)
    c = np.sort(np.asarray(d["cd"]).reshape(N, 8, 16, T, BS).transpose(0, 1, 3, 2, 4).reshape(N, 8, T, 16 * BS), axis=-1)
    if np.any(c[..., 1:] == c[..., :-1]): bad.append("equal numbers in a brood of cd")
    s = np.sort(np.stack([gentries(a) for a in d["snd"]]), axis=-1)
    if np.any(s[..., 1:] == s[..., :-1]): bad.append("equal numbers in snd")
    return bad
def windows(a, sl):
    res = []
    for r in range(N):
        w = [a[r]]
        for d in range(1, N):
            q = (r - d) % N; w.append(np.take_along_axis(a[q], sl[q, :, d - 1][:, None, :], 2))
        res.append(np.concatenate(w, axis=2))
    return np.stack(res)
def matches(come, xn, t):
    return np.add.reduce((np.abs(come - xn[:, None, :]) <= t[:, :, None]).astype(np.int64), axis=0) >= NEED
def reference(x, y0, tl, sd, cd, snd):
    X = x.astype(np.float32).astype(np.int32).reshape(N, 8, 16, P); Y = y0.astype(np.float32).astype(np.int32).reshape(N, 8, 16, P)
    t = tl.astype(np.float32).astype(np.int32).reshape(N, 8, 16, 1)
    C = (cd.astype(np.int64) >> SB).reshape(N, 8, 16, T * BS); sl = np.stack([gentries(a) for a in snd]).astype(np.int64).reshape(N, 8, N - 1, G)
    flag = np.zeros((N, 8, P), bool); flag[:, :, :BS] = sd.astype(np.float32) > 0.5; member = np.zeros((N, 8, P), bool)
    xw = windows(X, sl)
    for s in range(T):
        fl = flag[:, :, s * BS:(s + 1) * BS]
        member[:, :, s * BS:(s + 1) * BS] = fl & (np.add.accumulate(fl.astype(np.int64), axis=2) <= CAP)
        new = np.zeros((N, 8, W), bool)
        for r in range(N):
            for g in range(8):
                n = np.flatnonzero(member[r, g, s * BS:(s + 1) * BS]) + s * BS; c = C[r, g][:, n]
                come = xw[r, g][:, c.reshape(-1)].reshape(16, 16, len(n))
                new[r, g][c[matches(come, X[r, g][:, n], t[r, g])]] = True
        for r in range(N):
            flag[r] |= new[r, :, :P]
            for d in range(1, N):
                q = (r - d) % N
                for g in range(8): flag[q, g, sl[q, g, d - 1][new[r, g, P + (d - 1) * G:P + d * G]]] = True
    for s in range(T - 1, -1, -1):
        yw = windows(Y, sl); Z = Y.copy()
        for r in range(N):
            for g in range(8):
                n = np.flatnonzero(member[r, g, s * BS:(s + 1) * BS]) + s * BS; c = C[r, g][:, n]; xn = X[r, g][:, n]
                come = yw[r, g][:, c.reshape(-1)].reshape(16, 16, len(n))
                dead = np.add.reduce(matches(come, xn, t[r, g]).astype(np.int64), axis=0) >= KILL
                Z[r, g][:, n] = np.where(dead, 255, (xn + np.minimum(191, np.minimum.reduce(come, axis=1))) >> 1)
        Y = Z
    return {"yv": np.ascontiguousarray(Y[:, :, :, :T * BS]).reshape(N, 128, T * BS).astype(np.float32).astype(BF), "yf": np.where(member, 2, flag.astype(np.int64)).astype(np.float32).astype(BF)}

@@ -1,0 +1,423 @@
+from concourse.bass import DstId, RemoteDMATransfer
+from concourse.mybir import AluOpType as OP, ActivationFunctionType as AF
+
+N, P, BS, T4, CAP, GB, S2 = 4, 2368, 256, 4, 160, 128, 2
+NB = (N - 1) * GB
+W = P + NB
+ST = S2 * W
+MA = 96
+MB = CAP - MA
+EA, EB, E = 16 * MA, 16 * MB, 16 * CAP
+SWN = 2 * ST + E
+VS, VS3 = 88, 76
+SIN = 16 * 96
+SLOT = 768
+XSH = 14
+XDEF = 512
+LW = 148
+
+SCRATCH = {
+    "xw": ("sbuf", [128, W], "bfloat16"), "yw": ("sbuf", [128, P + 4 * NB], "bfloat16"),
+    "cdw": ("sbuf", [128, T4 * BS], "int32"), "snd32": ("sbuf", [128, NB // 16], "int32"),
+    "sndw": ("sbuf", [128, NB // 16], "uint16"), "tlc": ("sbuf", [128, 1], "bfloat16"), "sdrow": ("sbuf", [128, BS], "bfloat16"),
+    "swv": ("sbuf", [128, SWN], "bfloat16"), "sws": ("sbuf", [128, SWN], "float32"),
+    "swc": ("sbuf", [128, 2 * P], "bfloat16"), "swb": ("sbuf", [128, 2 * NB], "bfloat16"), "swo": ("sbuf", [128, 2 * BS], "bfloat16"),
+    "ones": ("sbuf", [128, 16], "bfloat16"), "sin": ("sbuf", [128, SIN], "float32"),
+    "come": ("sbuf", [128, E], "bfloat16"), "ab": ("sbuf", [128, E], "bfloat16"), "ind": ("sbuf", [128, E], "bfloat16"),
+    "mn": ("sbuf", [128, E], "bfloat16"), "d0": ("sbuf", [128, E], "bfloat16"),
+    "pk": ("sbuf", [128, T4 * BS], "int32"), "pkc": ("sbuf", [128, T4 * SLOT], "int32"),
+    "pkd0": ("sbuf", [128, CAP], "int32"), "pkd": ("sbuf", [128, CAP], "int32"),
+    "sel": ("sbuf", [128, 16 * 128], "bfloat16"), "qp": ("sbuf", [128, 128], "bfloat16"), "bd": ("sbuf", [128, 128], "bfloat16"),
+    "tri": ("sbuf", [128, 128], "bfloat16"), "idn": ("sbuf", [128, 128], "bfloat16"), "idx": ("sbuf", [128, 128], "bfloat16"),
+    "pmi": ("sbuf", [128, 1], "int32"), "pm2": ("sbuf", [128, 1], "int32"), "pmod": ("sbuf", [128, 1], "float32"),
+    "nmod": ("sbuf", [128, BS], "bfloat16"), "mask": ("sbuf", [128, BS], "bfloat16"), "seg0": ("sbuf", [128, BS], "bfloat16"),
+    "c16": ("sbuf", [128, 16], "float32"), "nrow": ("sbuf", [128, 16], "bfloat16"), "nc": ("sbuf", [128, 16], "float32"),
+    "i384": ("sbuf", [128, NB], "bfloat16"), "bp": ("sbuf", [128, P], "bfloat16"), "bposw": ("sbuf", [128, 48], "uint16"),
+    "fw": ("sbuf", [128, 64], "bfloat16"), "fb": ("sbuf", [128, BS], "bfloat16"), "fsc": ("sbuf", [128, BS], "bfloat16"),
+    "nown": ("sbuf", [128, 64], "bfloat16"), "cs": ("sbuf", [128, 32], "bfloat16"), "tp": ("sbuf", [128, 16], "float32"),
+    "of32": ("sbuf", [128, 16], "float32"), "offs": ("sbuf", [128, 64], "uint16"),
+    "shf": ("sbuf", [128, T4 * CAP], "int32"), "lst": ("sbuf", [128, T4 * CAP], "uint16"), "lsb": ("sbuf", [128, T4 * CAP], "uint16"),
+    "lf": ("sbuf", [128, CAP], "float32"), "lg": ("sbuf", [128, CAP], "float32"),
+    "xi": ("sbuf", [128, CAP], "int32"), "xmn": ("sbuf", [128, T4 * CAP], "bfloat16"), "vi": ("sbuf", [128, CAP], "int32"),
+    "nq": ("sbuf", [128, CAP], "float32"), "so": ("sbuf", [128, CAP], "float32"), "sof": ("sbuf", [128, CAP], "uint16"),
+    "mt": ("sbuf", [128, CAP], "bfloat16"), "dd": ("sbuf", [128, CAP], "float32"), "hs": ("sbuf", [128, CAP], "int32"),
+    "hv": ("sbuf", [128, CAP], "int32"), "vals": ("sbuf", [128, T4 * SLOT], "bfloat16"), "yb": ("sbuf", [128, T4 * BS], "bfloat16"),
+    "memc": ("sbuf", [128, SLOT], "bfloat16"), "memn": ("sbuf", [128, SLOT], "bfloat16"),
+    "memr": ("sbuf", [128, T4 * BS], "bfloat16"), "rw": ("sbuf", [128, P], "bfloat16"),
+    "yf1": ("sbuf", [128, LW], "float32"), "yf2": ("sbuf", [128, LW], "float32"), "yfs": ("sbuf", [128, LW], "bfloat16"),
+}
+EX = ["x", "y0", "f0", "f1", "f2", "f3", "y3", "y2", "y1"]
+for _e in EX:
+    SCRATCH["msg_" + _e] = ("sbuf", [128, NB], "bfloat16")
+for _s in range(4):
+    SCRATCH["land%d" % _s] = ("sbuf", [128, NB + 16], "bfloat16")
+PSB = ["pb0", "pb1", "pb2", "pb3", "pb4", "psc", "psm", "psf"]
+for _b in PSB:
+    SCRATCH[_b] = ("psum", [128, 512], "float32")
+DMAS = ["dx", "dsnd", "dsd", "dtl", "dcd0", "dcd1", "dy0", "oy0", "oy1", "oy2", "oy3", "oyf", "gcast"]
+SEMAPHORES = ["sv", "ss", "st", "sg", "snt"] + DMAS + ["arr_" + _e for _e in EX]
+
+
+def lanes(src, cores, topo):
+    near = [c for c in cores if c != src and c in topo.cores_of(src)]
+    far = [c for c in cores if c != src and c not in topo.cores_of(src)]
+    res, used = {}, []
+    for i, c in enumerate(far):
+        e = topo.engines(src, c); k = len(e) // len(far)
+        res[c] = e[i * k:(i + 1) * k]; used += e
+    for c in near:
+        e = [q for q in topo.engines(src, c) if q not in used]
+        res[c] = e[:4]; used += res[c]
+    return res
+
+
+def rank_program(g, core, T, topo):
+    rank = T.rank_of(core)
+    if rank is None:
+        return
+    cores = T.cores
+    qh = {"v": g.vector, "s": g.scalar, "t": g.tensor, "g": g, "y": g.sync}
+    qsem = {"v": "sv", "s": "ss", "t": "st", "g": "sg"}
+    cnt = {}
+    know = {q: {} for q in qh}
+    clocks = {}
+    acc = {}
+    seq = [0]
+
+    def conflicts(q, regs, write):
+        out = []
+        for name, c0, c1 in regs:
+            bank = name in PSB
+            for a0, a1, w, aq, tok in acc.get(name, []):
+                if bank:
+                    if aq != q:
+                        out.append(tok)
+                elif a0 < c1 and c0 < a1 and (w or write):
+                    if aq == q and (not w or q == "t"):
+                        continue
+                    out.append(tok)
+        return out
+
+    def wait_for(q, toks):
+        best = {}
+        for s, v in toks:
+            best[s] = max(best.get(s, 0), v)
+        for s, v in sorted(best.items(), key=lambda t: -clocks[t][1]):
+            if know[q].get(s, 0) >= v:
+                continue
+            qh[q].wait_ge(T.sem[s], v)
+            for k, x in clocks[(s, v)][0].items():
+                know[q][k] = max(know[q].get(k, 0), x)
+            know[q][s] = max(know[q].get(s, 0), v)
+
+    def note(q, reads, writes, tok):
+        for regs, w in ((reads, False), (writes, True)):
+            for name, c0, c1 in regs:
+                lst = acc.get(name, [])
+                if name in PSB:
+                    lst = [a for a in lst if a[3] != q]
+                elif w:
+                    lst = [a for a in lst if not (c0 <= a[0] and a[1] <= c1)]
+                else:
+                    lst = [a for a in lst if a[2] or a[3] != q or not (c0 <= a[0] and a[1] <= c1)]
+                acc[name] = lst + [(c0, c1, w, q, tok)]
+
+    def token(q, sem, n):
+        cnt[sem] = cnt.get(sem, 0) + n
+        seq[0] += 1
+        c = dict(know[q]) if q is not None else {}
+        c[sem] = cnt[sem]
+        clocks[(sem, cnt[sem])] = (c, seq[0])
+        return (sem, cnt[sem])
+
+    def A(name, c0, c1, step=1):
+        return ("op", T[name][:, c0:c1:step] if step != 1 else T[name][:, c0:c1], [(name, c0, c1)], [])
+
+    def I(win, off):
+        return ("op", win[1].indirect(off[1]), win[2], off[2])
+
+    def do(q, fn, out, *ins, **kw):
+        reads, writes, args = list(out[3]), list(out[2]), [out[1]]
+        for x in ins:
+            if isinstance(x, tuple):
+                reads += x[2] + x[3]; args.append(x[1])
+            else:
+                args.append(x)
+        wait_for(q, conflicts(q, reads, False) + conflicts(q, writes, True))
+        f = {"copy": lambda: g.vector.tensor_copy, "tt": lambda: g.vector.tensor_tensor, "ts": lambda: g.vector.tensor_scalar,
+             "scan": lambda: g.vector.tensor_tensor_scan, "memset": lambda: g.vector.memset, "act": lambda: g.scalar.activation,
+             "mm": lambda: g.tensor.matmul, "iota": lambda: g.iota, "asel": lambda: g.affine_select}[fn]()
+        r = f(*args, **kw)
+        tok = token(q, qsem[q], 1)
+        r.then_inc(T.sem[qsem[q]], 1)
+        note(q, reads, writes, tok)
+
+    def dma(q, sem, out_ap, in_ap, reads, writes):
+        wait_for(q, conflicts(q, reads, False) + conflicts(q, writes, True))
+        qh[q].dma_start(out_ap, in_ap).then_inc(T.sem[sem], 16)
+        note(q + "dma", reads, writes, token(q, sem, 16))
+
+    V = lambda fn, out, *a, **k: do("v", fn, out, *a, **k)
+    S = lambda out, in_, f, **k: do("s", "act", out, in_, f, **k)
+    M = lambda out, l, r, a, b: do("t", "mm", out, l, r, a, b)
+    G = lambda fn, out, *a, **k: do("g", fn, out, *a, **k)
+    sel = lambda a: A("sel", a * 128, (a + 1) * 128)
+
+    def landing(e):
+        if e[0] == "f":
+            return "land" + e[1], 0
+        if e == "x":
+            return "xw", P
+        return "yw", P + NB * (3 - int(e[1]) + 1 if e != "y0" else 0)
+
+    def send(e):
+        name, c0 = landing(e)
+        lan = lanes(core, cores, topo)
+        wait_for("g", conflicts("g", [("msg_" + e, 0, NB)], False))
+        tr = []
+        for d in range(1, N):
+            dst = cores[(rank + d) % N] if e[0] != "f" else cores[(rank - d) % N]
+            rid, pid = topo.addr(dst, core)
+            b = (d - 1) * GB
+            tr.append(RemoteDMATransfer(dst_ids=[DstId(rid=rid, pnc=pid)], dma_engine_mask=sum(1 << q for q in lan[dst]),
+                                        remote_sem=T.sem["arr_" + e], src=T["msg_" + e][:, b:b + GB], dst=T[name][:, c0 + b:c0 + b + GB]))
+            cnt["snt"] = cnt.get("snt", 0) + len(lan[dst])
+        g.remote_dma_fused(tr, local_sem=T.sem.snt)
+
+    for e in EX:
+        name, c0 = landing(e)
+        n = sum(len(lanes(c, cores, topo)[core]) for c in cores if c != core)
+        note("net", [], [(name, c0, c0 + NB)], token(None, "arr_" + e, n))
+
+    V("memset", A("sdrow", 0, BS), 0.0)
+    H = ST // 2
+    V("memset", A("swv", 0, H), 0.0)
+    dma("s", "dsnd", T.snd32[:, :], T.snd[:, :], [], [("snd32", 0, NB // 16)])
+    dma("y", "dx", T.xw[:, 0:P], T.x[:, :], [], [("xw", 0, P)])
+    dma("s", "dtl", T.tlc[:, :], T.tl[:, :], [], [("tlc", 0, 1)])
+    dma("s", "dsd", T.sdrow[0:128:16, :], T.sd[:, :], [], [("sdrow", 0, BS)])
+    dma("y", "dcd0", T.cdw[:, 0:BS], T.cd[:, 0:BS], [], [("cdw", 0, BS)])
+    dma("y", "dy0", T.yw[:, 0:P], T.y0[:, :], [], [("yw", 0, P)])
+    dma("y", "dcd1", T.cdw[:, BS:T4 * BS], T.cd[:, BS:T4 * BS], [], [("cdw", BS, T4 * BS)])
+    G("iota", A("pmi", 0, 1), [[0, 1]], 0, 1)
+    G("iota", A("qp", 0, 128), [[0, 8], [1, 16]], 0, 0, allow_small_or_imprecise_dtypes=True)
+    G("asel", A("qp", 0, 128), A("qp", 0, 128), [[-16, 8], [0, 16]], OP.is_ge, -1.0, 0, 1)
+    G("asel", A("qp", 0, 128), A("qp", 0, 128), [[16, 8], [0, 16]], OP.is_ge, -1.0, 15, -1)
+    G("iota", A("c16", 0, 16), [[16, 16]], 0, 0, allow_small_or_imprecise_dtypes=True)
+    G("iota", A("nmod", 0, BS), [[0, 16], [1, 16]], 0, 0, allow_small_or_imprecise_dtypes=True)
+    G("iota", A("pkd0", 0, CAP), [[16, CAP]], ST + (XDEF << XSH), 0)
+    G("iota", A("i384", 0, NB), [[1, NB]], -(NB // 2), 0, allow_small_or_imprecise_dtypes=True)
+    S(A("sws", 0, H), A("swv", 0, H), AF.Copy)
+    S(A("sin", 0, SIN), A("swv", 0, SIN), AF.Sigmoid)
+    V("ts", A("pm2", 0, 1), A("pmi", 0, 1), 15, None, OP.bitwise_and)
+    V("copy", A("pmod", 0, 1), A("pm2", 0, 1))
+    pmod = A("pmod", 0, 1)
+    for a in range(16):
+        V("ts", sel(a), A("qp", 0, 128), float(a), None, OP.is_equal)
+    V("ts", A("idn", 0, 128), A("qp", 0, 128), pmod, None, OP.is_equal)
+    V("copy", A("sndw", 0, 24), A("snd32", 0, 24))
+    V("memset", A("swv", H, ST), 0.0)
+    bd, tri, idn = A("bd", 0, 128), A("tri", 0, 128), A("idn", 0, 128)
+
+    def border(e, src, c1):
+        h = NB // 2
+        V("copy", A("msg_" + e, 0, h), I(A(src, 0, c1), A("sndw", 0, 12)))
+        S(A("msg_" + e, h, NB), I(A(src, 0, c1), A("sndw", 12, 24)), AF.Copy)
+        send(e)
+
+    border("x", "xw", P)
+    G("asel", A("d0", 0, E), A("swv", H, H + E), [[0, CAP], [1, 16]], OP.is_gt, 191.0, 0, 0)
+    S(A("sws", H, ST), A("swv", H, ST), AF.Copy)
+
+    def wrap(c1, src, ps):
+        tot = 16 * len(src); k = 0
+        for name, c0, st in src:
+            for a in range(16):
+                M(A(ps, 0, c1), sel(a), A(name, c0 + a * st, c0 + (16 * (c1 - 1) + a) * st + 1, 16 * st), k == 0, k == tot - 1)
+                k += 1
+
+    def pack(s):
+        b = s * BS
+        M(A("psf", 0, BS), A("idx", 0, 128), A("xw", b, b + BS), True, True)
+        V("tt", A("pk", b, b + BS), A("psf", 0, BS), A("cdw", b, b + BS), OP.add)
+
+    def prefill(s):
+        V("copy", A("pkc", s * SLOT, s * SLOT + CAP), A("pkd", 0, CAP))
+
+    def slots(s):
+        f, a, b = A("fw", 16 * s, 16 * s + 16), s * CAP, (s + 1) * CAP
+        M(A("psm", 0, 16), idn, A("nrow", 0, 16), True, False)
+        M(A("psm", 0, 16), tri, f, False, False)
+        V("scan", A("cs", 1, 17), A("ones", 0, 16), f, 0.0, OP.mult, OP.add)
+        M(A("psm", 0, 16), bd, A("cs", 0, 16), False, True)
+        V("tt", A("tp", 0, 16), f, A("nc", 0, 16), OP.mult)
+        V("tt", A("of32", 0, 16), A("psm", 0, 16), A("tp", 0, 16), OP.subtract)
+        V("ts", A("offs", 16 * s, 16 * s + 16), A("of32", 0, 16), 256.0, None, OP.add)
+        V("copy", I(A("pkc", s * SLOT, (s + 1) * SLOT), A("offs", 16 * s, 16 * s + 16)), A("pk", s * BS, (s + 1) * BS))
+        k = A("pkc", s * SLOT, s * SLOT + CAP)
+        V("ts", A("shf", a, b), k, (1 << XSH) - 1, 1, OP.bitwise_and, OP.logical_shift_right)
+        V("ts", A("lst", a, b), A("shf", a, b), float(W - 1), None, OP.min)
+        V("ts", A("xi", 0, CAP), k, XSH, None, OP.logical_shift_right)
+        V("ts", A("xmn", a, b), A("xi", 0, CAP), -1.0, None, OP.mult)
+
+    def match(s, win, wc, lst, between=None):
+        x0 = s * CAP
+        V("copy", A("come", 0, EA), I(A(win, 0, wc), A(lst, x0, x0 + MA)))
+        S(A("come", EA, E), I(A(win, 0, wc), A(lst, x0 + MA, x0 + CAP)), AF.Copy)
+        for base, m0, mc, e0 in ((0, MA, MB, EA), (EB, 0, MA, 0)):
+            for i in range(16):
+                lo = base + i * mc
+                cuts = [lo] + [c for c in range(512, E, 512) if lo < c < lo + mc] + [lo + mc]
+                for a, b in zip(cuts[:-1], cuts[1:]):
+                    out = A("pb%d" % (a // 512), a % 512, a % 512 + b - a)
+                    u, w = a - lo, b - lo
+                    M(out, idn, A("xmn", x0 + m0 + u, x0 + m0 + w), True, False)
+                    M(out, idn, A("come", e0 + 16 * u + i, e0 + 16 * (w - 1) + i + 1, 16), False, True)
+        for k in range(5):
+            S(A("ab", 512 * k, 512 * k + 512), A("pb%d" % k, 0, 512), AF.Abs)
+        if between:
+            between()
+        for k in range(5):
+            V("ts", A("ind", 512 * k, 512 * k + 512), A("ab", 512 * k, 512 * k + 512), A("tlc", 0, 1), None, OP.is_le)
+        for base, m0, mc in ((0, MA, MB), (EB, 0, MA)):
+            for i in range(16):
+                M(A("psc", m0, m0 + mc), sel(i), A("ind", base + i * mc, base + (i + 1) * mc), i == 0, i == 15)
+
+    def targets(s):
+        V("ts", A("nq", 0, CAP), A("psc", 0, CAP), 7.5, float(ST), OP.is_lt, OP.mult)
+        V("tt", A("so", 0, CAP), A("nq", 0, CAP), A("vi", 0, CAP), OP.add)
+        V("copy", A("sof", 0, CAP), A("so", 0, CAP))
+
+    def numbers(s):
+        V("ts", A("vi", 0, CAP), A("pkc", s * SLOT, s * SLOT + CAP), (1 << XSH) - 1, None, OP.bitwise_and)
+
+    def scatter(vs):
+        V("copy", I(A("swv", 0, SWN), A("sof", 0, vs)), A("sin", 0, 16 * vs))
+        S(I(A("sws", 0, SWN), A("sof", vs, CAP)), A("sin", 0, 16 * (CAP - vs)), AF.Sigmoid)
+
+    def tell(s):
+        S(A("swb", 0, 2 * NB), A("sws", 2 * P, ST), AF.Copy)
+        ps = A("psc", 0, NB)
+        M(ps, idn, A("swb", 0, 2 * NB, 2), True, False)
+        M(ps, idn, A("swb", 1, 2 * NB, 2), False, False)
+        M(ps, idn, A("swv", 2 * P, ST, 2), False, False)
+        M(ps, idn, A("swv", 2 * P + 1, ST, 2), False, True)
+        S(A("msg_f%d" % s, 0, NB), ps, AF.Copy)
+        send("f%d" % s)
+
+    def keep_y(s):
+        b = s * BS
+        V("tt", A("yb", b, b + BS), I(A("memn", 0, SLOT), A("offs", 16 * s, 16 * s + 16)), A("yw", b, b + BS), OP.mult)
+
+    def back_list(s):
+        a, b = s * CAP, (s + 1) * CAP
+        V("ts", A("lg", 0, CAP), A("shf", a, b), float(P), float(NB * (3 - s)), OP.is_ge, OP.mult)
+        V("tt", A("lf", 0, CAP), A("shf", a, b), A("lg", 0, CAP), OP.add)
+        V("ts", A("lsb", a, b), A("lf", 0, CAP), float(P + NB * (4 - s) - 1), None, OP.min)
+
+    def members(s):
+        S(A("memr", s * BS, (s + 1) * BS), I(A("memc", 0, SLOT), A("offs", 16 * s, 16 * s + 16)), AF.Copy)
+
+    def zero(name, c0, c1):
+        S(A(name, c0, c1), A("xw", 0, c1 - c0), AF.Copy, scale=0.0)
+
+    wrap(16, [("sdrow", 0, 1)], "psm")
+    V("ts", bd, A("qp", 0, 128), 0.0, None, OP.is_ge)
+    V("ts", tri, A("qp", 0, 128), pmod, None, OP.is_ge)
+    V("ts", A("idx", 0, 128), idn, float(1 << XSH), None, OP.mult)
+    V("ts", A("nrow", 0, 16), A("c16", 0, 16), pmod, None, OP.add)
+    V("ts", A("nc", 0, 16), A("c16", 0, 16), pmod, 257.0, OP.add, OP.add)
+    V("memset", A("cs", 0, 1), 0.0)
+    V("memset", A("ones", 0, 16), 1.0)
+    V("ts", A("fw", 0, 16), A("psm", 0, 16), 0.5, None, OP.is_ge)
+    V("ts", A("pkd", 0, CAP), A("pkd0", 0, CAP), pmod, None, OP.add)
+    prefill(0)
+    pack(0)
+    slots(0)
+    numbers(0)
+    border("y0", "yw", P)
+    V("copy", A("swv", 0, 2 * BS, 2), A("sdrow", 0, BS))
+    V("memset", A("bp", BS, 4 * BS), float(NB // 2))
+    for s in range(4):
+        if s:
+            ln = "land%d" % (s - 1)
+            V("tt", A("fb", 0, BS), I(A(ln, 0, NB + 16), A("bposw", 16 * (s - 1), 16 * s)), A("mask", 0, BS), OP.mult)
+            V("scan", A("fsc", 0, BS), A("seg0", 0, BS), A("fb", 0, BS), 0.0, OP.mult, OP.add)
+            V("tt", A("fw", 16 * s, 16 * s + 16), A("fsc", 15, BS, 16), A("nown", 16 * s, 16 * s + 16), OP.is_gt)
+            slots(s)
+        if s == 3:
+            break
+        match(s, "xw", W, "lst", (lambda s=s: numbers(s)) if s else None)
+        targets(s)
+        scatter(VS)
+        tell(s)
+        S(A("swo", 0, 2 * BS), A("sws", 2 * BS * (s + 1), 2 * BS * (s + 2)), AF.Copy)
+        if s == 0:
+            V("copy", I(A("bp", 0, P), A("sndw", 0, 24)), A("i384", 0, NB))
+            wrap(48, [("bp", BS, 1)], "psf")
+            V("ts", A("mask", 0, BS), A("nmod", 0, BS), pmod, None, OP.is_equal)
+            V("ts", A("seg0", 0, BS), A("nmod", 0, BS), 0.0, None, OP.not_equal)
+            V("ts", A("bposw", 0, 48), A("psf", 0, 48), 1.0 / 16, float(NB // 2), OP.mult, OP.add)
+        zero("land%d" % s, NB, NB + 16)
+        b = 2 * BS * (s + 1)
+        wrap(16, [("swv", b, 2), ("swv", b + 1, 2), ("swo", 0, 2), ("swo", 1, 2)], "psm")
+        prefill(s + 1)
+        pack(s + 1)
+        V("ts", A("nown", 16 * s + 16, 16 * s + 32), A("psm", 0, 16), 0.0, -1.0, OP.is_gt, OP.mult)
+        zero("vals", SLOT * s, SLOT * s + SLOT)
+        if s == 1:
+            for name, u, w in (("memc", 64.0, 0.0), ("memn", 0.0, 1.0)):
+                V("memset", A(name, 0, CAP), u)
+                V("memset", A(name, CAP, SLOT), w)
+        for k in ([], [0, 1], [2])[s]:
+            back_list(k)
+            keep_y(k)
+            members(k)
+    for s in range(3, -1, -1):
+        def low(s=s):
+            V("scan", A("mn", 0, E), A("d0", 0, E), A("come", 0, E), 0.0, OP.max, OP.min)
+            if s == 3:
+                keep_y(3)
+            V("tt", A("hs", 0, CAP), A("mn", 15, E, 16), A("xmn", s * CAP, (s + 1) * CAP), OP.subtract)
+            V("ts", A("hv", 0, CAP), A("hs", 0, CAP), 1, None, OP.logical_shift_right)
+        match(s, "yw", P + NB * (4 - s), "lst" if s == 3 else "lsb", low)
+        if s == 3:
+            zero("vals", SLOT * 3, SLOT * 4)
+        V("ts", A("mt", 0, CAP), A("psc", 0, CAP), 7.5, None, OP.is_ge)
+        M(A("psm", 0, CAP), bd, A("mt", 0, CAP), True, True)
+        V("ts", A("dd", 0, CAP), A("psm", 0, CAP), 2.5, 255.0, OP.is_ge, OP.mult)
+        V("tt", A("vals", s * SLOT, s * SLOT + CAP), A("dd", 0, CAP), A("hv", 0, CAP), OP.max)
+        V("tt", A("yw", s * BS, (s + 1) * BS), I(A("vals", s * SLOT, (s + 1) * SLOT), A("offs", 16 * s, 16 * s + 16)),
+          A("yb", s * BS, (s + 1) * BS), OP.add)
+        if s:
+            border("y%d" % s, "yw", P)
+        dma("y", "oy%d" % s, T.yv[:, s * BS:(s + 1) * BS], T.yw[:, s * BS:(s + 1) * BS], [("yw", s * BS, (s + 1) * BS)], [])
+        if s == 3:
+            match(3, "xw", W, "lst", lambda: numbers(3))
+            targets(3)
+            members(3)
+        elif s == 2:
+            scatter(VS3)
+            V("memset", A("rw", 0, P), 0.0)
+        elif s == 1:
+            tell(3)
+            dma("g", "gcast", T.swc[:, :], T.sws[:, 0:2 * P], [("sws", 0, 2 * P)], [("swc", 0, 2 * P)])
+            for st in range(2):
+                for h in range(16):
+                    M(A("psf", 0, LW), sel(h), A("swv", 2 * LW * h + st, 2 * LW * (h + 1), 2), st == 0 and h == 0, False)
+            for h in range(7):
+                n = min(LW, T4 * BS - LW * h)
+                M(A("psf", 0, n), sel(h), A("memr", LW * h, LW * h + n), False, False)
+    for st in range(2):
+        for h in range(16):
+            M(A("psf", 0, LW), sel(h), A("swc", 2 * LW * h + st, 2 * LW * (h + 1), 2), False, False)
+    V("copy", I(A("rw", 0, P), A("sndw", 0, 24)), A("land3", 0, NB))
+    for h in range(16):
+        M(A("psf", 0, LW), sel(h), A("rw", LW * h, LW * (h + 1)), False, h == 15)
+    V("ts", A("yf1", 0, LW), A("psf", 0, LW), 0.0, None, OP.is_gt)
+    V("ts", A("yf2", 0, LW), A("psf", 0, LW), 500.0, None, OP.is_ge)
+    V("tt", A("yfs", 0, LW), A("yf1", 0, LW), A("yf2", 0, LW), OP.add)
+    dma("y", "oyf", T.yf[:, :], T.yfs[:, :], [("yfs", 0, LW)], [])
+    for sname in SEMAPHORES:
+        if cnt.get(sname, 0) and know["g"].get(sname, 0) < cnt[sname]:
+            g.wait_ge(T.sem[sname], cnt[sname])

@@ -5,56 +5,47 @@ N, P, BS, T4, CAP, GB, S2 = 4, 2368, 256, 4, 160, 128, 2
 NB = (N - 1) * GB
 W = P + NB
 ST = S2 * W
-MA = 96
-MB = CAP - MA
-EA, EB, E = 16 * MA, 16 * MB, 16 * CAP
-SWN = 2 * ST + E
-VS, VS3 = 88, 76
-SIN = 16 * 96
-SLOT = 768
-XSH = 14
-XDEF = 512
+MA = 64
+LOTS = [(0, MA), (MA, CAP - MA)]
+ALL = [(64 * k, 64) for k in range(4)]
+RING = 5 * 512
+OFF = 2816
+FAR, FARC = 8192, 8320
+SWN = OFF + FARC + ST
+SIN = 1536
+SLOT = 1024
+XF = 1024.0
+Y0 = 256
+HOLE = 256
 LW = 148
+MAGIC = 12582912.0
+PAR = {'VS': [64, 80, 72, 64], 'by_s': [(), (), ()], 'l0': 'v', 'tq': 'v', 'tu': 2, 'b1': 32, 'b2': 80, 'b3': (2, 3, 4), 'h1': 0, 'h2': 64, 'h3': (), 's3': 48, 't3': 0, 'g1': 32, 'g2': 80}
 
-SCRATCH = {
-    "xw": ("sbuf", [128, W], "bfloat16"), "yw": ("sbuf", [128, P + 4 * NB], "bfloat16"),
-    "cdw": ("sbuf", [128, T4 * BS], "int32"), "snd32": ("sbuf", [128, NB // 16], "int32"),
-    "sndw": ("sbuf", [128, NB // 16], "uint16"), "tlc": ("sbuf", [128, 1], "bfloat16"), "sdrow": ("sbuf", [128, BS], "bfloat16"),
-    "swv": ("sbuf", [128, SWN], "bfloat16"), "sws": ("sbuf", [128, SWN], "float32"),
-    "swc": ("sbuf", [128, 2 * P], "bfloat16"), "swb": ("sbuf", [128, 2 * NB], "bfloat16"), "swo": ("sbuf", [128, 2 * BS], "bfloat16"),
-    "ones": ("sbuf", [128, 16], "bfloat16"), "sin": ("sbuf", [128, SIN], "float32"),
-    "come": ("sbuf", [128, E], "bfloat16"), "ab": ("sbuf", [128, E], "bfloat16"), "ind": ("sbuf", [128, E], "bfloat16"),
-    "mn": ("sbuf", [128, E], "bfloat16"), "d0": ("sbuf", [128, E], "bfloat16"),
-    "pk": ("sbuf", [128, T4 * BS], "int32"), "pkc": ("sbuf", [128, T4 * SLOT], "int32"),
-    "pkd0": ("sbuf", [128, CAP], "int32"), "pkd": ("sbuf", [128, CAP], "int32"),
-    "sel": ("sbuf", [128, 16 * 128], "bfloat16"), "qp": ("sbuf", [128, 128], "bfloat16"), "bd": ("sbuf", [128, 128], "bfloat16"),
-    "tri": ("sbuf", [128, 128], "bfloat16"), "idn": ("sbuf", [128, 128], "bfloat16"), "idx": ("sbuf", [128, 128], "bfloat16"),
-    "pmi": ("sbuf", [128, 1], "int32"), "pm2": ("sbuf", [128, 1], "int32"), "pmod": ("sbuf", [128, 1], "float32"),
-    "nmod": ("sbuf", [128, BS], "bfloat16"), "mask": ("sbuf", [128, BS], "bfloat16"), "seg0": ("sbuf", [128, BS], "bfloat16"),
-    "c16": ("sbuf", [128, 16], "float32"), "nrow": ("sbuf", [128, 16], "bfloat16"), "nc": ("sbuf", [128, 16], "float32"),
-    "i384": ("sbuf", [128, NB], "bfloat16"), "bp": ("sbuf", [128, P], "bfloat16"), "bposw": ("sbuf", [128, 48], "uint16"),
-    "fw": ("sbuf", [128, 64], "bfloat16"), "fb": ("sbuf", [128, BS], "bfloat16"), "fsc": ("sbuf", [128, BS], "bfloat16"),
-    "nown": ("sbuf", [128, 64], "bfloat16"), "cs": ("sbuf", [128, 32], "bfloat16"), "tp": ("sbuf", [128, 16], "float32"),
-    "of32": ("sbuf", [128, 16], "float32"), "offs": ("sbuf", [128, 64], "uint16"),
-    "shf": ("sbuf", [128, T4 * CAP], "int32"), "lst": ("sbuf", [128, T4 * CAP], "uint16"), "lsb": ("sbuf", [128, T4 * CAP], "uint16"),
-    "lf": ("sbuf", [128, CAP], "float32"), "lg": ("sbuf", [128, CAP], "float32"),
-    "xi": ("sbuf", [128, CAP], "int32"), "xmn": ("sbuf", [128, T4 * CAP], "bfloat16"), "vi": ("sbuf", [128, CAP], "int32"),
-    "nq": ("sbuf", [128, CAP], "float32"), "so": ("sbuf", [128, CAP], "float32"), "sof": ("sbuf", [128, CAP], "uint16"),
-    "mt": ("sbuf", [128, CAP], "bfloat16"), "dd": ("sbuf", [128, CAP], "float32"), "hs": ("sbuf", [128, CAP], "int32"),
-    "hv": ("sbuf", [128, CAP], "int32"), "vals": ("sbuf", [128, T4 * SLOT], "bfloat16"), "yb": ("sbuf", [128, T4 * BS], "bfloat16"),
-    "memc": ("sbuf", [128, SLOT], "bfloat16"), "memn": ("sbuf", [128, SLOT], "bfloat16"),
-    "memr": ("sbuf", [128, T4 * BS], "bfloat16"), "rw": ("sbuf", [128, P], "bfloat16"),
-    "yf1": ("sbuf", [128, LW], "float32"), "yf2": ("sbuf", [128, LW], "float32"), "yfs": ("sbuf", [128, LW], "bfloat16"),
-}
+B16, F32, I32, U16 = "bfloat16", "float32", "int32", "uint16"
+SCRATCH = {}
+for _n, _c, _d in [
+        ("xw", W, B16), ("ya", Y0 + W, B16), ("yb", Y0 + W, B16), ("cdw", T4 * BS, I32), ("snd32", 24, I32), ("sndw", 24, U16),
+        ("tlc", 1, B16), ("sdrow", BS, B16), ("swv", SWN, B16), ("sws", SWN, F32), ("swb", 2 * NB, B16),
+        ("swo", 2 * BS, B16), ("own", BS, B16), ("sin", SIN, F32), ("come", 16 * BS, B16), ("ab", 1536, B16), ("ind", RING, B16),
+        ("mn", 16 * BS, B16), ("d0", 16 * (CAP - MA), B16), ("pk", BS, F32), ("pkc", T4 * SLOT, F32), ("sel", 16 * 128, B16),
+        ("qp", 128, B16), ("bd", 128, B16), ("bdk", 128, B16), ("tri", 128, B16), ("dg", 128, B16), ("idn", 128, B16),
+        ("dr", 128, B16), ("ndr", 128, B16), ("ndk", 128, B16), ("hlf", 128, B16), ("ihk", 128, B16), ("ihf", 128, F32),
+        ("ik", 128, B16), ("pmi", 1, I32), ("pm2", 2, I32), ("col", 8, F32), ("nm", BS, B16), ("dsel", BS, B16), ("dtm", BS, B16),
+        ("c32", 32, B16), ("nb", 48, F32), ("i384", NB, B16), ("bp", P, B16), ("bposw", 48, U16), ("fw", 16, B16), ("fb", BS, B16),
+        ("fsc", BS, B16), ("cs", 32, B16), ("tp", 16, B16), ("offs", 64, U16), ("of2", 64, U16), ("oa", 48, F32), ("ob", 48, F32),
+        ("lsf", 3 * BS, U16), ("lst", T4 * CAP, U16), ("i32", CAP, I32), ("shf", CAP, I32), ("xq", T4 * CAP, B16), ("t1", BS, B16),
+        ("so", CAP, F32), ("sof", CAP, U16), ("mt", BS, B16), ("hv", BS, I32), ("memi", SLOT, B16), ("memr", P, B16),
+        ("fv", 2 * LW, B16), ("fs", 2 * LW, F32), ("fr", LW, B16), ("fm", LW, B16), ("yf1", LW, F32), ("yfs", LW, B16)]:
+    SCRATCH[_n] = ("sbuf", [128, _c], _d)
 EX = ["x", "y0", "f0", "f1", "f2", "f3", "y3", "y2", "y1"]
 for _e in EX:
-    SCRATCH["msg_" + _e] = ("sbuf", [128, NB], "bfloat16")
+    SCRATCH["msg_" + _e] = ("sbuf", [128, NB], B16)
 for _s in range(4):
-    SCRATCH["land%d" % _s] = ("sbuf", [128, NB + 16], "bfloat16")
-PSB = ["pb0", "pb1", "pb2", "pb3", "pb4", "psc", "psm", "psf"]
+    SCRATCH["land%d" % _s] = ("sbuf", [128, NB + 16], B16)
+PSB = ["pd0", "pd1", "pd2", "pd3", "pd4", "psc", "psm", "psf"]
 for _b in PSB:
-    SCRATCH[_b] = ("psum", [128, 512], "float32")
-DMAS = ["dx", "dsnd", "dsd", "dtl", "dcd0", "dcd1", "dy0", "oy0", "oy1", "oy2", "oy3", "oyf", "gcast"]
+    SCRATCH[_b] = ("psum", [128, 512], F32)
+DMAS = ["dx", "dsnd", "dsd", "dtl", "dcd0", "dcd1", "dya", "dyb", "dfv", "dfs", "dfr", "dfm", "oy0", "oy1", "oy2", "oy3", "oyf"]
 SEMAPHORES = ["sv", "ss", "st", "sg", "snt"] + DMAS + ["arr_" + _e for _e in EX]
 
 
@@ -90,11 +81,9 @@ def rank_program(g, core, T, topo):
             bank = name in PSB
             for a0, a1, w, aq, tok in acc.get(name, []):
                 if bank:
-                    if aq != q:
+                    if aq != q or (q != "t" and (w or write)):
                         out.append(tok)
                 elif a0 < c1 and c0 < a1 and (w or write):
-                    if aq == q and (not w or q == "t"):
-                        continue
                     out.append(tok)
         return out
 
@@ -115,7 +104,7 @@ def rank_program(g, core, T, topo):
             for name, c0, c1 in regs:
                 lst = acc.get(name, [])
                 if name in PSB:
-                    lst = [a for a in lst if a[3] != q]
+                    lst = [a for a in lst if a[3] != q or (a[2] and not w)]
                 elif w:
                     lst = [a for a in lst if not (c0 <= a[0] and a[1] <= c1)]
                 else:
@@ -146,6 +135,7 @@ def rank_program(g, core, T, topo):
         wait_for(q, conflicts(q, reads, False) + conflicts(q, writes, True))
         f = {"copy": lambda: g.vector.tensor_copy, "tt": lambda: g.vector.tensor_tensor, "ts": lambda: g.vector.tensor_scalar,
              "scan": lambda: g.vector.tensor_tensor_scan, "memset": lambda: g.vector.memset, "act": lambda: g.scalar.activation,
+             "rec": lambda: g.vector.reciprocal,
              "mm": lambda: g.tensor.matmul, "iota": lambda: g.iota, "asel": lambda: g.affine_select}[fn]()
         r = f(*args, **kw)
         tok = token(q, qsem[q], 1)
@@ -161,263 +151,447 @@ def rank_program(g, core, T, topo):
     S = lambda out, in_, f, **k: do("s", "act", out, in_, f, **k)
     M = lambda out, l, r, a, b: do("t", "mm", out, l, r, a, b)
     G = lambda fn, out, *a, **k: do("g", fn, out, *a, **k)
+    iota = lambda out, pat, base, cm=0: G("iota", out, pat, base, cm, allow_small_or_imprecise_dtypes=True)
     sel = lambda a: A("sel", a * 128, (a + 1) * 128)
+    mat = lambda n: A(n, 0, 128)
+    col = lambda j: A("col", j, j + 1)
 
-    def landing(e):
+    def move(q, out, in_):
+        if q == "v":
+            V("copy", out, in_)
+        else:
+            S(out, in_, AF.Copy)
+
+    def landing(e, d):
+        b = (d - 1) * GB
         if e[0] == "f":
-            return "land" + e[1], 0
+            return "land" + e[1], b + (16 if b >= HOLE and e != "f3" else 0)
         if e == "x":
-            return "xw", P
-        return "yw", P + NB * (3 - int(e[1]) + 1 if e != "y0" else 0)
+            return "xw", P + b
+        return ("ya" if e in ("y0", "y2") else "yb"), Y0 + P + b
+
+    arrival = {}
+    for e in EX:
+        n = sum(len(lanes(c, cores, topo)[core]) for c in cores if c != core)
+        arrival[e] = token(None, "arr_" + e, n)
+
+    def expect(e):
+        note("net", [], [(landing(e, d)[0], landing(e, d)[1], landing(e, d)[1] + GB) for d in range(1, N)], arrival[e])
 
     def send(e):
-        name, c0 = landing(e)
         lan = lanes(core, cores, topo)
         wait_for("g", conflicts("g", [("msg_" + e, 0, NB)], False))
         tr = []
         for d in range(1, N):
             dst = cores[(rank + d) % N] if e[0] != "f" else cores[(rank - d) % N]
             rid, pid = topo.addr(dst, core)
-            b = (d - 1) * GB
+            name, c0 = landing(e, d)
             tr.append(RemoteDMATransfer(dst_ids=[DstId(rid=rid, pnc=pid)], dma_engine_mask=sum(1 << q for q in lan[dst]),
-                                        remote_sem=T.sem["arr_" + e], src=T["msg_" + e][:, b:b + GB], dst=T[name][:, c0 + b:c0 + b + GB]))
+                                        remote_sem=T.sem["arr_" + e], src=T["msg_" + e][:, (d - 1) * GB:d * GB], dst=T[name][:, c0:c0 + GB]))
             cnt["snt"] = cnt.get("snt", 0) + len(lan[dst])
         g.remote_dma_fused(tr, local_sem=T.sem.snt)
 
-    for e in EX:
-        name, c0 = landing(e)
-        n = sum(len(lanes(c, cores, topo)[core]) for c in cores if c != core)
-        note("net", [], [(name, c0, c0 + NB)], token(None, "arr_" + e, n))
+    for e in EX[:-2]:
+        expect(e)
 
-    V("memset", A("sdrow", 0, BS), 0.0)
-    H = ST // 2
-    V("memset", A("swv", 0, H), 0.0)
-    dma("s", "dsnd", T.snd32[:, :], T.snd[:, :], [], [("snd32", 0, NB // 16)])
-    dma("y", "dx", T.xw[:, 0:P], T.x[:, :], [], [("xw", 0, P)])
-    dma("s", "dtl", T.tlc[:, :], T.tl[:, :], [], [("tlc", 0, 1)])
-    dma("s", "dsd", T.sdrow[0:128:16, :], T.sd[:, :], [], [("sdrow", 0, BS)])
-    dma("y", "dcd0", T.cdw[:, 0:BS], T.cd[:, 0:BS], [], [("cdw", 0, BS)])
-    dma("y", "dy0", T.yw[:, 0:P], T.y0[:, :], [], [("yw", 0, P)])
-    dma("y", "dcd1", T.cdw[:, BS:T4 * BS], T.cd[:, BS:T4 * BS], [], [("cdw", BS, T4 * BS)])
-    G("iota", A("pmi", 0, 1), [[0, 1]], 0, 1)
-    G("iota", A("qp", 0, 128), [[0, 8], [1, 16]], 0, 0, allow_small_or_imprecise_dtypes=True)
-    G("asel", A("qp", 0, 128), A("qp", 0, 128), [[-16, 8], [0, 16]], OP.is_ge, -1.0, 0, 1)
-    G("asel", A("qp", 0, 128), A("qp", 0, 128), [[16, 8], [0, 16]], OP.is_ge, -1.0, 15, -1)
-    G("iota", A("c16", 0, 16), [[16, 16]], 0, 0, allow_small_or_imprecise_dtypes=True)
-    G("iota", A("nmod", 0, BS), [[0, 16], [1, 16]], 0, 0, allow_small_or_imprecise_dtypes=True)
-    G("iota", A("pkd0", 0, CAP), [[16, CAP]], ST + (XDEF << XSH), 0)
-    G("iota", A("i384", 0, NB), [[1, NB]], -(NB // 2), 0, allow_small_or_imprecise_dtypes=True)
-    S(A("sws", 0, H), A("swv", 0, H), AF.Copy)
-    S(A("sin", 0, SIN), A("swv", 0, SIN), AF.Sigmoid)
-    V("ts", A("pm2", 0, 1), A("pmi", 0, 1), 15, None, OP.bitwise_and)
-    V("copy", A("pmod", 0, 1), A("pm2", 0, 1))
-    pmod = A("pmod", 0, 1)
-    for a in range(16):
-        V("ts", sel(a), A("qp", 0, 128), float(a), None, OP.is_equal)
-    V("ts", A("idn", 0, 128), A("qp", 0, 128), pmod, None, OP.is_equal)
-    V("copy", A("sndw", 0, 24), A("snd32", 0, 24))
-    V("memset", A("swv", H, ST), 0.0)
-    bd, tri, idn = A("bd", 0, 128), A("tri", 0, 128), A("idn", 0, 128)
-
-    def border(e, src, c1):
-        h = NB // 2
-        V("copy", A("msg_" + e, 0, h), I(A(src, 0, c1), A("sndw", 0, 12)))
-        S(A("msg_" + e, h, NB), I(A(src, 0, c1), A("sndw", 12, 24)), AF.Copy)
+    def border(e, src, c0, hv=NB // 2):
+        if hv:
+            move("v", A("msg_" + e, 0, hv), I(A(src, c0, c0 + P), A("sndw", 0, hv // 16)))
+        move("s", A("msg_" + e, hv, NB), I(A(src, c0, c0 + P), A("sndw", hv // 16, NB // 16)))
         send(e)
 
-    border("x", "xw", P)
-    G("asel", A("d0", 0, E), A("swv", H, H + E), [[0, CAP], [1, 16]], OP.is_gt, 191.0, 0, 0)
-    S(A("sws", H, ST), A("swv", H, ST), AF.Copy)
+    def wrap(c1, name, c0, ps):
+        for a in range(16):
+            M(A(ps, 0, c1), sel(a), A(name, c0 + a, c0 + 16 * (c1 - 1) + a + 1, 16), a == 0, a == 15)
 
-    def wrap(c1, src, ps):
-        tot = 16 * len(src); k = 0
-        for name, c0, st in src:
-            for a in range(16):
-                M(A(ps, 0, c1), sel(a), A(name, c0 + a * st, c0 + (16 * (c1 - 1) + a) * st + 1, 16 * st), k == 0, k == tot - 1)
-                k += 1
+    def lot(lots, u):
+        return [l for l in lots if 16 * l[0] <= 512 * u < 16 * (l[0] + l[1])][0]
 
-    def pack(s):
+    def pieces(lots, u):
+        m0, mc = lot(lots, u)
+        for i in range(16):
+            lo = 16 * m0 + i * mc
+            a, b = max(lo, 512 * u), min(lo + mc, 512 * u + 512)
+            if a < b:
+                yield i, m0 + a - lo, m0 + b - lo, A("pd%d" % (u % 5), a % 512, a % 512 + b - a), a % 512 == 0, b % 512 == 0
+
+    def gather(q, win, lst, c0, m0, m1):
+        if m1 > m0:
+            move(q, A("come", 16 * m0, 16 * m1), I(win, A(lst, c0 + m0, c0 + m1)))
+
+    def xpart(lots, m, name, c0, us):
+        for u in us:
+            for i, a, b, out, first, last in pieces(lots, u):
+                M(out, mat(m), A(name, c0 + a, c0 + b), first, False)
+
+    def cpart(lots, us):
+        for u in us:
+            for i, a, b, out, first, last in pieces(lots, u):
+                M(out, mat("dr"), A("come", 16 * a + i, 16 * (b - 1) + i + 1, 16), False, last)
+
+    def near(u, q="v"):
+        k = u % 5
+        out, ps, ab = A("ind", 512 * k, 512 * k + 512), A("pd%d" % k, 0, 512), A("ab", 512 * (u % 3), 512 * (u % 3) + 512)
+        if q == "v":
+            V("ts", out, ps, MAGIC, MAGIC, OP.add, OP.is_equal)
+        elif q == "s":
+            S(ab, ps, AF.Abs)
+        else:
+            V("ts", out, ab, 0.5, None, OP.is_lt)
+
+    def count(lots, u, ps):
+        m0, mc = lot(lots, u)
+        for i in range(16):
+            a = 16 * m0 + i * mc
+            if (a + mc - 1) // 512 == u:
+                M(A(ps, m0, m0 + mc), sel(i), A("ind", a % RING, a % RING + mc), i == 0, i == 15)
+
+    def low(m0, m1):
+        V("scan", A("mn", 16 * m0, 16 * m1), A("d0", 0, 16 * (m1 - m0)), A("come", 16 * m0, 16 * m1), 0.0, OP.max, OP.min)
+
+    def halves(n, m, x, ps):
+        M(A(ps, 0, n), mat(m), x, True, False)
+        M(A(ps, 0, n), mat("hlf"), A("mn", 15, 16 * n, 16), False, True)
+        V("ts", A("hv", 0, n), A(ps, 0, n), -0.25, None, OP.add)
+
+    def fresh(n, win):
+        V("ts", A("mt", 0, n), A("psc", 0, n), 7.5, -0.125, OP.is_ge, OP.add)
+        M(A("psm", 0, n), mat("bdk"), A("mt", 0, n), True, True)
+        V("tt", A(win, 0, n), A("psm", 0, n), A("hv", 0, n), OP.max)
+
+    def pack(s, far):
         b = s * BS
-        M(A("psf", 0, BS), A("idx", 0, 128), A("xw", b, b + BS), True, True)
-        V("tt", A("pk", b, b + BS), A("psf", 0, BS), A("cdw", b, b + BS), OP.add)
+        M(A("psf", 0, BS), mat("ik"), A("xw", b, b + BS), True, not far)
+        if far:
+            V("ts", A("t1", 0, BS), A("psc", 0, BS), 7.5, float(FAR), OP.is_lt, OP.mult)
+            M(A("psf", 0, BS), mat("idn"), A("t1", 0, BS), False, True)
+        V("tt", A("pk", 0, BS), A("psf", 0, BS), A("cdw", b, b + BS), OP.add)
 
-    def prefill(s):
-        V("copy", A("pkc", s * SLOT, s * SLOT + CAP), A("pkd", 0, CAP))
+    def flags(s):
+        V("tt", A("fb", 0, BS), I(A("land%d" % (s - 1), 0, NB + 16), A("bposw", 16 * (s - 1), 16 * s)), A("own", 0, BS), OP.add)
+        V("scan", A("fsc", 0, BS), A("dsel", 0, BS), A("fb", 0, BS), 0.0, OP.add, OP.min)
+        V("ts", A("fw", 0, 16), A("fsc", 15, BS, 16), col(3), -15.7, OP.subtract, OP.is_gt)
+
+    def ranks():
+        f = A("fw", 0, 16)
+        M(A("psm", 0, 16), mat("idn"), A("c32", 0, 16), True, False)
+        M(A("psm", 0, 16), mat("tri"), f, False, False)
+        M(A("psm", 0, 16), mat("dg"), f, False, False)
+        V("scan", A("cs", 1, 17), A("c32", 16, 32), f, 0.0, OP.max, OP.add)
+        M(A("psm", 0, 16), mat("bd"), A("cs", 0, 16), False, False)
+        V("tt", A("tp", 0, 16), f, A("c32", 16, 32), OP.mult)
+        M(A("psm", 0, 16), mat("idn"), A("tp", 0, 16), False, True)
 
     def slots(s):
-        f, a, b = A("fw", 16 * s, 16 * s + 16), s * CAP, (s + 1) * CAP
-        M(A("psm", 0, 16), idn, A("nrow", 0, 16), True, False)
-        M(A("psm", 0, 16), tri, f, False, False)
-        V("scan", A("cs", 1, 17), A("ones", 0, 16), f, 0.0, OP.mult, OP.add)
-        M(A("psm", 0, 16), bd, A("cs", 0, 16), False, True)
-        V("tt", A("tp", 0, 16), f, A("nc", 0, 16), OP.mult)
-        V("tt", A("of32", 0, 16), A("psm", 0, 16), A("tp", 0, 16), OP.subtract)
-        V("ts", A("offs", 16 * s, 16 * s + 16), A("of32", 0, 16), 256.0, None, OP.add)
-        V("copy", I(A("pkc", s * SLOT, (s + 1) * SLOT), A("offs", 16 * s, 16 * s + 16)), A("pk", s * BS, (s + 1) * BS))
-        k = A("pkc", s * SLOT, s * SLOT + CAP)
-        V("ts", A("shf", a, b), k, (1 << XSH) - 1, 1, OP.bitwise_and, OP.logical_shift_right)
-        V("ts", A("lst", a, b), A("shf", a, b), float(W - 1), None, OP.min)
-        V("ts", A("xi", 0, CAP), k, XSH, None, OP.logical_shift_right)
-        V("ts", A("xmn", a, b), A("xi", 0, CAP), -1.0, None, OP.mult)
+        V("ts", A("offs", 16 * s, 16 * s + 16), A("psm", 0, 16), col(2), None, OP.add)
+        V("copy", I(A("pkc", s * SLOT, (s + 1) * SLOT), A("offs", 16 * s, 16 * s + 16)), A("pk", 0, BS))
 
-    def match(s, win, wc, lst, between=None):
-        x0 = s * CAP
-        V("copy", A("come", 0, EA), I(A(win, 0, wc), A(lst, x0, x0 + MA)))
-        S(A("come", EA, E), I(A(win, 0, wc), A(lst, x0 + MA, x0 + CAP)), AF.Copy)
-        for base, m0, mc, e0 in ((0, MA, MB, EA), (EB, 0, MA, 0)):
-            for i in range(16):
-                lo = base + i * mc
-                cuts = [lo] + [c for c in range(512, E, 512) if lo < c < lo + mc] + [lo + mc]
-                for a, b in zip(cuts[:-1], cuts[1:]):
-                    out = A("pb%d" % (a // 512), a % 512, a % 512 + b - a)
-                    u, w = a - lo, b - lo
-                    M(out, idn, A("xmn", x0 + m0 + u, x0 + m0 + w), True, False)
-                    M(out, idn, A("come", e0 + 16 * u + i, e0 + 16 * (w - 1) + i + 1, 16), False, True)
-        for k in range(5):
-            S(A("ab", 512 * k, 512 * k + 512), A("pb%d" % k, 0, 512), AF.Abs)
-        if between:
-            between()
-        for k in range(5):
-            V("ts", A("ind", 512 * k, 512 * k + 512), A("ab", 512 * k, 512 * k + 512), A("tlc", 0, 1), None, OP.is_le)
-        for base, m0, mc in ((0, MA, MB), (EB, 0, MA)):
-            for i in range(16):
-                M(A("psc", m0, m0 + mc), sel(i), A("ind", base + i * mc, base + (i + 1) * mc), i == 0, i == 15)
+    def lists(s, far):
+        k, a, b = A("pkc", s * SLOT, s * SLOT + CAP), s * CAP, (s + 1) * CAP
+        if not far:
+            V("ts", A("lst", a, b), k, 0.5, -0.25, OP.mult, OP.add)
+        V("copy", A("i32", 0, CAP), k)
+        V("tt", A("xq", a, b), k, A("i32", 0, CAP), OP.subtract)
+        if far:
+            V("ts", A("shf", 0, CAP), A("i32", 0, CAP), FAR - 1, 1, OP.bitwise_and, OP.logical_shift_right)
+            V("ts", A("lst", a, b), A("shf", 0, CAP), float(W - 1), None, OP.min)
 
-    def targets(s):
-        V("ts", A("nq", 0, CAP), A("psc", 0, CAP), 7.5, float(ST), OP.is_lt, OP.mult)
-        V("tt", A("so", 0, CAP), A("nq", 0, CAP), A("vi", 0, CAP), OP.add)
-        V("copy", A("sof", 0, CAP), A("so", 0, CAP))
+    def targets(s, m0, mc, ps):
+        p = A(ps, m0, m0 + mc)
+        V("ts", p, p, 7.5, float(FARC), OP.is_lt, OP.mult)
+        V("tt", A("so", m0, m0 + mc), p, A("pkc", s * SLOT + m0, s * SLOT + m0 + mc), OP.add)
+        V("ts", A("sof", m0, m0 + mc), A("so", m0, m0 + mc), float(OFF), None, OP.add)
 
-    def numbers(s):
-        V("ts", A("vi", 0, CAP), A("pkc", s * SLOT, s * SLOT + CAP), (1 << XSH) - 1, None, OP.bitwise_and)
+    def scatter(q, m0, m1):
+        for a in range(m0, m1, SIN // 16):
+            b = min(m1, a + SIN // 16)
+            if q == "v":
+                V("copy", I(A("swv", 0, SWN), A("sof", a, b)), A("sin", 0, 16 * (b - a)))
+            else:
+                S(I(A("sws", 0, SWN), A("sof", a, b)), A("sin", 0, 16 * (b - a)), AF.Silu)
 
-    def scatter(vs):
-        V("copy", I(A("swv", 0, SWN), A("sof", 0, vs)), A("sin", 0, 16 * vs))
-        S(I(A("sws", 0, SWN), A("sof", vs, CAP)), A("sin", 0, 16 * (CAP - vs)), AF.Sigmoid)
+    def merge(c0, n, tmp, ps):
+        S(A(tmp, 0, 2 * n), A("sws", OFF + c0, OFF + c0 + 2 * n), AF.Copy)
+        p = A(ps, 0, n)
+        M(p, mat("idn"), A(tmp, 0, 2 * n, 2), True, False)
+        M(p, mat("idn"), A(tmp, 1, 2 * n, 2), False, False)
+        M(p, mat("idn"), A("swv", OFF + c0, OFF + c0 + 2 * n, 2), False, False)
+        M(p, mat("idn"), A("swv", OFF + c0 + 1, OFF + c0 + 2 * n, 2), False, True)
 
-    def tell(s):
-        S(A("swb", 0, 2 * NB), A("sws", 2 * P, ST), AF.Copy)
-        ps = A("psc", 0, NB)
-        M(ps, idn, A("swb", 0, 2 * NB, 2), True, False)
-        M(ps, idn, A("swb", 1, 2 * NB, 2), False, False)
-        M(ps, idn, A("swv", 2 * P, ST, 2), False, False)
-        M(ps, idn, A("swv", 2 * P + 1, ST, 2), False, True)
-        S(A("msg_f%d" % s, 0, NB), ps, AF.Copy)
+    def tell(s, q):
+        move(q, A("msg_f%d" % s, 0, NB), A("psf", 0, NB))
         send("f%d" % s)
 
-    def keep_y(s):
-        b = s * BS
-        V("tt", A("yb", b, b + BS), I(A("memn", 0, SLOT), A("offs", 16 * s, 16 * s + 16)), A("yw", b, b + BS), OP.mult)
-
-    def back_list(s):
-        a, b = s * CAP, (s + 1) * CAP
-        V("ts", A("lg", 0, CAP), A("shf", a, b), float(P), float(NB * (3 - s)), OP.is_ge, OP.mult)
-        V("tt", A("lf", 0, CAP), A("shf", a, b), A("lg", 0, CAP), OP.add)
-        V("ts", A("lsb", a, b), A("lf", 0, CAP), float(P + NB * (4 - s) - 1), None, OP.min)
-
     def members(s):
-        S(A("memr", s * BS, (s + 1) * BS), I(A("memc", 0, SLOT), A("offs", 16 * s, 16 * s + 16)), AF.Copy)
+        S(A("memr", s * BS, (s + 1) * BS), I(A("memi", 0, SLOT), A("offs", 16 * s, 16 * s + 16)), AF.Relu, scale=64.0)
 
-    def zero(name, c0, c1):
-        S(A(name, c0, c1), A("xw", 0, c1 - c0), AF.Copy, scale=0.0)
+    def places(s):
+        V("ts", A("lsf", (s - 1) * BS, s * BS), A("cdw", s * BS, (s + 1) * BS), 0.5, -0.25, OP.mult, OP.add)
 
-    wrap(16, [("sdrow", 0, 1)], "psm")
-    V("ts", bd, A("qp", 0, 128), 0.0, None, OP.is_ge)
-    V("ts", tri, A("qp", 0, 128), pmod, None, OP.is_ge)
-    V("ts", A("idx", 0, 128), idn, float(1 << XSH), None, OP.mult)
-    V("ts", A("nrow", 0, 16), A("c16", 0, 16), pmod, None, OP.add)
-    V("ts", A("nc", 0, 16), A("c16", 0, 16), pmod, 257.0, OP.add, OP.add)
+    xwin, awin, bwin = A("xw", 0, W), A("ya", Y0, Y0 + W), A("yb", Y0, Y0 + W)
+
+    H = ST // 2
+    V("memset", A("sdrow", 0, BS), 0.0)
+    dma("s", "dsnd", T.snd32[:, :], T.snd[:, :], [], [("snd32", 0, 24)])
+    dma("y", "dx", T.xw[:, 0:P], T.x[:, :], [], [("xw", 0, P)])
+    dma("y", "dtl", T.tlc[:, :], T.tl[:, :], [], [("tlc", 0, 1)])
+    dma("y", "dsd", T.sdrow[0:128:16, :], T.sd[:, :], [], [("sdrow", 0, BS)])
+    dma("y", "dcd0", T.cdw[:, 0:BS], T.cd[:, 0:BS], [], [("cdw", 0, BS)])
+    G("iota", A("pmi", 0, 1), [[0, 1]], 0, 1)
+    iota(mat("qp"), [[0, 8], [1, 16]], 0)
+    G("asel", mat("qp"), mat("qp"), [[-16, 8], [0, 16]], OP.is_ge, -1.0, 0, 1)
+    G("asel", mat("qp"), mat("qp"), [[16, 8], [0, 16]], OP.is_ge, -1.0, 15, -1)
+    iota(A("c32", 0, 16), [[32, 16]], 0)
+    iota(A("c32", 16, 32), [[-32, 16]], 0)
+    empty = lambda s: iota(A("pkc", s * SLOT, s * SLOT + CAP), [[-16, CAP]], -1, -1)
+    empty(0)
+    iota(A("i384", 0, HOLE), [[1, HOLE]], -HOLE)
+    iota(A("i384", HOLE, NB), [[1, NB - HOLE]], 16)
+    V("memset", A("swv", OFF + H, OFF + H + 1024), 0.0)
+    zs = [(OFF + a, min(1024, ST - a)) for a in range(0, ST, 1024)]
+    for k, (a, n) in enumerate(zs[:2]):
+        S(A("sws", a, a + n), A("swv", OFF + H, OFF + H + n), AF.Copy if k else AF.Silu)
+    V("memset", A("swv", OFF + H + 1024, OFF + ST), 0.0)
+    V("ts", A("pm2", 0, 1), A("pmi", 0, 1), 15, None, OP.bitwise_and)
+    V("copy", col(0), A("pm2", 0, 1))
+    pmod = col(0)
+    for a in range(16):
+        V("ts", sel(a), mat("qp"), float(a), None, OP.is_equal)
+    wrap(16, "sdrow", 0, "psm")
+    V("ts", mat("idn"), mat("qp"), pmod, None, OP.is_equal)
+    V("ts", mat("bd"), mat("qp"), 0.0, None, OP.is_ge)
+    V("ts", mat("tri"), mat("qp"), pmod, None, OP.is_gt)
+    V("ts", col(2), pmod, 2.0, 256.0, OP.mult, OP.add)
+    V("ts", mat("dg"), mat("idn"), col(2), -1.0, OP.mult, OP.mult)
+    V("ts", mat("ik"), mat("idn"), 1.0 / XF, None, OP.mult)
     V("memset", A("cs", 0, 1), 0.0)
-    V("memset", A("ones", 0, 16), 1.0)
+    V("memset", A("bp", BS, T4 * BS), 0.0)
+    V("copy", A("sndw", 0, 24), A("snd32", 0, 24))
+    border("x", "xw", 0)
+    V("memset", A("swv", OFF, OFF + H), 0.0)
+    for a, n in zs[2:]:
+        S(A("sws", a, a + n), A("swv", OFF + H, OFF + H + n), AF.Copy)
+    iota(A("sin", 0, SIN), [[0, SIN]], 1)
+    iota(A("nm", 0, BS), [[0, 16], [1, 16]], 0)
+    empty(1)
+    iota(A("memi", 0, SLOT), [[-1, SLOT]], CAP)
+    for s in range(3):
+        iota(A("land%d" % s, HOLE, HOLE + 16), [[0, 16]], 0)
+    wait_for("y", [arrival["x"]])
+    dma("y", "dcd1", T.cdw[:, BS:T4 * BS], T.cd[:, BS:T4 * BS], [], [("cdw", BS, T4 * BS)])
+    dma("y", "dya", T.ya[:, Y0:Y0 + P], T.y0[:, :], [], [("ya", Y0, Y0 + P)])
+    dma("y", "dyb", T.yb[:, Y0:Y0 + P], T.y0[:, :], [], [("yb", Y0, Y0 + P)])
+
+    V("ts", col(5), A("tlc", 0, 1), 2.0, 1.0, OP.mult, OP.add)
+    V("rec", col(6), col(5))
     V("ts", A("fw", 0, 16), A("psm", 0, 16), 0.5, None, OP.is_ge)
-    V("ts", A("pkd", 0, CAP), A("pkd0", 0, CAP), pmod, None, OP.add)
-    prefill(0)
-    pack(0)
+    pack(0, False)
+    ranks()
+    V("ts", mat("ndk"), mat("idn"), col(6), -XF, OP.mult, OP.mult)
     slots(0)
-    numbers(0)
-    border("y0", "yw", P)
-    V("copy", A("swv", 0, 2 * BS, 2), A("sdrow", 0, BS))
-    V("memset", A("bp", BS, 4 * BS), float(NB // 2))
-    for s in range(4):
-        if s:
-            ln = "land%d" % (s - 1)
-            V("tt", A("fb", 0, BS), I(A(ln, 0, NB + 16), A("bposw", 16 * (s - 1), 16 * s)), A("mask", 0, BS), OP.mult)
-            V("scan", A("fsc", 0, BS), A("seg0", 0, BS), A("fb", 0, BS), 0.0, OP.mult, OP.add)
-            V("tt", A("fw", 16 * s, 16 * s + 16), A("fsc", 15, BS, 16), A("nown", 16 * s, 16 * s + 16), OP.is_gt)
-            slots(s)
-        if s == 3:
-            break
-        match(s, "xw", W, "lst", (lambda s=s: numbers(s)) if s else None)
-        targets(s)
-        scatter(VS)
-        tell(s)
-        S(A("swo", 0, 2 * BS), A("sws", 2 * BS * (s + 1), 2 * BS * (s + 2)), AF.Copy)
+    lists(0, False)
+    ahead = lambda s: xpart(LOTS, "ndk", "xq", s * CAP, range(5))
+    ahead(0)
+    V("ts", mat("dr"), mat("idn"), col(6), None, OP.mult)
+    V("ts", mat("ndr"), mat("idn"), col(6), -1.0, OP.mult, OP.mult)
+    V("copy", A("swv", OFF, OFF + 2 * BS, 2), A("sdrow", 0, BS))
+
+    def outward(s, g1, g2, early, by_s=()):
+        c = s * CAP
+        gather("v", xwin, "lst", c, 0, g1)
+        gather("s", xwin, "lst", c, g1, MA)
+        cpart(LOTS, [0, 1])
+        gather("v", xwin, "lst", c, MA, g2)
+        gather("s", xwin, "lst", c, g2, CAP)
+        for u in (0, 1):
+            near(u); count(LOTS, u, "psm")
+        cpart(LOTS, [2, 3, 4])
+        targets(s, 0, MA, "psm")
+        for u in by_s:
+            near(u, "s")
+        scatter("s", 0, early)
+        for u in (2, 3, 4):
+            near(u, "l" if u in by_s else "v"); count(LOTS, u, "psc")
+        targets(s, MA, CAP - MA, "psc")
+
+    VS = PAR.get("VS", [72, 84, 84, 64])
+    outward(0, PAR.get("g1", 32), PAR.get("g2", 80), MA)
+    scatter("v", MA, MA + VS[0])
+    scatter("s", MA + VS[0], CAP)
+
+    wins = [xwin, xwin, awin]
+    fetch = lambda q, s, k: gather(q, wins[s], "lsf", BS * s, 64 * k, 64 * k + 64)
+    load = lambda s, us: xpart(ALL, "ndr", "xw", BS * (s + 1), us)
+    places(1)
+    load(0, range(5))
+    by_s = PAR.get("by_s", [(), (), ()])
+    for s in range(3):
+        merge(2 * P, NB, "swb", "psf")
         if s == 0:
+            if PAR.get("l0", "v") == "v":
+                fetch("v", 0, 0)
+                tell(0, "s")
+            else:
+                tell(0, "v")
+                fetch("s", 0, 0)
+            fetch("s", 0, 1)
             V("copy", I(A("bp", 0, P), A("sndw", 0, 24)), A("i384", 0, NB))
-            wrap(48, [("bp", BS, 1)], "psf")
-            V("ts", A("mask", 0, BS), A("nmod", 0, BS), pmod, None, OP.is_equal)
-            V("ts", A("seg0", 0, BS), A("nmod", 0, BS), 0.0, None, OP.not_equal)
-            V("ts", A("bposw", 0, 48), A("psf", 0, 48), 1.0 / 16, float(NB // 2), OP.mult, OP.add)
-        zero("land%d" % s, NB, NB + 16)
-        b = 2 * BS * (s + 1)
-        wrap(16, [("swv", b, 2), ("swv", b + 1, 2), ("swo", 0, 2), ("swo", 1, 2)], "psm")
-        prefill(s + 1)
-        pack(s + 1)
-        V("ts", A("nown", 16 * s + 16, 16 * s + 32), A("psm", 0, 16), 0.0, -1.0, OP.is_gt, OP.mult)
-        zero("vals", SLOT * s, SLOT * s + SLOT)
+            cpart(ALL, range(4))
+            wrap(48, "bp", BS, "psf")
+            empty(2)
+            iota(A("nb", 0, 48), [[16, 48]], Y0)
+            iota(A("d0", 0, 16 * (CAP - MA)), [[0, CAP - MA], [-256, 16]], 191)
+        if s and PAR.get("tq", "v") == "s":
+            tell(s, "s")
+        fetch("s", s, 2)
+        for u in range(8):
+            if s == 2 and u % 2 == 0:
+                low(32 * u, 32 * u + 64)
+            if u in by_s[s]:
+                near(u, "s"); near(u, "l")
+            else:
+                near(u)
+            if u == PAR.get("tu", 0) and s and PAR.get("tq", "v") == "v":
+                tell(s, "v")
+            if u == 1:
+                fetch("s", s, 3)
+            count(ALL, u, "psc")
+            if u < 3:
+                load(s, [u + 5])
+            if 1 <= u < 5:
+                cpart(ALL, [u + 3])
+            if u == 3:
+                merge(2 * BS * (s + 1), BS, "swo", "psm")
+                move("s", A("own", 0, BS), A("psm", 0, BS))
+            if u == 3 and s == 0:
+                V("ts", A("bposw", 0, 48), A("psf", 0, 48), 1.0 / 16, float(HOLE), OP.mult, OP.add)
+                V("ts", A("pm2", 1, 2), A("pmi", 0, 1), 1.0, None, OP.add)
+                V("ts", A("pm2", 0, 1), A("pm2", 1, 2), 15, None, OP.bitwise_and)
+                V("copy", col(1), A("pm2", 0, 1))
+                V("ts", A("dsel", 0, BS), A("nm", 0, BS), pmod, 64.0, OP.is_equal, OP.mult)
+                V("ts", A("dtm", 0, BS), A("nm", 0, BS), col(1), -16.0, OP.is_equal, OP.mult)
+                V("tt", A("dsel", 0, BS), A("dsel", 0, BS), A("dtm", 0, BS), OP.add)
+                V("ts", col(3), pmod, 15.0, 16.0, OP.is_ge, OP.mult)
+            if u == 4 and s < 2:
+                places(s + 2)
+                if s == 0:
+                    border("y0", "ya", Y0, 0)
+                fetch("s", s + 1, 0)
         if s == 1:
-            for name, u, w in (("memc", 64.0, 0.0), ("memn", 0.0, 1.0)):
-                V("memset", A(name, 0, CAP), u)
-                V("memset", A(name, CAP, SLOT), w)
-        for k in ([], [0, 1], [2])[s]:
-            back_list(k)
-            keep_y(k)
-            members(k)
-    for s in range(3, -1, -1):
-        def low(s=s):
-            V("scan", A("mn", 0, E), A("d0", 0, E), A("come", 0, E), 0.0, OP.max, OP.min)
-            if s == 3:
-                keep_y(3)
-            V("tt", A("hs", 0, CAP), A("mn", 15, E, 16), A("xmn", s * CAP, (s + 1) * CAP), OP.subtract)
-            V("ts", A("hv", 0, CAP), A("hs", 0, CAP), 1, None, OP.logical_shift_right)
-        match(s, "yw", P + NB * (4 - s), "lst" if s == 3 else "lsb", low)
-        if s == 3:
-            zero("vals", SLOT * 3, SLOT * 4)
-        V("ts", A("mt", 0, CAP), A("psc", 0, CAP), 7.5, None, OP.is_ge)
-        M(A("psm", 0, CAP), bd, A("mt", 0, CAP), True, True)
-        V("ts", A("dd", 0, CAP), A("psm", 0, CAP), 2.5, 255.0, OP.is_ge, OP.mult)
-        V("tt", A("vals", s * SLOT, s * SLOT + CAP), A("dd", 0, CAP), A("hv", 0, CAP), OP.max)
-        V("tt", A("yw", s * BS, (s + 1) * BS), I(A("vals", s * SLOT, (s + 1) * SLOT), A("offs", 16 * s, 16 * s + 16)),
-          A("yb", s * BS, (s + 1) * BS), OP.add)
+            empty(3)
+            iota(A("bp", 0, BS), [[0, BS]], 0)
+            iota(A("bp", T4 * BS, P), [[0, P - T4 * BS]], 0)
+            iota(A("yb", 0, Y0), [[0, Y0]], 0)
+        if s == 2:
+            iota(A("memr", T4 * BS, P), [[0, P - T4 * BS]], 0)
+            break
+        pack(s + 1, True)
+        fetch("s", s + 1, 1)
+        flags(s + 1)
+        ranks()
+        slots(s + 1)
+        V("ts", A("sof", 0, CAP), A("pkc", (s + 1) * SLOT, (s + 1) * SLOT + CAP), float(OFF), None, OP.add)
+        load(s + 1, range(5))
+        cpart(ALL, range(4))
+        scatter("s", VS[s + 1], CAP)
+        scatter("v", 0, VS[s + 1])
+        if s == 0:
+            V("ts", mat("hlf"), mat("idn"), 0.5, None, OP.mult)
+            V("ts", mat("ihk"), mat("idn"), XF / 2, None, OP.mult)
+            V("ts", mat("ihf"), mat("idn"), XF / 2, None, OP.mult)
+            V("ts", mat("bdk"), mat("bd"), 255.0, None, OP.mult)
+            V("ts", A("nb", 0, 48), A("nb", 0, 48), pmod, None, OP.add)
+            V("ts", col(4), col(2), -1.0, CAP - 0.5, OP.mult, OP.add)
+
+    def settle(s, win, out):
+        a = Y0 + s * BS
+        V("ts", A(out, a, a + BS), I(A(win, 0, a + BS), A("of2", 16 * s, 16 * s + 16)), 255.0, None, OP.min)
         if s:
-            border("y%d" % s, "yw", P)
-        dma("y", "oy%d" % s, T.yv[:, s * BS:(s + 1) * BS], T.yw[:, s * BS:(s + 1) * BS], [("yw", s * BS, (s + 1) * BS)], [])
-        if s == 3:
-            match(3, "xw", W, "lst", lambda: numbers(3))
-            targets(3)
-            members(3)
-        elif s == 2:
-            scatter(VS3)
-            V("memset", A("rw", 0, P), 0.0)
-        elif s == 1:
-            tell(3)
-            dma("g", "gcast", T.swc[:, :], T.sws[:, 0:2 * P], [("sws", 0, 2 * P)], [("swc", 0, 2 * P)])
-            for st in range(2):
-                for h in range(16):
-                    M(A("psf", 0, LW), sel(h), A("swv", 2 * LW * h + st, 2 * LW * (h + 1), 2), st == 0 and h == 0, False)
-            for h in range(7):
-                n = min(LW, T4 * BS - LW * h)
-                M(A("psf", 0, n), sel(h), A("memr", LW * h, LW * h + n), False, False)
-    for st in range(2):
-        for h in range(16):
-            M(A("psf", 0, LW), sel(h), A("swc", 2 * LW * h + st, 2 * LW * (h + 1), 2), False, False)
-    V("copy", I(A("rw", 0, P), A("sndw", 0, 24)), A("land3", 0, NB))
-    for h in range(16):
-        M(A("psf", 0, LW), sel(h), A("rw", LW * h, LW * (h + 1)), False, h == 15)
-    V("ts", A("yf1", 0, LW), A("psf", 0, LW), 0.0, None, OP.is_gt)
-    V("ts", A("yf2", 0, LW), A("psf", 0, LW), 500.0, None, OP.is_ge)
-    V("tt", A("yfs", 0, LW), A("yf1", 0, LW), A("yf2", 0, LW), OP.add)
-    dma("y", "oyf", T.yf[:, :], T.yfs[:, :], [("yfs", 0, LW)], [])
+            border("y%d" % s, out, Y0)
+            wait_for("y", [arrival["y%d" % s]])
+        dma("y", "oy%d" % s, T.yv[:, s * BS:(s + 1) * BS], T[out][:, a:a + BS], [(out, a, a + BS)], [])
+
+    def inward(s, win, name):
+        c, g1, g2 = s * CAP, PAR.get("b1", 32), PAR.get("b2", 88)
+        gather("v", win, "lst", c, 0, g1)
+        gather("s", win, "lst", c, g1, MA)
+        cpart(LOTS, [0, 1])
+        gather("v", win, "lst", c, MA, g2)
+        gather("s", win, "lst", c, g2, CAP)
+        for u in (0, 1):
+            near(u); count(LOTS, u, "psc")
+        cpart(LOTS, [2, 3, 4])
+        low(0, MA)
+        by_s = PAR.get("b3", (2, 3, 4))
+        for u in by_s:
+            near(u, "s")
+        low(MA, CAP)
+        near(2, "l" if 2 in by_s else "v"); count(LOTS, 2, "psc")
+        halves(CAP, "ihk", A("xq", c, c + CAP), "psm")
+        for u in (3, 4):
+            near(u, "l" if u in by_s else "v"); count(LOTS, u, "psc")
+        fresh(CAP, name)
+
+    def part(name, src, c0, n):
+        dma("y", "d" + name, T[name][:, :], T[src][0:128:16, c0:c0 + n], [(src, c0, c0 + n)], [(name, 0, n // 16)])
+
+    for s in range(3):
+        members(s)
+    halves(BS, "hlf", A("xw", 3 * BS, 4 * BS), "psf")
+    fresh(BS, "ya")
+    pack(3, False)
+    flags(3)
+    ranks()
+    V("ts", A("oa", 0, 16), A("psm", 0, 16), col(4), 1024.0, OP.is_ge, OP.mult)
+    V("tt", A("ob", 0, 16), A("oa", 0, 16), A("nb", 0, 16), OP.add)
+    V("ts", A("of2", 48, 64), A("ob", 0, 16), -float(Y0), None, OP.add)
+    settle(3, "ya", "yb")
+    expect("y2")
+    slots(3)
+    lists(3, False)
+    ahead(3)
+    members(3)
+    lists(2, True)
+    outward(3, PAR.get("h1", 0), PAR.get("h2", MA), 0, PAR.get("h3", ()))
+    ahead(2)
+    V("ts", A("oa", 0, 48), A("offs", 0, 48), CAP - 0.5, 2048.0, OP.is_ge, OP.mult)
+    V("copy", A("ob", 0, 48), A("offs", 0, 48))
+    V("tt", A("oa", 0, 48), A("oa", 0, 48), A("ob", 0, 48), OP.add)
+    V("tt", A("ob", 0, 48), A("oa", 0, 48), A("nb", 0, 48), OP.min)
+    V("copy", A("of2", 0, 48), A("ob", 0, 48))
+    V("copy", A("ya", Y0 + 3 * BS, Y0 + 4 * BS), A("yb", Y0 + 3 * BS, Y0 + 4 * BS))
+    inward(2, bwin, "yb")
+    s3 = PAR.get("s3", 32)
+    scatter("s", VS[3], VS[3] + s3)
+    settle(2, "yb", "ya")
+    expect("y1")
+    lists(1, True)
+    ahead(1)
+    scatter("s", VS[3] + s3, CAP)
+    scatter("v", 0, VS[3])
+    V("copy", A("yb", Y0 + 2 * BS, Y0 + 3 * BS), A("ya", Y0 + 2 * BS, Y0 + 3 * BS))
+    part("fv", "swv", OFF, 2 * P)
+    part("fs", "sws", OFF, 2 * P)
+    part("fm", "memr", 0, P)
+    if PAR.get("t3", 0) == 0:
+        merge(2 * P, NB, "swb", "psf")
+        tell(3, "s")
+    inward(1, awin, "ya")
+    if PAR.get("t3", 0) == 1:
+        merge(2 * P, NB, "swb", "psf")
+        tell(3, "s")
+    settle(1, "ya", "yb")
+    ahead(0)
+    V("copy", I(A("bp", 0, P), A("sndw", 0, 24)), A("land3", 0, NB))
+    part("fr", "bp", 0, P)
+    inward(0, bwin, "yb")
+    settle(0, "yb", "ya")
+    terms = [("ihk", "fv", 0, 2), ("ihk", "fv", 1, 2), ("ihf", "fs", 0, 2), ("ihf", "fs", 1, 2), ("ihk", "fm", 0, 1), ("ihk", "fr", 0, 1)]
+    for k, (m, name, c0, step) in enumerate(terms):
+        M(A("psf", 0, LW), mat(m), A(name, c0, step * LW, step), k == 0, k == len(terms) - 1)
+    V("ts", A("yf1", 0, LW), A("psf", 0, LW), 10000.0, 1.0, OP.is_ge, OP.add)
+    V("tt", A("yfs", 0, LW), A("psf", 0, LW), A("yf1", 0, LW), OP.min)
+    dma("s", "oyf", T.yf[:, :], T.yfs[:, :], [("yfs", 0, LW)], [])
     for sname in SEMAPHORES:
         if cnt.get(sname, 0) and know["g"].get(sname, 0) < cnt[sname]:
             g.wait_ge(T.sem[sname], cnt[sname])

@@ -7,8 +7,6 @@ W = P + NB
 ST = S2 * W
 MA = 64
 LOTS = [(0, MA), (MA, CAP - MA)]
-ALL = [(64 * k, 64) for k in range(4)]
-RING = 5 * 512
 OFF = 2816
 FAR, FARC = 8192, 8320
 SWN = OFF + FARC + ST
@@ -19,22 +17,24 @@ Y0 = 256
 HOLE = 256
 LW = 148
 MAGIC = 12582912.0
-PAR = {'VS': [64, 80, 72, 64], 'by_s': [(), (), ()], 'l0': 'v', 'tq': 'v', 'tu': 2, 'b1': 32, 'b2': 80, 'b3': (2, 3, 4), 'h1': 0, 'h2': 64, 'h3': (), 's3': 48, 't3': 0, 'g1': 32, 'g2': 80}
+PAR = dict(whole=(1, 2), cb=3, gp=32, sp=16, absd=0.0, first3="b", mb="swb", mo=None, dz=1, lam=1.0, rest=0.5, turns=6,
+           cyc=0.92, pe=0.35, fix=0.06, gam=1.15, sig=3.1, hop=0.08, pel=0.18, net=3.9, dma=1.5)
 
 B16, F32, I32, U16 = "bfloat16", "float32", "int32", "uint16"
 SCRATCH = {}
 for _n, _c, _d in [
         ("xw", W, B16), ("ya", Y0 + W, B16), ("yb", Y0 + W, B16), ("cdw", T4 * BS, I32), ("snd32", 24, I32), ("sndw", 24, U16),
         ("tlc", 1, B16), ("sdrow", BS, B16), ("swv", SWN, B16), ("sws", SWN, F32), ("swb", 2 * NB, B16),
-        ("swo", 2 * BS, B16), ("own", BS, B16), ("sin", SIN, F32), ("come", 16 * BS, B16), ("ab", 1536, B16), ("ind", RING, B16),
-        ("mn", 16 * BS, B16), ("d0", 16 * (CAP - MA), B16), ("pk", BS, F32), ("pkc", T4 * SLOT, F32), ("sel", 16 * 128, B16),
-        ("qp", 128, B16), ("bd", 128, B16), ("bdk", 128, B16), ("tri", 128, B16), ("dg", 128, B16), ("idn", 128, B16),
-        ("dr", 128, B16), ("ndr", 128, B16), ("ndk", 128, B16), ("hlf", 128, B16), ("ihk", 128, B16), ("ihf", 128, F32),
-        ("ik", 128, B16), ("pmi", 1, I32), ("pm2", 2, I32), ("col", 8, F32), ("nm", BS, B16), ("dsel", BS, B16), ("dtm", BS, B16),
-        ("c32", 32, B16), ("nb", 48, F32), ("i384", NB, B16), ("bp", P, B16), ("bposw", 48, U16), ("fw", 16, B16), ("fb", BS, B16),
-        ("fsc", BS, B16), ("cs", 32, B16), ("tp", 16, B16), ("offs", 64, U16), ("of2", 64, U16), ("oa", 48, F32), ("ob", 48, F32),
-        ("lsf", 3 * BS, U16), ("lst", T4 * CAP, U16), ("i32", CAP, I32), ("shf", CAP, I32), ("xq", T4 * CAP, B16), ("t1", BS, B16),
-        ("so", CAP, F32), ("sof", CAP, U16), ("mt", BS, B16), ("hv", BS, I32), ("memi", SLOT, B16), ("memr", P, B16),
+        ("swo", 2 * BS, B16), ("own", BS, B16), ("sin", SIN, F32), ("come", 16 * CAP, B16), ("cw", 32 * BS, B16), ("ab", 2560, B16),
+        ("ind", 7 * 512, B16), ("mn", 16 * BS, B16), ("d0", 16 * (CAP - MA), B16), ("pk", BS, F32), ("pkc", T4 * SLOT, F32),
+        ("sel", 144, B16), ("qp", 144, B16), ("idf", 128, F32), ("bd", 128, B16), ("bdk", 128, B16), ("tri", 128, B16),
+        ("dg", 128, B16), ("idn", 128, B16), ("dr", 128, B16), ("ndr", 128, B16), ("ndk", 128, B16), ("hlf", 128, B16),
+        ("ihk", 128, B16), ("ihf", 128, F32), ("ik", 128, B16), ("pmi", 1, I32), ("pm2", 1, I32), ("col", 8, F32),
+        ("nm", BS + 16, B16), ("dsel", BS, B16), ("dtm", BS, B16), ("c32", 32, B16), ("nb", 48, F32), ("i384", NB, B16),
+        ("bp", P, B16), ("bposw", 48, U16), ("fw", 16, B16), ("fb", BS, B16), ("fsc", BS, B16), ("cs", 32, B16), ("tp", 16, B16),
+        ("offs", 64, U16), ("of2", 64, U16), ("oa", 64, F32), ("ob", 64, F32), ("lsf", 3 * BS, U16), ("lst", 4 * CAP, U16),
+        ("i32", CAP, I32), ("shf", CAP, I32), ("xq", 4 * CAP, B16), ("t1", BS, B16), ("so", CAP, F32), ("sof", CAP, U16),
+        ("mt", BS, B16), ("hv", BS, I32), ("memi", SLOT, B16), ("memr", P, B16),
         ("fv", 2 * LW, B16), ("fs", 2 * LW, F32), ("fr", LW, B16), ("fm", LW, B16), ("yf1", LW, F32), ("yfs", LW, B16)]:
     SCRATCH[_n] = ("sbuf", [128, _c], _d)
 EX = ["x", "y0", "f0", "f1", "f2", "f3", "y3", "y2", "y1"]
@@ -45,7 +45,7 @@ for _s in range(4):
 PSB = ["pd0", "pd1", "pd2", "pd3", "pd4", "psc", "psm", "psf"]
 for _b in PSB:
     SCRATCH[_b] = ("psum", [128, 512], F32)
-DMAS = ["dx", "dsnd", "dsd", "dtl", "dcd0", "dcd1", "dya", "dyb", "dfv", "dfs", "dfr", "dfm", "oy0", "oy1", "oy2", "oy3", "oyf"]
+DMAS = ["dx", "dsnd", "dsd", "dtl", "dcd0", "dcd1", "dya", "dyb", "dz", "dfv", "dfs", "dfr", "dfm", "oy0", "oy1", "oy2", "oy3", "oyf"]
 SEMAPHORES = ["sv", "ss", "st", "sg", "snt"] + DMAS + ["arr_" + _e for _e in EX]
 
 
@@ -62,25 +62,530 @@ def lanes(src, cores, topo):
     return res
 
 
+def A(name, c0, c1, step=1):
+    return (name, c0, c1, step, None)
+
+
+def I(win, off):
+    return win[:4] + (off,)
+
+
+def elems(a):
+    return 16 * (a[4][2] - a[4][1]) if a[4] else len(range(a[1], a[2], a[3]))
+
+
+def touched(call):
+    if call[1] in ("dma", "send"):
+        return call[4]["reads"], call[4]["writes"]
+    out, ops = call[2], [x for x in list(call[3]) + list(call[4].values()) if isinstance(x, tuple)]
+    return [x[:3] for x in ops] + [x[4][:3] for x in ops + [out] if x[4]], [out[:3]]
+
+
+def lasts(call):
+    q, fn, out, ins = call[:4]
+    if fn in ("dma", "send"):
+        return 0.05 if fn == "dma" else 0.5
+    n, ops = elems(out), [x for x in (out,) + tuple(ins) if isinstance(x, tuple)]
+    if q == "t":
+        return max(64, n) * PAR["pe"] * (4 if SCRATCH[ins[0][0]][2] == F32 else 1) / 1000
+    if q == "g":
+        return 0.15 + 2 * n * PAR["cyc"] / 1000
+    if out[4] or (len(ops) > 1 and ops[1][4]):
+        return 0.06 + n * PAR["sig" if out[4] else "gam"] / 1000
+    narrow = all(SCRATCH[x[0]][2] in (B16, U16) for x in ops if elems(x) > 1)
+    per = 1 if q == "s" else (1 if any(x[0] in PSB for x in ops) else 2) if fn == "tt" else 0.5 if narrow else 1
+    return PAR["fix"] + max(64, n * per) * PAR["cyc"] / 1000 + (1.3 if fn == "act" and ins[1] == AF.Silu else 0)
+
+
+def plan():
+    tasks = []
+
+    def task(*ways, after=(), pool=None, lag=0.0):
+        rd, wr = set(), set()
+        for way in ways:
+            for step in way:
+                for c in step:
+                    r, w = touched(c)
+                    rd.update(r); wr.update(w)
+        tasks.append(dict(ways=ways, rd=rd, wr=wr, after=after, pool=pool, lag=lag))
+        return len(tasks) - 1
+
+    V = lambda fn, out, *a: task([[("v", fn, out, a, {})]])
+    sc = lambda out, in_, f, **k: ("s", "act", out, (in_, f), k)
+    S = lambda out, in_, f, **k: task([[sc(out, in_, f, **k)]])
+    mm = lambda out, l, r, a, b: ("t", "mm", out, (l, r, a, b), {})
+    PE = lambda calls: task([calls])
+    iota = lambda out, pat, base, cm=0: task([[("g", "iota", out, (pat, base, cm), {})]])
+    asel = lambda out, *a: task([[("g", "asel", out, (out,) + a, {})]])
+    sel = lambda a: A("sel", 15 - a, 143 - a)
+    mat = lambda n: A(n, 0, 128)
+    col = lambda j: A("col", j, j + 1)
+    mv = lambda q, out, in_: ("v", "copy", out, (in_,), {}) if q == "v" else sc(out, in_, AF.Copy)
+    move = lambda out, in_: task([[mv("v", out, in_)]], [[mv("s", out, in_)]])
+
+    def dma(sem, out, in_, reads, writes, kb, after=(), q="y"):
+        return task([[(q, "dma", sem, (out, in_), dict(reads=reads, writes=writes))]], after=after, lag=PAR["dma"] + kb / 300)
+
+    def zero(name, c0, c1):
+        for a in range(c0, c1, 512):
+            iota(A(name, a, min(c1, a + 512)), [[0, min(c1, a + 512) - a]], 0)
+
+    def pool(make, m0, m1, size, most, end=None):
+        key = (make, m0, most)
+        for a in range(m0, m1, size):
+            k = task([[make("v", m0, m1)]], [[make("s", m0, m1)]], pool=key)
+            tasks[k]["ways"] = tuple([[make(q, a, min(m1, a + size))]] for q in "vs")
+            tasks[k]["rest"] = PAR["rest"] * lasts(make("v", a, end or m1))
+
+    sent = {}
+
+    def send(e):
+        land = [(landing(e, d)[0], landing(e, d)[1], landing(e, d)[1] + GB) for d in range(1, N)]
+        sent[e] = task([[("g", "send", e, (), dict(reads=[("msg_" + e, 0, NB)], writes=land))]], lag=PAR["net"] + (1 if e == "x" else 0))
+
+    def border(e, src, c0):
+        pool(lambda q, a, b: mv(q, A("msg_" + e, 16 * a, 16 * b), I(A(src, c0, c0 + P), A("sndw", a, b))), 0, NB // 16, NB // 32, NB // 16)
+        send(e)
+
+    def wrap(c1, name, c0, ps):
+        PE([mm(A(ps, 0, c1), sel(a), A(name, c0 + a, c0 + 16 * (c1 - 1) + a + 1, 16), a == 0, a == 15) for a in range(16)])
+
+    CB = PAR["cb"]
+
+    def pieces(u):
+        m0, mc = LOTS[0] if 512 * u < 16 * MA else LOTS[1]
+        for i in range(16):
+            lo = 16 * m0 + i * mc
+            a, b = max(lo, 512 * u), min(lo + mc, 512 * u + 512)
+            if a < b:
+                yield i, m0 + a - lo, m0 + b - lo, A("pd%d" % (u % CB), a % 512, a % 512 + b - a), a % 512 == 0, b % 512 == 0
+
+    def near(k, slot):
+        out, ps, ab = A("ind", 512 * slot, 512 * slot + 512), A("pd%d" % k, 0, 512), A("ab", 512 * k, 512 * k + 512)
+        task([[("v", "ts", out, (ps, MAGIC, MAGIC, OP.add, OP.is_equal), {})]],
+             [[sc(ab, ps, AF.Abs)], [("v", "ts", out, (ab, 0.5, None, OP.is_lt), {})]])
+
+    def low(m0, m1, src, e0):
+        V("scan", A("mn", 16 * m0, 16 * m1), A("d0", 0, 16 * (m1 - m0)), A(src, e0, e0 + 16 * (m1 - m0)), 0.0, OP.max, OP.min)
+
+    def match(s, win, back):
+        c = s * CAP
+        for m0, mc in LOTS:
+            pool(lambda q, a, b: mv(q, A("come", 16 * a, 16 * b), I(win, A("lst", c + a, c + b))), m0, m0 + mc, PAR["gp"], 256)
+        for u in range(5):
+            PE([mm(out, mat("ndk"), A("xq", c + a, c + b), first, False) for i, a, b, out, first, last in pieces(u)])
+            PE([mm(out, mat("dr"), A("come", 16 * a + i, 16 * (b - 1) + i + 1, 16), False, last) for i, a, b, out, first, last in pieces(u)])
+            near(u % CB, u)
+            m0, mc = LOTS[0] if u < 2 else LOTS[1]
+            ps = "psc" if back else "psm" if u < 2 else "psf"
+            PE([mm(A(ps, m0, m0 + mc), sel(i), A("ind", 16 * m0 + i * mc, 16 * m0 + (i + 1) * mc), i == 0, i == 15)
+                for i in range(16) if (16 * m0 + (i + 1) * mc - 1) // 512 == u])
+            if u in (1, 4):
+                if back:
+                    low(m0, m0 + mc, "come", 16 * m0)
+                else:
+                    targets(s, ps, m0, mc)
+
+    def targets(s, ps, m0, mc):
+        p = A(ps, m0, m0 + mc)
+        V("ts", p, p, 7.5, float(FARC), OP.is_lt, OP.mult)
+        V("tt", A("so", m0, m0 + mc), p, A("pkc", s * SLOT + m0, s * SLOT + m0 + mc), OP.add)
+        V("ts", A("sof", m0, m0 + mc), A("so", m0, m0 + mc), float(OFF), None, OP.add)
+        scatter(m0, m0 + mc)
+
+    ring = [0, 0]
+
+    def aside(n, lst, l0, m, xn, x0, win, ps, c0, then=None):
+        for m0 in range(0, n, 64):
+            mc, e0 = min(64, n - m0), 1024 * (ring[1] % 8)
+            ring[1] += 1
+            x, per = A(xn, x0 + m0, x0 + m0 + mc), 512 // mc
+            pool(lambda q, a, b, e0=e0, m0=m0: mv(q, A("cw", e0 + 16 * a, e0 + 16 * b), I(win, A(lst, l0 + m0 + a, l0 + m0 + b))),
+                 0, mc, PAR["gp"], 256)
+            for i0 in range(0, 16, per):
+                b = CB + ring[0] % (5 - CB)
+                slot = 5 + ring[0] % 2
+                ring[0] += 1
+                out = lambda j: A("pd%d" % b, mc * j, mc * j + mc)
+                PE([mm(out(j), mat(m), x, j == 0, False) for j in range(per)])
+                PE([mm(out(j), mat("dr"), A("cw", e0 + i0 + j, e0 + i0 + j + 16 * (mc - 1) + 1, 16), False, j == per - 1) for j in range(per)])
+                near(b, slot)
+                PE([mm(A(ps, c0 + m0, c0 + m0 + mc), sel(i0 + j), A("ind", 512 * slot + mc * j, 512 * slot + mc * j + mc),
+                       i0 + j == 0, i0 + j == 15) for j in range(per)])
+            if then:
+                then(m0, mc, e0)
+
+    def whole(s, win, c0, back):
+        aside(BS, "lsf", (s - 1) * BS, "ndr", "xw", s * BS, win, "psc", c0, (lambda m0, mc, e0: low(m0, m0 + mc, "cw", e0)) if back else None)
+
+    def fresh(n, m, x, win, c0):
+        PE([mm(A("psm", 0, n), mat(m), x, True, False), mm(A("psm", 0, n), mat("hlf"), A("mn", 15, 16 * n, 16), False, True)])
+        V("ts", A("hv", 0, n), A("psm", 0, n), -0.25, None, OP.add)
+        V("ts", A("mt", 0, n), A("psc", c0, c0 + n), 7.5, -0.125, OP.is_ge, OP.add)
+        PE([mm(A("psm", 0, n), mat("bdk"), A("mt", 0, n), True, True)])
+        V("tt", A(win, 0, n), A("psm", 0, n), A("hv", 0, n), OP.max)
+
+    def pack(s, c0=None):
+        b = s * BS
+        calls = [mm(A("psf", 0, BS), mat("ik"), A("xw", b, b + BS), True, c0 is None)]
+        if c0 is not None:
+            V("ts", A("t1", 0, BS), A("psc", c0, c0 + BS), 7.5, float(FAR), OP.is_lt, OP.mult)
+            calls.append(mm(A("psf", 0, BS), mat("idn"), A("t1", 0, BS), False, True))
+        PE(calls)
+        V("tt", A("pk", 0, BS), A("psf", 0, BS), A("cdw", b, b + BS), OP.add)
+
+    def flags(s):
+        V("tt", A("fb", 0, BS), I(A("land%d" % (s - 1), 0, NB + 16), A("bposw", 16 * (s - 1), 16 * s)), A("own", 0, BS), OP.add)
+        V("scan", A("fsc", 0, BS), A("dsel", 0, BS), A("fb", 0, BS), 0.0, OP.add, OP.min)
+        V("ts", A("fw", 0, 16), A("fsc", 15, BS, 16), col(3), -15.7, OP.subtract, OP.is_gt)
+
+    def ranks():
+        f, p = A("fw", 0, 16), A("psm", 0, 16)
+        V("scan", A("cs", 1, 17), A("c32", 16, 32), f, 0.0, OP.max, OP.add)
+        V("tt", A("tp", 0, 16), f, A("c32", 16, 32), OP.mult)
+        PE([mm(p, mat("idn"), A("c32", 0, 16), True, False), mm(p, mat("tri"), f, False, False), mm(p, mat("dg"), f, False, False)])
+        PE([mm(p, mat("bd"), A("cs", 0, 16), False, False), mm(p, mat("idn"), A("tp", 0, 16), False, True)])
+
+    def slots(s):
+        V("ts", A("offs", 16 * s, 16 * s + 16), A("psm", 0, 16), col(2), None, OP.add)
+        V("copy", I(A("pkc", s * SLOT, (s + 1) * SLOT), A("offs", 16 * s, 16 * s + 16)), A("pk", 0, BS))
+
+    def lists(s, far):
+        k, a, b = A("pkc", s * SLOT, s * SLOT + CAP), s * CAP, (s + 1) * CAP
+        if not far:
+            V("ts", A("lst", a, b), k, 0.5, -0.25, OP.mult, OP.add)
+        V("copy", A("i32", 0, CAP), k)
+        V("tt", A("xq", a, b), k, A("i32", 0, CAP), OP.subtract)
+        if far:
+            V("ts", A("shf", 0, CAP), A("i32", 0, CAP), FAR - 1, 1, OP.bitwise_and, OP.logical_shift_right)
+            V("ts", A("lst", a, b), A("shf", 0, CAP), float(W - 1), None, OP.min)
+
+    def scatter(m0, m1):
+        def make(q, a, b):
+            if q == "v":
+                return mv("v", I(A("swv", 0, SWN), A("sof", a, b)), A("sin", 0, min(SIN, 16 * (b - a))))
+            return sc(I(A("sws", 0, SWN), A("sof", a, b)), A("sin", 0, min(SIN, 16 * (b - a))), AF.Silu)
+        pool(make, m0, m1, PAR["sp"], SIN // 16, CAP)
+
+    def known(s):
+        V("ts", A("sof", 0, CAP), A("pkc", s * SLOT, s * SLOT + CAP), float(OFF), None, OP.add)
+        scatter(0, CAP)
+
+    def merge(c0, n, tmp, ps, out):
+        p = A(ps, 0, n)
+        if tmp:
+            move(A(tmp, 0, 2 * n), A("sws", OFF + c0, OFF + c0 + 2 * n))
+        terms = [("idn", "swv", OFF + c0), ("idn", tmp, 0) if tmp else ("idf", "sws", OFF + c0)]
+        for k, (m, name, a) in enumerate(terms):
+            PE([mm(p, mat(m), A(name, a, a + 2 * n, 2), k == 0, False), mm(p, mat(m), A(name, a + 1, a + 2 * n, 2), False, k == 1)])
+        move(out, p)
+
+    def tell(s):
+        merge(2 * P, NB, PAR["mb"], "psf", A("msg_f%d" % s, 0, NB))
+        send("f%d" % s)
+
+    def members(s):
+        S(A("memr", s * BS, (s + 1) * BS), I(A("memi", 0, SLOT), A("offs", 16 * s, 16 * s + 16)), AF.Relu, scale=64.0)
+
+    def places(s):
+        V("ts", A("lsf", (s - 1) * BS, s * BS), A("cdw", s * BS, (s + 1) * BS), 0.5, -0.25, OP.mult, OP.add)
+
+    def settle(s, win, out):
+        a = Y0 + s * BS
+        V("ts", A(out, a, a + BS), I(A(win, 0, a + BS), A("of2", 16 * s, 16 * s + 16)), 255.0, None, OP.min)
+        if s:
+            border("y%d" % s, out, Y0)
+        dma("oy%d" % s, ("yv", slice(None), s * BS, (s + 1) * BS), (out, slice(None), a, a + BS), [(out, a, a + BS)], [], 64,
+            after=[sent["y%d" % s]] if s else [])
+
+    def part(name, src, c0, n):
+        dma("d" + name, (name, slice(None), 0, n // 16), (src, slice(0, 128, 16), c0, c0 + n), [(src, c0, c0 + n)], [(name, 0, n // 16)], 100)
+
+    def load(sem, name, c0, src, a, b, kb, after=(), q="y", rows=slice(None)):
+        return dma(sem, (name, rows, c0, c0 + b - a), (src, slice(None), a, b), [], [(name, c0, c0 + b - a)], kb, after, q)
+
+    xwin, awin, bwin = A("xw", 0, W), A("ya", Y0, Y0 + W), A("yb", Y0, Y0 + W)
+    H, pmod, qp = ST // 2, col(0), A("qp", 0, 144)
+
+    V("memset", A("sdrow", 0, BS), 0.0)
+    load("dsnd", "snd32", 0, "snd", 0, 24, 20, q="s")
+    dx = load("dx", "xw", 0, "x", 0, P, 600)
+    load("dtl", "tlc", 0, "tl", 0, 1, 700)
+    load("dsd", "sdrow", 0, "sd", 0, BS, 700, rows=slice(0, 128, 16))
+    load("dcd0", "cdw", 0, "cd", 0, BS, 900)
+    iota(A("pmi", 0, 1), [[0, 1]], 0, 1)
+    iota(qp, [[0, 9], [1, 16]], 0)
+    asel(qp, [[-16, 9], [0, 16]], OP.is_ge, -1.0, 0, 1)
+    asel(qp, [[16, 9], [0, 16]], OP.is_ge, -1.0, 15, -1)
+    iota(A("c32", 0, 16), [[32, 16]], 0)
+    iota(A("c32", 16, 32), [[-32, 16]], 0)
+    for s in range(4):
+        iota(A("pkc", s * SLOT, s * SLOT + CAP), [[-16, CAP]], -1, -1)
+    iota(A("i384", 0, HOLE), [[1, HOLE]], -HOLE)
+    iota(A("i384", HOLE, NB), [[1, NB - HOLE]], 16)
+    iota(A("nm", 0, BS + 16), [[0, 17], [1, 16]], 0)
+    for a in range(0, SIN, 512):
+        iota(A("sin", a, a + 512), [[0, 512]], 1)
+        iota(A("d0", a, a + 512), [[0, 32], [-256, 16]], 191)
+    for a in range(0, SLOT, 512):
+        iota(A("memi", a, a + 512), [[-1, 512]], CAP - a)
+    for s in range(3):
+        zero("land%d" % s, HOLE, HOLE + 16)
+    iota(A("nb", 0, 48), [[16, 48]], Y0)
+    zero("yb", 0, Y0)
+    zero("memr", T4 * BS, P)
+    for a in range(OFF + H, OFF + ST, 688):
+        V("memset", A("swv", a, a + 688), 0.0)
+    for k, a in enumerate(range(OFF, OFF + ST, 688)):
+        S(A("sws", a, a + 688), A("swv", OFF + H, OFF + H + 688), AF.Copy if k else AF.Silu)
+    V("memset", A("swv", OFF, OFF + 2 * BS), 0.0)
+    V("ts", A("pm2", 0, 1), A("pmi", 0, 1), 15, None, OP.bitwise_and)
+    V("copy", pmod, A("pm2", 0, 1))
+    V("ts", A("sel", 0, 144), qp, 15.0, None, OP.is_equal)
+    V("ts", mat("idn"), mat("qp"), pmod, None, OP.is_equal)
+    V("ts", mat("bd"), mat("qp"), 0.0, None, OP.is_ge)
+    V("ts", mat("tri"), mat("qp"), pmod, None, OP.is_gt)
+    V("ts", col(2), pmod, 2.0, 256.0, OP.mult, OP.add)
+    V("ts", mat("dg"), mat("idn"), col(2), -1.0, OP.mult, OP.mult)
+    for name, f in (("ik", 1.0 / XF), ("hlf", 0.5), ("ihk", XF / 2), ("ihf", XF / 2), ("idf", 1.0)):
+        V("ts", mat(name), mat("idn"), f, None, OP.mult)
+    V("ts", mat("bdk"), mat("bd"), 255.0, None, OP.mult)
+    V("ts", col(4), col(2), -1.0, CAP - 0.5, OP.mult, OP.add)
+    V("ts", col(3), pmod, 15.0, 16.0, OP.is_ge, OP.mult)
+    V("ts", A("nb", 0, 48), A("nb", 0, 48), pmod, None, OP.add)
+    V("memset", A("cs", 0, 1), 0.0)
+    V("copy", A("sndw", 0, 24), A("snd32", 0, 24))
+    border("x", "xw", 0)
+    z = (OFF + 2 * BS, OFF + H, OFF + H, OFF + ST - 2 * BS)
+    if PAR["dz"]:
+        dma("dz", ("swv", slice(None), z[0], z[1]), ("swv", slice(None), z[2], z[3]), [("swv", z[2], z[3])], [("swv", z[0], z[1])], 600, [sent["x"]])
+    else:
+        for a in range(z[0], z[1], 560):
+            V("memset", A("swv", a, a + 560), 0.0)
+    load("dcd1", "cdw", BS, "cd", BS, T4 * BS, 1000, [sent["x"]])
+    load("dya", "ya", Y0, "y0", 0, P, 1600, [sent["x"]])
+    load("dyb", "yb", Y0, "y0", 0, P, 2200, [sent["x"]])
+    V("ts", col(5), A("tlc", 0, 1), 2.0, 1.0, OP.mult, OP.add)
+    V("rec", col(6), col(5))
+    for name, f in (("ndk", -XF), ("dr", 1.0), ("ndr", -1.0)):
+        V("ts", mat(name), mat("idn"), col(6), f, OP.mult, OP.mult)
+    V("copy", A("swv", OFF, OFF + 2 * BS, 2), A("sdrow", 0, BS))
+    V("ts", A("dsel", 0, BS), A("nm", 0, BS), pmod, 64.0, OP.is_equal, OP.mult)
+    V("ts", A("dtm", 0, BS), A("nm", 15, BS + 15), pmod, -16.0, OP.is_equal, OP.mult)
+    V("tt", A("dsel", 0, BS), A("dsel", 0, BS), A("dtm", 0, BS), OP.add)
+    V("memset", A("bp", BS, T4 * BS), 0.0)
+    V("copy", I(A("bp", 0, P), A("sndw", 0, 24)), A("i384", 0, NB))
+    wrap(48, "bp", BS, "psc")
+    V("ts", A("bposw", 0, 48), A("psc", 0, 48), 1.0 / 16, float(HOLE), OP.mult, OP.add)
+    zero("bp", 0, BS)
+    zero("bp", T4 * BS, P)
+    border("y0", "ya", Y0)
+
+    wrap(16, "sdrow", 0, "psm")
+    V("ts", A("fw", 0, 16), A("psm", 0, 16), 0.5, None, OP.is_ge)
+    WH = PAR["whole"]
+    last = [("b", awin, 0), ("o", xwin, BS)] if PAR["first3"] == "b" else [("o", xwin, BS), ("b", awin, 0)]
+    for s in range(3):
+        if s in WH:
+            places(s)
+            whole(s, xwin, BS * (s % 2), False)
+        pack(s, BS * (s % 2) if s in WH else None)
+        if s == 2:
+            places(3)
+            for kind, win, c0 in last:
+                if kind == "b" or 3 in WH:
+                    whole(3, win, c0, kind == "b")
+        if s:
+            flags(s)
+        ranks()
+        slots(s)
+        if s in WH:
+            known(s)
+        else:
+            lists(s, False)
+            match(s, xwin, False)
+        tell(s)
+        merge(2 * BS * (s + 1), BS, PAR["mo"], "psm", A("own", 0, BS))
+        members(s)
+
+    fresh(BS, "hlf", A("xw", 3 * BS, 4 * BS), "ya", 0)
+    flags(3)
+    ranks()
+    V("ts", A("oa", 48, 64), A("psm", 0, 16), col(4), 1024.0, OP.is_ge, OP.mult)
+    V("tt", A("ob", 48, 64), A("oa", 48, 64), A("nb", 0, 16), OP.add)
+    V("ts", A("of2", 48, 64), A("ob", 48, 64), -float(Y0), None, OP.add)
+    settle(3, "ya", "yb")
+    pack(3, BS if 3 in WH else None)
+    slots(3)
+    members(3)
+    if 3 in WH:
+        known(3)
+    else:
+        lists(3, False)
+        aside(CAP, "lst", 3 * CAP, "ndk", "xq", 3 * CAP, xwin, "psf", 0)
+        targets(3, "psf", 0, CAP)
+    tell(3)
+    part("fv", "swv", OFF, 2 * P)
+    part("fs", "sws", OFF, 2 * P)
+    part("fm", "memr", 0, P)
+    V("copy", I(A("bp", 0, P), A("sndw", 0, 24)), A("land3", 0, NB))
+    part("fr", "bp", 0, P)
+    V("ts", A("oa", 0, 48), A("offs", 0, 48), CAP - 0.5, 2048.0, OP.is_ge, OP.mult)
+    V("copy", A("ob", 0, 48), A("offs", 0, 48))
+    V("tt", A("oa", 0, 48), A("oa", 0, 48), A("ob", 0, 48), OP.add)
+    V("tt", A("ob", 0, 48), A("oa", 0, 48), A("nb", 0, 48), OP.min)
+    V("copy", A("of2", 0, 48), A("ob", 0, 48))
+    for s, (win, name, other) in ((2, (bwin, "yb", "ya")), (1, (awin, "ya", "yb")), (0, (bwin, "yb", "ya"))):
+        if s in WH:
+            lists(s, True)
+        if s:
+            move(A(other, Y0 + (s + 1) * BS, Y0 + (s + 2) * BS), A(name, Y0 + (s + 1) * BS, Y0 + (s + 2) * BS))
+        match(s, win, True)
+        fresh(CAP, "ihk", A("xq", s * CAP, (s + 1) * CAP), name, 0)
+        settle(s, name, other)
+    terms = [("ihk", "fv", 0, 2), ("ihk", "fv", 1, 2), ("ihf", "fs", 0, 2), ("ihf", "fs", 1, 2), ("ihk", "fm", 0, 1), ("ihk", "fr", 0, 1)]
+    PE([mm(A("pd4", 0, LW), mat(m), A(name, c0, step * LW, step), k == 0, k == 5) for k, (m, name, c0, step) in enumerate(terms)])
+    V("ts", A("yf1", 0, LW), A("pd4", 0, LW), 10000.0, 1.0, OP.is_ge, OP.add)
+    V("tt", A("yfs", 0, LW), A("pd4", 0, LW), A("yf1", 0, LW), OP.min)
+    dma("oyf", ("yf", slice(None), 0, P), ("yfs", slice(None), 0, LW), [("yfs", 0, LW)], [], 40)
+    return tasks
+
+
+def landing(e, d):
+    b = (d - 1) * GB
+    if e[0] == "f":
+        return "land" + e[1], b + (16 if b >= HOLE and e != "f3" else 0)
+    if e == "x":
+        return "xw", P + b
+    return ("ya" if e in ("y0", "y2") else "yb"), Y0 + P + b
+
+
+def order(tasks):
+    seen, before = {}, []
+    for k, t in enumerate(tasks):
+        deps = set(t["after"])
+        for regs, w in ((t["rd"], False), (t["wr"], True)):
+            for name, c0, c1 in regs:
+                for a0, a1, aw, j in seen.get(name, []):
+                    if (name in PSB or (a0 < c1 and c0 < a1 and (w or aw))) and not (t["pool"] and mates(tasks[j], t)):
+                        deps.add(j)
+        for regs, w in ((t["rd"], False), (t["wr"], True)):
+            for name, c0, c1 in regs:
+                old = seen.get(name, [])
+                if name in PSB:
+                    old = []
+                elif w and not t["pool"]:
+                    old = [a for a in old if not (c0 <= a[0] and a[1] <= c1)]
+                seen[name] = old + [(c0, c1, w, k)]
+        deps.discard(k)
+        before.append(deps)
+    cost = [[[sum(lasts(c) for c in step) for step in way] for way in t["ways"]] for t in tasks]
+    hop = lambda a, b: 0.0 if a == b else PAR["hop"] + (PAR["pel"] if a == "t" else 0)
+    chain = [0.0] * len(tasks)
+    for k in range(len(tasks) - 1, -1, -1):
+        chain[k] += max(sum(cost[k][0]), tasks[k].get("rest", 0)) + tasks[k]["lag"]
+        for j in before[k]:
+            chain[j] = max(chain[j], chain[k] + hop(tasks[j]["ways"][0][-1][0][0], tasks[k]["ways"][0][0][0][0]))
+    behind = [[] for t in tasks]
+    for k in range(len(tasks)):
+        for j in before[k]:
+            behind[j].append(k)
+
+    def sweep(rank, back):
+        busy, done, placed = {q: [] for q in "vstgy"}, {}, []
+
+        def room(q, t, d):
+            for a, b in busy[q]:
+                if t + d <= a + 1e-9:
+                    break
+                t = max(t, b)
+            return t
+
+        for k in sorted(range(len(tasks)), key=lambda k: (-rank[k], -k if back else k)):
+            best, lag = None, tasks[k]["lag"]
+            for w, way in enumerate(tasks[k]["ways"]):
+                steps = list(zip(way, cost[k][w]))[::-1 if back else 1]
+                q, at = steps[0][0][0][0], []
+                if back:
+                    t = max([done[j][0] + hop("-" if lag else q, done[j][1]) for j in behind[k]] + [0.0]) + lag
+                else:
+                    t = max([done[j][0] + hop(done[j][1], q) for j in before[k]] + [0.0])
+                for step, d in steps:
+                    t = room(step[0][0], t + (hop(q, step[0][0]) if at else 0), d)
+                    at.append(t); t += d; q = step[0][0]
+                score = t + (PAR["absd"] if len(way) > 1 else 0) + PAR["lam"] * sum(d for step, d in steps if step[0][0] == "v")
+                if best is None or score < best[0] - 1e-9:
+                    best = (score, steps, at, t, q)
+            score, steps, at, t, q = best
+            done[k] = (t, q) if back else (t + lag, "-" if lag else q)
+            for (step, d), a in zip(steps, at):
+                busy[step[0][0]] = sorted(busy[step[0][0]] + [(a, a + d)])
+                placed.append([a, k, step])
+        return [done[k][0] for k in range(len(tasks))], placed
+
+    best = None
+    for turn in range(PAR["turns"]):
+        ends, placed = sweep(chain, False)
+        if best is None or max(ends) < best[0]:
+            best = (max(ends), placed)
+        chain = sweep(ends, True)[0]
+    span, placed = best
+    placed.sort(key=lambda p: (p[0], p[1]))
+    pools = {}
+    for p in placed:
+        if tasks[p[1]]["pool"]:
+            pools.setdefault(tasks[p[1]]["pool"], []).append(p)
+    for (make, m0, most), ps in pools.items():
+        a = m0
+        for q in "vs":
+            mine = [p for p in placed if p[2] and p[2][0][0] == q]
+            run = None
+            for p in [p for p in ps if p[2] and p[2][0][0] == q]:
+                n = elems(p[2][0][2]) // 16
+                if run and mine[mine.index(p) - 1] is run[1] and a + n - run[2] <= most:
+                    run[0][2] = [make(q, run[2], a + n)]
+                    run[1] = p
+                    run[3].append(p)
+                else:
+                    for x in (run[3] if run else []):
+                        x[2] = []
+                    p[2] = [make(q, a, a + n)]
+                    run = [p, p, a, []]
+                a += n
+            for x in (run[3] if run else []):
+                x[2] = []
+    return [c for p in placed for c in p[2]], span
+
+
+def mates(a, b):
+    return a["pool"] and (a["pool"] == b["pool"] or any(r[0] == "swv" for r in a["wr"]) and any(r[0] == "swv" for r in b["wr"]))
+
+
+CALLS = []
+
+
 def rank_program(g, core, T, topo):
     rank = T.rank_of(core)
     if rank is None:
         return
+    if not CALLS:
+        CALLS.extend(order(plan())[0])
     cores = T.cores
     qh = {"v": g.vector, "s": g.scalar, "t": g.tensor, "g": g, "y": g.sync}
     qsem = {"v": "sv", "s": "ss", "t": "st", "g": "sg"}
+    fns = {"copy": g.vector.tensor_copy, "tt": g.vector.tensor_tensor, "ts": g.vector.tensor_scalar, "scan": g.vector.tensor_tensor_scan,
+           "memset": g.vector.memset, "rec": g.vector.reciprocal, "act": g.scalar.activation, "mm": g.tensor.matmul,
+           "iota": g.iota, "asel": g.affine_select}
     cnt = {}
     know = {q: {} for q in qh}
     clocks = {}
     acc = {}
-    seq = [0]
 
     def conflicts(q, regs, write):
         out = []
         for name, c0, c1 in regs:
-            bank = name in PSB
             for a0, a1, w, aq, tok in acc.get(name, []):
-                if bank:
+                if name in PSB:
                     if aq != q or (q != "t" and (w or write)):
                         out.append(tok)
                 elif a0 < c1 and c0 < a1 and (w or write):
@@ -97,7 +602,6 @@ def rank_program(g, core, T, topo):
             qh[q].wait_ge(T.sem[s], v)
             for k, x in clocks[(s, v)][0].items():
                 know[q][k] = max(know[q].get(k, 0), x)
-            know[q][s] = max(know[q].get(s, 0), v)
 
     def note(q, reads, writes, tok):
         for regs, w in ((reads, False), (writes, True)):
@@ -113,485 +617,51 @@ def rank_program(g, core, T, topo):
 
     def token(q, sem, n):
         cnt[sem] = cnt.get(sem, 0) + n
-        seq[0] += 1
         c = dict(know[q]) if q is not None else {}
         c[sem] = cnt[sem]
-        clocks[(sem, cnt[sem])] = (c, seq[0])
+        clocks[(sem, cnt[sem])] = (c, len(clocks))
         return (sem, cnt[sem])
 
-    def A(name, c0, c1, step=1):
-        return ("op", T[name][:, c0:c1:step] if step != 1 else T[name][:, c0:c1], [(name, c0, c1)], [])
+    def ap(x):
+        if not isinstance(x, tuple):
+            return x
+        a = T[x[0]][:, x[1]:x[2]:x[3]] if x[3] != 1 else T[x[0]][:, x[1]:x[2]]
+        return a.indirect(ap(x[4])) if x[4] else a
 
-    def I(win, off):
-        return ("op", win[1].indirect(off[1]), win[2], off[2])
-
-    def do(q, fn, out, *ins, **kw):
-        reads, writes, args = list(out[3]), list(out[2]), [out[1]]
-        for x in ins:
-            if isinstance(x, tuple):
-                reads += x[2] + x[3]; args.append(x[1])
-            else:
-                args.append(x)
-        wait_for(q, conflicts(q, reads, False) + conflicts(q, writes, True))
-        f = {"copy": lambda: g.vector.tensor_copy, "tt": lambda: g.vector.tensor_tensor, "ts": lambda: g.vector.tensor_scalar,
-             "scan": lambda: g.vector.tensor_tensor_scan, "memset": lambda: g.vector.memset, "act": lambda: g.scalar.activation,
-             "rec": lambda: g.vector.reciprocal,
-             "mm": lambda: g.tensor.matmul, "iota": lambda: g.iota, "asel": lambda: g.affine_select}[fn]()
-        r = f(*args, **kw)
-        tok = token(q, qsem[q], 1)
-        r.then_inc(T.sem[qsem[q]], 1)
-        note(q, reads, writes, tok)
-
-    def dma(q, sem, out_ap, in_ap, reads, writes):
-        wait_for(q, conflicts(q, reads, False) + conflicts(q, writes, True))
-        qh[q].dma_start(out_ap, in_ap).then_inc(T.sem[sem], 16)
-        note(q + "dma", reads, writes, token(q, sem, 16))
-
-    V = lambda fn, out, *a, **k: do("v", fn, out, *a, **k)
-    S = lambda out, in_, f, **k: do("s", "act", out, in_, f, **k)
-    M = lambda out, l, r, a, b: do("t", "mm", out, l, r, a, b)
-    G = lambda fn, out, *a, **k: do("g", fn, out, *a, **k)
-    iota = lambda out, pat, base, cm=0: G("iota", out, pat, base, cm, allow_small_or_imprecise_dtypes=True)
-    sel = lambda a: A("sel", a * 128, (a + 1) * 128)
-    mat = lambda n: A(n, 0, 128)
-    col = lambda j: A("col", j, j + 1)
-
-    def move(q, out, in_):
-        if q == "v":
-            V("copy", out, in_)
-        else:
-            S(out, in_, AF.Copy)
-
-    def landing(e, d):
-        b = (d - 1) * GB
-        if e[0] == "f":
-            return "land" + e[1], b + (16 if b >= HOLE and e != "f3" else 0)
-        if e == "x":
-            return "xw", P + b
-        return ("ya" if e in ("y0", "y2") else "yb"), Y0 + P + b
-
-    arrival = {}
-    for e in EX:
-        n = sum(len(lanes(c, cores, topo)[core]) for c in cores if c != core)
-        arrival[e] = token(None, "arr_" + e, n)
-
-    def expect(e):
-        note("net", [], [(landing(e, d)[0], landing(e, d)[1], landing(e, d)[1] + GB) for d in range(1, N)], arrival[e])
-
-    def send(e):
-        lan = lanes(core, cores, topo)
-        wait_for("g", conflicts("g", [("msg_" + e, 0, NB)], False))
-        tr = []
-        for d in range(1, N):
-            dst = cores[(rank + d) % N] if e[0] != "f" else cores[(rank - d) % N]
-            rid, pid = topo.addr(dst, core)
-            name, c0 = landing(e, d)
-            tr.append(RemoteDMATransfer(dst_ids=[DstId(rid=rid, pnc=pid)], dma_engine_mask=sum(1 << q for q in lan[dst]),
-                                        remote_sem=T.sem["arr_" + e], src=T["msg_" + e][:, (d - 1) * GB:d * GB], dst=T[name][:, c0:c0 + GB]))
-            cnt["snt"] = cnt.get("snt", 0) + len(lan[dst])
-        g.remote_dma_fused(tr, local_sem=T.sem.snt)
-
-    for e in EX[:-2]:
-        expect(e)
-
-    def border(e, src, c0, hv=NB // 2):
-        if hv:
-            move("v", A("msg_" + e, 0, hv), I(A(src, c0, c0 + P), A("sndw", 0, hv // 16)))
-        move("s", A("msg_" + e, hv, NB), I(A(src, c0, c0 + P), A("sndw", hv // 16, NB // 16)))
-        send(e)
-
-    def wrap(c1, name, c0, ps):
-        for a in range(16):
-            M(A(ps, 0, c1), sel(a), A(name, c0 + a, c0 + 16 * (c1 - 1) + a + 1, 16), a == 0, a == 15)
-
-    def lot(lots, u):
-        return [l for l in lots if 16 * l[0] <= 512 * u < 16 * (l[0] + l[1])][0]
-
-    def pieces(lots, u):
-        m0, mc = lot(lots, u)
-        for i in range(16):
-            lo = 16 * m0 + i * mc
-            a, b = max(lo, 512 * u), min(lo + mc, 512 * u + 512)
-            if a < b:
-                yield i, m0 + a - lo, m0 + b - lo, A("pd%d" % (u % 5), a % 512, a % 512 + b - a), a % 512 == 0, b % 512 == 0
-
-    def gather(q, win, lst, c0, m0, m1):
-        if m1 > m0:
-            move(q, A("come", 16 * m0, 16 * m1), I(win, A(lst, c0 + m0, c0 + m1)))
-
-    def xpart(lots, m, name, c0, us):
-        for u in us:
-            for i, a, b, out, first, last in pieces(lots, u):
-                M(out, mat(m), A(name, c0 + a, c0 + b), first, False)
-
-    def cpart(lots, us):
-        for u in us:
-            for i, a, b, out, first, last in pieces(lots, u):
-                M(out, mat("dr"), A("come", 16 * a + i, 16 * (b - 1) + i + 1, 16), False, last)
-
-    def near(u, q="v"):
-        k = u % 5
-        out, ps, ab = A("ind", 512 * k, 512 * k + 512), A("pd%d" % k, 0, 512), A("ab", 512 * (u % 3), 512 * (u % 3) + 512)
-        if q == "v":
-            V("ts", out, ps, MAGIC, MAGIC, OP.add, OP.is_equal)
-        elif q == "s":
-            S(ab, ps, AF.Abs)
-        else:
-            V("ts", out, ab, 0.5, None, OP.is_lt)
-
-    def count(lots, u, ps):
-        m0, mc = lot(lots, u)
-        for i in range(16):
-            a = 16 * m0 + i * mc
-            if (a + mc - 1) // 512 == u:
-                M(A(ps, m0, m0 + mc), sel(i), A("ind", a % RING, a % RING + mc), i == 0, i == 15)
-
-    def low(m0, m1):
-        V("scan", A("mn", 16 * m0, 16 * m1), A("d0", 0, 16 * (m1 - m0)), A("come", 16 * m0, 16 * m1), 0.0, OP.max, OP.min)
-
-    def halves(n, m, x, ps):
-        M(A(ps, 0, n), mat(m), x, True, False)
-        M(A(ps, 0, n), mat("hlf"), A("mn", 15, 16 * n, 16), False, True)
-        V("ts", A("hv", 0, n), A(ps, 0, n), -0.25, None, OP.add)
-
-    def fresh(n, win):
-        V("ts", A("mt", 0, n), A("psc", 0, n), 7.5, -0.125, OP.is_ge, OP.add)
-        M(A("psm", 0, n), mat("bdk"), A("mt", 0, n), True, True)
-        V("tt", A(win, 0, n), A("psm", 0, n), A("hv", 0, n), OP.max)
-
-    def pack(s, far):
-        b = s * BS
-        M(A("psf", 0, BS), mat("ik"), A("xw", b, b + BS), True, not far)
-        if far:
-            V("ts", A("t1", 0, BS), A("psc", 0, BS), 7.5, float(FAR), OP.is_lt, OP.mult)
-            M(A("psf", 0, BS), mat("idn"), A("t1", 0, BS), False, True)
-        V("tt", A("pk", 0, BS), A("psf", 0, BS), A("cdw", b, b + BS), OP.add)
-
-    def flags(s):
-        V("tt", A("fb", 0, BS), I(A("land%d" % (s - 1), 0, NB + 16), A("bposw", 16 * (s - 1), 16 * s)), A("own", 0, BS), OP.add)
-        V("scan", A("fsc", 0, BS), A("dsel", 0, BS), A("fb", 0, BS), 0.0, OP.add, OP.min)
-        V("ts", A("fw", 0, 16), A("fsc", 15, BS, 16), col(3), -15.7, OP.subtract, OP.is_gt)
-
-    def ranks():
-        f = A("fw", 0, 16)
-        M(A("psm", 0, 16), mat("idn"), A("c32", 0, 16), True, False)
-        M(A("psm", 0, 16), mat("tri"), f, False, False)
-        M(A("psm", 0, 16), mat("dg"), f, False, False)
-        V("scan", A("cs", 1, 17), A("c32", 16, 32), f, 0.0, OP.max, OP.add)
-        M(A("psm", 0, 16), mat("bd"), A("cs", 0, 16), False, False)
-        V("tt", A("tp", 0, 16), f, A("c32", 16, 32), OP.mult)
-        M(A("psm", 0, 16), mat("idn"), A("tp", 0, 16), False, True)
-
-    def slots(s):
-        V("ts", A("offs", 16 * s, 16 * s + 16), A("psm", 0, 16), col(2), None, OP.add)
-        V("copy", I(A("pkc", s * SLOT, (s + 1) * SLOT), A("offs", 16 * s, 16 * s + 16)), A("pk", 0, BS))
-
-    def lists(s, far):
-        k, a, b = A("pkc", s * SLOT, s * SLOT + CAP), s * CAP, (s + 1) * CAP
-        if not far:
-            V("ts", A("lst", a, b), k, 0.5, -0.25, OP.mult, OP.add)
-        V("copy", A("i32", 0, CAP), k)
-        V("tt", A("xq", a, b), k, A("i32", 0, CAP), OP.subtract)
-        if far:
-            V("ts", A("shf", 0, CAP), A("i32", 0, CAP), FAR - 1, 1, OP.bitwise_and, OP.logical_shift_right)
-            V("ts", A("lst", a, b), A("shf", 0, CAP), float(W - 1), None, OP.min)
-
-    def targets(s, m0, mc, ps):
-        p = A(ps, m0, m0 + mc)
-        V("ts", p, p, 7.5, float(FARC), OP.is_lt, OP.mult)
-        V("tt", A("so", m0, m0 + mc), p, A("pkc", s * SLOT + m0, s * SLOT + m0 + mc), OP.add)
-        V("ts", A("sof", m0, m0 + mc), A("so", m0, m0 + mc), float(OFF), None, OP.add)
-
-    def scatter(q, m0, m1):
-        for a in range(m0, m1, SIN // 16):
-            b = min(m1, a + SIN // 16)
-            if q == "v":
-                V("copy", I(A("swv", 0, SWN), A("sof", a, b)), A("sin", 0, 16 * (b - a)))
-            else:
-                S(I(A("sws", 0, SWN), A("sof", a, b)), A("sin", 0, 16 * (b - a)), AF.Silu)
-
-    def merge(c0, n, tmp, ps):
-        S(A(tmp, 0, 2 * n), A("sws", OFF + c0, OFF + c0 + 2 * n), AF.Copy)
-        p = A(ps, 0, n)
-        M(p, mat("idn"), A(tmp, 0, 2 * n, 2), True, False)
-        M(p, mat("idn"), A(tmp, 1, 2 * n, 2), False, False)
-        M(p, mat("idn"), A("swv", OFF + c0, OFF + c0 + 2 * n, 2), False, False)
-        M(p, mat("idn"), A("swv", OFF + c0 + 1, OFF + c0 + 2 * n, 2), False, True)
-
-    def tell(s, q):
-        move(q, A("msg_f%d" % s, 0, NB), A("psf", 0, NB))
-        send("f%d" % s)
-
-    def members(s):
-        S(A("memr", s * BS, (s + 1) * BS), I(A("memi", 0, SLOT), A("offs", 16 * s, 16 * s + 16)), AF.Relu, scale=64.0)
-
-    def places(s):
-        V("ts", A("lsf", (s - 1) * BS, s * BS), A("cdw", s * BS, (s + 1) * BS), 0.5, -0.25, OP.mult, OP.add)
-
-    xwin, awin, bwin = A("xw", 0, W), A("ya", Y0, Y0 + W), A("yb", Y0, Y0 + W)
-
-    H = ST // 2
-    V("memset", A("sdrow", 0, BS), 0.0)
-    dma("s", "dsnd", T.snd32[:, :], T.snd[:, :], [], [("snd32", 0, 24)])
-    dma("y", "dx", T.xw[:, 0:P], T.x[:, :], [], [("xw", 0, P)])
-    dma("y", "dtl", T.tlc[:, :], T.tl[:, :], [], [("tlc", 0, 1)])
-    dma("y", "dsd", T.sdrow[0:128:16, :], T.sd[:, :], [], [("sdrow", 0, BS)])
-    dma("y", "dcd0", T.cdw[:, 0:BS], T.cd[:, 0:BS], [], [("cdw", 0, BS)])
-    G("iota", A("pmi", 0, 1), [[0, 1]], 0, 1)
-    iota(mat("qp"), [[0, 8], [1, 16]], 0)
-    G("asel", mat("qp"), mat("qp"), [[-16, 8], [0, 16]], OP.is_ge, -1.0, 0, 1)
-    G("asel", mat("qp"), mat("qp"), [[16, 8], [0, 16]], OP.is_ge, -1.0, 15, -1)
-    iota(A("c32", 0, 16), [[32, 16]], 0)
-    iota(A("c32", 16, 32), [[-32, 16]], 0)
-    empty = lambda s: iota(A("pkc", s * SLOT, s * SLOT + CAP), [[-16, CAP]], -1, -1)
-    empty(0)
-    iota(A("i384", 0, HOLE), [[1, HOLE]], -HOLE)
-    iota(A("i384", HOLE, NB), [[1, NB - HOLE]], 16)
-    V("memset", A("swv", OFF + H, OFF + H + 1024), 0.0)
-    zs = [(OFF + a, min(1024, ST - a)) for a in range(0, ST, 1024)]
-    for k, (a, n) in enumerate(zs[:2]):
-        S(A("sws", a, a + n), A("swv", OFF + H, OFF + H + n), AF.Copy if k else AF.Silu)
-    V("memset", A("swv", OFF + H + 1024, OFF + ST), 0.0)
-    V("ts", A("pm2", 0, 1), A("pmi", 0, 1), 15, None, OP.bitwise_and)
-    V("copy", col(0), A("pm2", 0, 1))
-    pmod = col(0)
-    for a in range(16):
-        V("ts", sel(a), mat("qp"), float(a), None, OP.is_equal)
-    wrap(16, "sdrow", 0, "psm")
-    V("ts", mat("idn"), mat("qp"), pmod, None, OP.is_equal)
-    V("ts", mat("bd"), mat("qp"), 0.0, None, OP.is_ge)
-    V("ts", mat("tri"), mat("qp"), pmod, None, OP.is_gt)
-    V("ts", col(2), pmod, 2.0, 256.0, OP.mult, OP.add)
-    V("ts", mat("dg"), mat("idn"), col(2), -1.0, OP.mult, OP.mult)
-    V("ts", mat("ik"), mat("idn"), 1.0 / XF, None, OP.mult)
-    V("memset", A("cs", 0, 1), 0.0)
-    V("memset", A("bp", BS, T4 * BS), 0.0)
-    V("copy", A("sndw", 0, 24), A("snd32", 0, 24))
-    border("x", "xw", 0)
-    V("memset", A("swv", OFF, OFF + H), 0.0)
-    for a, n in zs[2:]:
-        S(A("sws", a, a + n), A("swv", OFF + H, OFF + H + n), AF.Copy)
-    iota(A("sin", 0, SIN), [[0, SIN]], 1)
-    iota(A("nm", 0, BS), [[0, 16], [1, 16]], 0)
-    empty(1)
-    iota(A("memi", 0, SLOT), [[-1, SLOT]], CAP)
-    for s in range(3):
-        iota(A("land%d" % s, HOLE, HOLE + 16), [[0, 16]], 0)
-    wait_for("y", [arrival["x"]])
-    dma("y", "dcd1", T.cdw[:, BS:T4 * BS], T.cd[:, BS:T4 * BS], [], [("cdw", BS, T4 * BS)])
-    dma("y", "dya", T.ya[:, Y0:Y0 + P], T.y0[:, :], [], [("ya", Y0, Y0 + P)])
-    dma("y", "dyb", T.yb[:, Y0:Y0 + P], T.y0[:, :], [], [("yb", Y0, Y0 + P)])
-
-    V("ts", col(5), A("tlc", 0, 1), 2.0, 1.0, OP.mult, OP.add)
-    V("rec", col(6), col(5))
-    V("ts", A("fw", 0, 16), A("psm", 0, 16), 0.5, None, OP.is_ge)
-    pack(0, False)
-    ranks()
-    V("ts", mat("ndk"), mat("idn"), col(6), -XF, OP.mult, OP.mult)
-    slots(0)
-    lists(0, False)
-    ahead = lambda s: xpart(LOTS, "ndk", "xq", s * CAP, range(5))
-    ahead(0)
-    V("ts", mat("dr"), mat("idn"), col(6), None, OP.mult)
-    V("ts", mat("ndr"), mat("idn"), col(6), -1.0, OP.mult, OP.mult)
-    V("copy", A("swv", OFF, OFF + 2 * BS, 2), A("sdrow", 0, BS))
-
-    def outward(s, g1, g2, early, by_s=()):
-        c = s * CAP
-        gather("v", xwin, "lst", c, 0, g1)
-        gather("s", xwin, "lst", c, g1, MA)
-        cpart(LOTS, [0, 1])
-        gather("v", xwin, "lst", c, MA, g2)
-        gather("s", xwin, "lst", c, g2, CAP)
-        for u in (0, 1):
-            near(u); count(LOTS, u, "psm")
-        cpart(LOTS, [2, 3, 4])
-        targets(s, 0, MA, "psm")
-        for u in by_s:
-            near(u, "s")
-        scatter("s", 0, early)
-        for u in (2, 3, 4):
-            near(u, "l" if u in by_s else "v"); count(LOTS, u, "psc")
-        targets(s, MA, CAP - MA, "psc")
-
-    VS = PAR.get("VS", [72, 84, 84, 64])
-    outward(0, PAR.get("g1", 32), PAR.get("g2", 80), MA)
-    scatter("v", MA, MA + VS[0])
-    scatter("s", MA + VS[0], CAP)
-
-    wins = [xwin, xwin, awin]
-    fetch = lambda q, s, k: gather(q, wins[s], "lsf", BS * s, 64 * k, 64 * k + 64)
-    load = lambda s, us: xpart(ALL, "ndr", "xw", BS * (s + 1), us)
-    places(1)
-    load(0, range(5))
-    by_s = PAR.get("by_s", [(), (), ()])
-    for s in range(3):
-        merge(2 * P, NB, "swb", "psf")
-        if s == 0:
-            if PAR.get("l0", "v") == "v":
-                fetch("v", 0, 0)
-                tell(0, "s")
-            else:
-                tell(0, "v")
-                fetch("s", 0, 0)
-            fetch("s", 0, 1)
-            V("copy", I(A("bp", 0, P), A("sndw", 0, 24)), A("i384", 0, NB))
-            cpart(ALL, range(4))
-            wrap(48, "bp", BS, "psf")
-            empty(2)
-            iota(A("nb", 0, 48), [[16, 48]], Y0)
-            iota(A("d0", 0, 16 * (CAP - MA)), [[0, CAP - MA], [-256, 16]], 191)
-        if s and PAR.get("tq", "v") == "s":
-            tell(s, "s")
-        fetch("s", s, 2)
-        for u in range(8):
-            if s == 2 and u % 2 == 0:
-                low(32 * u, 32 * u + 64)
-            if u in by_s[s]:
-                near(u, "s"); near(u, "l")
-            else:
-                near(u)
-            if u == PAR.get("tu", 0) and s and PAR.get("tq", "v") == "v":
-                tell(s, "v")
-            if u == 1:
-                fetch("s", s, 3)
-            count(ALL, u, "psc")
-            if u < 3:
-                load(s, [u + 5])
-            if 1 <= u < 5:
-                cpart(ALL, [u + 3])
-            if u == 3:
-                merge(2 * BS * (s + 1), BS, "swo", "psm")
-                move("s", A("own", 0, BS), A("psm", 0, BS))
-            if u == 3 and s == 0:
-                V("ts", A("bposw", 0, 48), A("psf", 0, 48), 1.0 / 16, float(HOLE), OP.mult, OP.add)
-                V("ts", A("pm2", 1, 2), A("pmi", 0, 1), 1.0, None, OP.add)
-                V("ts", A("pm2", 0, 1), A("pm2", 1, 2), 15, None, OP.bitwise_and)
-                V("copy", col(1), A("pm2", 0, 1))
-                V("ts", A("dsel", 0, BS), A("nm", 0, BS), pmod, 64.0, OP.is_equal, OP.mult)
-                V("ts", A("dtm", 0, BS), A("nm", 0, BS), col(1), -16.0, OP.is_equal, OP.mult)
-                V("tt", A("dsel", 0, BS), A("dsel", 0, BS), A("dtm", 0, BS), OP.add)
-                V("ts", col(3), pmod, 15.0, 16.0, OP.is_ge, OP.mult)
-            if u == 4 and s < 2:
-                places(s + 2)
-                if s == 0:
-                    border("y0", "ya", Y0, 0)
-                fetch("s", s + 1, 0)
-        if s == 1:
-            empty(3)
-            iota(A("bp", 0, BS), [[0, BS]], 0)
-            iota(A("bp", T4 * BS, P), [[0, P - T4 * BS]], 0)
-            iota(A("yb", 0, Y0), [[0, Y0]], 0)
-        if s == 2:
-            iota(A("memr", T4 * BS, P), [[0, P - T4 * BS]], 0)
-            break
-        pack(s + 1, True)
-        fetch("s", s + 1, 1)
-        flags(s + 1)
-        ranks()
-        slots(s + 1)
-        V("ts", A("sof", 0, CAP), A("pkc", (s + 1) * SLOT, (s + 1) * SLOT + CAP), float(OFF), None, OP.add)
-        load(s + 1, range(5))
-        cpart(ALL, range(4))
-        scatter("s", VS[s + 1], CAP)
-        scatter("v", 0, VS[s + 1])
-        if s == 0:
-            V("ts", mat("hlf"), mat("idn"), 0.5, None, OP.mult)
-            V("ts", mat("ihk"), mat("idn"), XF / 2, None, OP.mult)
-            V("ts", mat("ihf"), mat("idn"), XF / 2, None, OP.mult)
-            V("ts", mat("bdk"), mat("bd"), 255.0, None, OP.mult)
-            V("ts", A("nb", 0, 48), A("nb", 0, 48), pmod, None, OP.add)
-            V("ts", col(4), col(2), -1.0, CAP - 0.5, OP.mult, OP.add)
-
-    def settle(s, win, out):
-        a = Y0 + s * BS
-        V("ts", A(out, a, a + BS), I(A(win, 0, a + BS), A("of2", 16 * s, 16 * s + 16)), 255.0, None, OP.min)
-        if s:
-            border("y%d" % s, out, Y0)
-            wait_for("y", [arrival["y%d" % s]])
-        dma("y", "oy%d" % s, T.yv[:, s * BS:(s + 1) * BS], T[out][:, a:a + BS], [(out, a, a + BS)], [])
-
-    def inward(s, win, name):
-        c, g1, g2 = s * CAP, PAR.get("b1", 32), PAR.get("b2", 88)
-        gather("v", win, "lst", c, 0, g1)
-        gather("s", win, "lst", c, g1, MA)
-        cpart(LOTS, [0, 1])
-        gather("v", win, "lst", c, MA, g2)
-        gather("s", win, "lst", c, g2, CAP)
-        for u in (0, 1):
-            near(u); count(LOTS, u, "psc")
-        cpart(LOTS, [2, 3, 4])
-        low(0, MA)
-        by_s = PAR.get("b3", (2, 3, 4))
-        for u in by_s:
-            near(u, "s")
-        low(MA, CAP)
-        near(2, "l" if 2 in by_s else "v"); count(LOTS, 2, "psc")
-        halves(CAP, "ihk", A("xq", c, c + CAP), "psm")
-        for u in (3, 4):
-            near(u, "l" if u in by_s else "v"); count(LOTS, u, "psc")
-        fresh(CAP, name)
-
-    def part(name, src, c0, n):
-        dma("y", "d" + name, T[name][:, :], T[src][0:128:16, c0:c0 + n], [(src, c0, c0 + n)], [(name, 0, n // 16)])
-
-    for s in range(3):
-        members(s)
-    halves(BS, "hlf", A("xw", 3 * BS, 4 * BS), "psf")
-    fresh(BS, "ya")
-    pack(3, False)
-    flags(3)
-    ranks()
-    V("ts", A("oa", 0, 16), A("psm", 0, 16), col(4), 1024.0, OP.is_ge, OP.mult)
-    V("tt", A("ob", 0, 16), A("oa", 0, 16), A("nb", 0, 16), OP.add)
-    V("ts", A("of2", 48, 64), A("ob", 0, 16), -float(Y0), None, OP.add)
-    settle(3, "ya", "yb")
-    expect("y2")
-    slots(3)
-    lists(3, False)
-    ahead(3)
-    members(3)
-    lists(2, True)
-    outward(3, PAR.get("h1", 0), PAR.get("h2", MA), 0, PAR.get("h3", ()))
-    ahead(2)
-    V("ts", A("oa", 0, 48), A("offs", 0, 48), CAP - 0.5, 2048.0, OP.is_ge, OP.mult)
-    V("copy", A("ob", 0, 48), A("offs", 0, 48))
-    V("tt", A("oa", 0, 48), A("oa", 0, 48), A("ob", 0, 48), OP.add)
-    V("tt", A("ob", 0, 48), A("oa", 0, 48), A("nb", 0, 48), OP.min)
-    V("copy", A("of2", 0, 48), A("ob", 0, 48))
-    V("copy", A("ya", Y0 + 3 * BS, Y0 + 4 * BS), A("yb", Y0 + 3 * BS, Y0 + 4 * BS))
-    inward(2, bwin, "yb")
-    s3 = PAR.get("s3", 32)
-    scatter("s", VS[3], VS[3] + s3)
-    settle(2, "yb", "ya")
-    expect("y1")
-    lists(1, True)
-    ahead(1)
-    scatter("s", VS[3] + s3, CAP)
-    scatter("v", 0, VS[3])
-    V("copy", A("yb", Y0 + 2 * BS, Y0 + 3 * BS), A("ya", Y0 + 2 * BS, Y0 + 3 * BS))
-    part("fv", "swv", OFF, 2 * P)
-    part("fs", "sws", OFF, 2 * P)
-    part("fm", "memr", 0, P)
-    if PAR.get("t3", 0) == 0:
-        merge(2 * P, NB, "swb", "psf")
-        tell(3, "s")
-    inward(1, awin, "ya")
-    if PAR.get("t3", 0) == 1:
-        merge(2 * P, NB, "swb", "psf")
-        tell(3, "s")
-    settle(1, "ya", "yb")
-    ahead(0)
-    V("copy", I(A("bp", 0, P), A("sndw", 0, 24)), A("land3", 0, NB))
-    part("fr", "bp", 0, P)
-    inward(0, bwin, "yb")
-    settle(0, "yb", "ya")
-    terms = [("ihk", "fv", 0, 2), ("ihk", "fv", 1, 2), ("ihf", "fs", 0, 2), ("ihf", "fs", 1, 2), ("ihk", "fm", 0, 1), ("ihk", "fr", 0, 1)]
-    for k, (m, name, c0, step) in enumerate(terms):
-        M(A("psf", 0, LW), mat(m), A(name, c0, step * LW, step), k == 0, k == len(terms) - 1)
-    V("ts", A("yf1", 0, LW), A("psf", 0, LW), 10000.0, 1.0, OP.is_ge, OP.add)
-    V("tt", A("yfs", 0, LW), A("psf", 0, LW), A("yf1", 0, LW), OP.min)
-    dma("s", "oyf", T.yf[:, :], T.yfs[:, :], [("yfs", 0, LW)], [])
+    lan = lanes(core, cores, topo)
+    coming = sum(len(lanes(c, cores, topo)[core]) for c in cores if c != core)
+    arrived = {}
+    for call in CALLS:
+        q, fn, out, ins, kw = call
+        reads, writes = touched(call)
+        if fn == "send":
+            wait_for("g", conflicts("g", reads, False))
+            tr = []
+            for d in range(1, N):
+                dst = cores[(rank + d) % N] if out[0] != "f" else cores[(rank - d) % N]
+                rid, pid = topo.addr(dst, core)
+                name, c0 = landing(out, d)
+                tr.append(RemoteDMATransfer(dst_ids=[DstId(rid=rid, pnc=pid)], dma_engine_mask=sum(1 << e for e in lan[dst]),
+                                            remote_sem=T.sem["arr_" + out], src=T["msg_" + out][:, (d - 1) * GB:d * GB],
+                                            dst=T[name][:, c0:c0 + GB]))
+                cnt["snt"] = cnt.get("snt", 0) + len(lan[dst])
+            g.remote_dma_fused(tr, local_sem=T.sem.snt)
+            arrived[out] = token(None, "arr_" + out, coming)
+            note("net", [], writes, arrived[out])
+            continue
+        toks = conflicts(q, reads, False) + conflicts(q, writes, True)
+        if fn == "dma":
+            hold = {"dz": "x", "dcd1": "x", "dya": "x", "dyb": "x", "oy3": "y3", "oy2": "y2", "oy1": "y1"}.get(out)
+            wait_for(q, toks + ([arrived[hold]] if hold else []))
+            side = lambda x: T[x[0]][x[1], x[2]:x[3]]
+            qh[q].dma_start(side(ins[0]), side(ins[1])).then_inc(T.sem[out], 16)
+            note(q + "dma", reads, writes, token(q, out, 16))
+            continue
+        wait_for(q, toks)
+        if fn == "iota" and SCRATCH[out[0]][2] != I32:
+            kw = dict(allow_small_or_imprecise_dtypes=True)
+        fns[fn](ap(out), *[ap(x) for x in ins], **{k: ap(x) for k, x in kw.items()}).then_inc(T.sem[qsem[q]], 1)
+        note(q, reads, writes, token(q, qsem[q], 1))
     for sname in SEMAPHORES:
         if cnt.get(sname, 0) and know["g"].get(sname, 0) < cnt[sname]:
             g.wait_ge(T.sem[sname], cnt[sname])

@@ -17,8 +17,9 @@ Y0 = 256
 HOLE = 256
 LW = 148
 MAGIC = 12582912.0
-PAR = dict(whole=(1, 2), cb=3, gp=32, sp=16, absd=0.0, first3="b", mb="swb", mo=None, dz=1, lam=1.0, rest=0.5, turns=6,
-           cyc=0.92, pe=0.35, fix=0.06, gam=1.15, sig=3.1, hop=0.08, pel=0.18, net=3.9, dma=1.5)
+PAR = dict(whole=(1, 2, 3), cb=(5, 5, 3), turn=1, gp=32, sp=16, cut=(0, 3, 9), by=["vs"] * 4, mb="swb", mo=None, dz=0, zv=4,
+           lam=[(0.4, 0.3), (0.4, 0.3), (0.8, 0.2), (1, 0)], rest=0.5, turns=2, sx=0.0, margin=99, bw=[["vs"] * 5] * 3, lowa=0,
+           cyc=0.9, pe=0.44, fix=0.03, sfix=0.05, gam=1.25, sig=3.6, hop=0.06, pel=0.3, net=2.9, wire=1.0, y0=1.0, dma=1.5)
 
 B16, F32, I32, U16 = "bfloat16", "float32", "int32", "uint16"
 SCRATCH = {}
@@ -34,7 +35,7 @@ for _n, _c, _d in [
         ("bp", P, B16), ("bposw", 48, U16), ("fw", 16, B16), ("fb", BS, B16), ("fsc", BS, B16), ("cs", 32, B16), ("tp", 16, B16),
         ("offs", 64, U16), ("of2", 64, U16), ("oa", 64, F32), ("ob", 64, F32), ("lsf", 3 * BS, U16), ("lst", 4 * CAP, U16),
         ("i32", CAP, I32), ("shf", CAP, I32), ("xq", 4 * CAP, B16), ("t1", BS, B16), ("so", CAP, F32), ("sof", CAP, U16),
-        ("mt", BS, B16), ("hv", BS, I32), ("memi", SLOT, B16), ("memr", P, B16),
+        ("mt", BS, B16), ("hv", BS, I32), ("memi", SLOT, B16), ("memr", P, B16), ("yo", T4 * BS, B16),
         ("fv", 2 * LW, B16), ("fs", 2 * LW, F32), ("fr", LW, B16), ("fm", LW, B16), ("yf1", LW, F32), ("yfs", LW, B16)]:
     SCRATCH[_n] = ("sbuf", [128, _c], _d)
 EX = ["x", "y0", "f0", "f1", "f2", "f3", "y3", "y2", "y1"]
@@ -45,7 +46,7 @@ for _s in range(4):
 PSB = ["pd0", "pd1", "pd2", "pd3", "pd4", "psc", "psm", "psf"]
 for _b in PSB:
     SCRATCH[_b] = ("psum", [128, 512], F32)
-DMAS = ["dx", "dsnd", "dsd", "dtl", "dcd0", "dcd1", "dya", "dyb", "dz", "dfv", "dfs", "dfr", "dfm", "oy0", "oy1", "oy2", "oy3", "oyf"]
+DMAS = ["dx", "dsnd", "dsd", "dtl", "dcd0", "dcd1", "dya", "dyb", "dz0", "dz1", "dz2", "dc2", "dc1", "dfv", "dfs", "dfr", "dfm", "oy0", "oy1", "oy2", "oy3", "oyf"]
 SEMAPHORES = ["sv", "ss", "st", "sg", "snt"] + DMAS + ["arr_" + _e for _e in EX]
 
 
@@ -75,7 +76,7 @@ def elems(a):
 
 
 def touched(call):
-    if call[1] in ("dma", "send"):
+    if call[1] in ("dma", "send", "wire"):
         return call[4]["reads"], call[4]["writes"]
     out, ops = call[2], [x for x in list(call[3]) + list(call[4].values()) if isinstance(x, tuple)]
     return [x[:3] for x in ops] + [x[4][:3] for x in ops + [out] if x[4]], [out[:3]]
@@ -83,8 +84,8 @@ def touched(call):
 
 def lasts(call):
     q, fn, out, ins = call[:4]
-    if fn in ("dma", "send"):
-        return 0.05 if fn == "dma" else 0.5
+    if fn in ("dma", "send", "wire"):
+        return {"dma": 0.05, "send": 0.5, "wire": PAR["wire"]}[fn]
     n, ops = elems(out), [x for x in (out,) + tuple(ins) if isinstance(x, tuple)]
     if q == "t":
         return max(64, n) * PAR["pe"] * (4 if SCRATCH[ins[0][0]][2] == F32 else 1) / 1000
@@ -94,11 +95,11 @@ def lasts(call):
         return 0.06 + n * PAR["sig" if out[4] else "gam"] / 1000
     narrow = all(SCRATCH[x[0]][2] in (B16, U16) for x in ops if elems(x) > 1)
     per = 1 if q == "s" else (1 if any(x[0] in PSB for x in ops) else 2) if fn == "tt" else 0.5 if narrow else 1
-    return PAR["fix"] + max(64, n * per) * PAR["cyc"] / 1000 + (1.3 if fn == "act" and ins[1] == AF.Silu else 0)
+    return PAR["fix"] + (PAR["sfix"] if q == "s" else 0) + max(64, n * per) * PAR["cyc"] / 1000 + (1.3 if fn == "act" and ins[1] == AF.Silu else 0)
 
 
 def plan():
-    tasks = []
+    tasks, spare = [], [PAR["lam"][0]]
 
     def task(*ways, after=(), pool=None, lag=0.0):
         rd, wr = set(), set()
@@ -107,7 +108,7 @@ def plan():
                 for c in step:
                     r, w = touched(c)
                     rd.update(r); wr.update(w)
-        tasks.append(dict(ways=ways, rd=rd, wr=wr, after=after, pool=pool, lag=lag))
+        tasks.append(dict(ways=ways, rd=rd, wr=wr, after=after, pool=pool, lag=lag, spare=spare[0]))
         return len(tasks) - 1
 
     V = lambda fn, out, *a: task([[("v", fn, out, a, {})]])
@@ -141,7 +142,8 @@ def plan():
 
     def send(e):
         land = [(landing(e, d)[0], landing(e, d)[1], landing(e, d)[1] + GB) for d in range(1, N)]
-        sent[e] = task([[("g", "send", e, (), dict(reads=[("msg_" + e, 0, NB)], writes=land))]], lag=PAR["net"] + (1 if e == "x" else 0))
+        sent[e] = task([[("g", "send", e, (), dict(reads=[("msg_" + e, 0, NB)], writes=land))], [("n", "wire", e, (), dict(reads=[], writes=[]))]],
+                       lag=PAR["net"] - PAR["wire"] + {"x": 1, "y0": PAR["y0"]}.get(e, 0))
 
     def border(e, src, c0):
         pool(lambda q, a, b: mv(q, A("msg_" + e, 16 * a, 16 * b), I(A(src, c0, c0 + P), A("sndw", a, b))), 0, NB // 16, NB // 32, NB // 16)
@@ -150,9 +152,7 @@ def plan():
     def wrap(c1, name, c0, ps):
         PE([mm(A(ps, 0, c1), sel(a), A(name, c0 + a, c0 + 16 * (c1 - 1) + a + 1, 16), a == 0, a == 15) for a in range(16)])
 
-    CB = PAR["cb"]
-
-    def pieces(u):
+    def pieces(u, CB):
         m0, mc = LOTS[0] if 512 * u < 16 * MA else LOTS[1]
         for i in range(16):
             lo = 16 * m0 + i * mc
@@ -160,29 +160,30 @@ def plan():
             if a < b:
                 yield i, m0 + a - lo, m0 + b - lo, A("pd%d" % (u % CB), a % 512, a % 512 + b - a), a % 512 == 0, b % 512 == 0
 
-    def near(k, slot):
+    def near(k, slot, by="vs", after=()):
         out, ps, ab = A("ind", 512 * slot, 512 * slot + 512), A("pd%d" % k, 0, 512), A("ab", 512 * k, 512 * k + 512)
-        task([[("v", "ts", out, (ps, MAGIC, MAGIC, OP.add, OP.is_equal), {})]],
-             [[sc(ab, ps, AF.Abs)], [("v", "ts", out, (ab, 0.5, None, OP.is_lt), {})]])
+        ways = {"v": [[("v", "ts", out, (ps, MAGIC, MAGIC, OP.add, OP.is_equal), {})]],
+                "s": [[sc(ab, ps, AF.Abs)], [("v", "ts", out, (ab, 0.5, None, OP.is_lt), {})]]}
+        return task(*[ways[q] for q in by], after=after)
 
     def low(m0, m1, src, e0):
-        V("scan", A("mn", 16 * m0, 16 * m1), A("d0", 0, 16 * (m1 - m0)), A(src, e0, e0 + 16 * (m1 - m0)), 0.0, OP.max, OP.min)
+        return V("scan", A("mn", 16 * m0, 16 * m1), A("d0", 0, 16 * (m1 - m0)), A(src, e0, e0 + 16 * (m1 - m0)), 0.0, OP.max, OP.min)
 
     def match(s, win, back):
-        c = s * CAP
+        c, CB = s * CAP, PAR["cb"][s] if back else 5
         for m0, mc in LOTS:
             pool(lambda q, a, b: mv(q, A("come", 16 * a, 16 * b), I(win, A("lst", c + a, c + b))), m0, m0 + mc, PAR["gp"], 256)
         for u in range(5):
-            PE([mm(out, mat("ndk"), A("xq", c + a, c + b), first, False) for i, a, b, out, first, last in pieces(u)])
-            PE([mm(out, mat("dr"), A("come", 16 * a + i, 16 * (b - 1) + i + 1, 16), False, last) for i, a, b, out, first, last in pieces(u)])
-            near(u % CB, u)
+            PE([mm(out, mat("ndk"), A("xq", c + a, c + b), first, False) for i, a, b, out, first, last in pieces(u, CB)])
+            PE([mm(out, mat("dr"), A("come", 16 * a + i, 16 * (b - 1) + i + 1, 16), False, last) for i, a, b, out, first, last in pieces(u, CB)])
+            near(u % CB, u, PAR["bw"][s][u] if back else "vs", [first] if back and u > 1 and PAR["lowa"] else ())
             m0, mc = LOTS[0] if u < 2 else LOTS[1]
             ps = "psc" if back else "psm" if u < 2 else "psf"
             PE([mm(A(ps, m0, m0 + mc), sel(i), A("ind", 16 * m0 + i * mc, 16 * m0 + (i + 1) * mc), i == 0, i == 15)
                 for i in range(16) if (16 * m0 + (i + 1) * mc - 1) // 512 == u])
             if u in (1, 4):
                 if back:
-                    low(m0, m0 + mc, "come", 16 * m0)
+                    first = low(m0, m0 + mc, "come", 16 * m0)
                 else:
                     targets(s, ps, m0, mc)
 
@@ -195,16 +196,15 @@ def plan():
 
     ring = [0, 0]
 
-    def aside(n, lst, l0, m, xn, x0, win, ps, c0, then=None):
-        for m0 in range(0, n, 64):
+    def aside(n, lst, l0, m, xn, x0, win, ps, c0, then=None, first=0):
+        for m0 in range(first, n, 64):
             mc, e0 = min(64, n - m0), 1024 * (ring[1] % 8)
             ring[1] += 1
             x, per = A(xn, x0 + m0, x0 + m0 + mc), 512 // mc
             pool(lambda q, a, b, e0=e0, m0=m0: mv(q, A("cw", e0 + 16 * a, e0 + 16 * b), I(win, A(lst, l0 + m0 + a, l0 + m0 + b))),
                  0, mc, PAR["gp"], 256)
             for i0 in range(0, 16, per):
-                b = CB + ring[0] % (5 - CB)
-                slot = 5 + ring[0] % 2
+                b, slot = (3 + ring[0] % 2, 5 + ring[0] % 2) if ps == "psf" else (ring[0] % 5, ring[0] % 5)
                 ring[0] += 1
                 out = lambda j: A("pd%d" % b, mc * j, mc * j + mc)
                 PE([mm(out(j), mat(m), x, j == 0, False) for j in range(per)])
@@ -215,21 +215,24 @@ def plan():
             if then:
                 then(m0, mc, e0)
 
-    def whole(s, win, c0, back):
-        aside(BS, "lsf", (s - 1) * BS, "ndr", "xw", s * BS, win, "psc", c0, (lambda m0, mc, e0: low(m0, m0 + mc, "cw", e0)) if back else None)
+    def whole(s, win, c0, back, k):
+        if k == 0 and (s < 3 or back):
+            places(s)
+        aside(64 * k + 64, "lsf", (s - 1) * BS, "ndr", "xw", s * BS, win, "psc", c0,
+              (lambda m0, mc, e0: low(m0, m0 + mc, "cw", e0)) if back else None, 64 * k)
 
     def fresh(n, m, x, win, c0):
-        PE([mm(A("psm", 0, n), mat(m), x, True, False), mm(A("psm", 0, n), mat("hlf"), A("mn", 15, 16 * n, 16), False, True)])
-        V("ts", A("hv", 0, n), A("psm", 0, n), -0.25, None, OP.add)
+        PE([mm(A("pd2", 0, n), mat(m), x, True, False), mm(A("pd2", 0, n), mat("hlf"), A("mn", 15, 16 * n, 16), False, True)])
+        V("ts", A("hv", 0, n), A("pd2", 0, n), -0.25, None, OP.add)
         V("ts", A("mt", 0, n), A("psc", c0, c0 + n), 7.5, -0.125, OP.is_ge, OP.add)
         PE([mm(A("psm", 0, n), mat("bdk"), A("mt", 0, n), True, True)])
         V("tt", A(win, 0, n), A("psm", 0, n), A("hv", 0, n), OP.max)
 
-    def pack(s, c0=None):
+    def pack(s, c0=None, ps="psc"):
         b = s * BS
         calls = [mm(A("psf", 0, BS), mat("ik"), A("xw", b, b + BS), True, c0 is None)]
         if c0 is not None:
-            V("ts", A("t1", 0, BS), A("psc", c0, c0 + BS), 7.5, float(FAR), OP.is_lt, OP.mult)
+            V("ts", A("t1", 0, BS), A(ps, c0, c0 + BS), 7.5, float(FAR), OP.is_lt, OP.mult)
             calls.append(mm(A("psf", 0, BS), mat("idn"), A("t1", 0, BS), False, True))
         PE(calls)
         V("tt", A("pk", 0, BS), A("psf", 0, BS), A("cdw", b, b + BS), OP.add)
@@ -271,17 +274,19 @@ def plan():
         V("ts", A("sof", 0, CAP), A("pkc", s * SLOT, s * SLOT + CAP), float(OFF), None, OP.add)
         scatter(0, CAP)
 
-    def merge(c0, n, tmp, ps, out):
+    def merge(c0, n, tmp, ps, out, by="vs"):
         p = A(ps, 0, n)
         if tmp:
-            move(A(tmp, 0, 2 * n), A("sws", OFF + c0, OFF + c0 + 2 * n))
+            a, b = A(tmp, 0, 2 * n), A("sws", OFF + c0, OFF + c0 + 2 * n)
+            ways = {"v": [[mv("v", a, b)]], "s": [[mv("s", a, b)]], "g": [[("g", "asel", a, (b, [[0, 2 * n]], OP.is_gt, 0.0, 1, 0), {})]]}
+            task(*[ways[q] for q in by])
         terms = [("idn", "swv", OFF + c0), ("idn", tmp, 0) if tmp else ("idf", "sws", OFF + c0)]
         for k, (m, name, a) in enumerate(terms):
             PE([mm(p, mat(m), A(name, a, a + 2 * n, 2), k == 0, False), mm(p, mat(m), A(name, a + 1, a + 2 * n, 2), False, k == 1)])
         move(out, p)
 
     def tell(s):
-        merge(2 * P, NB, PAR["mb"], "psf", A("msg_f%d" % s, 0, NB))
+        merge(2 * P, NB, PAR["mb"], "psf", A("msg_f%d" % s, 0, NB), PAR["by"][s])
         send("f%d" % s)
 
     def members(s):
@@ -292,10 +297,13 @@ def plan():
 
     def settle(s, win, out):
         a = Y0 + s * BS
-        V("ts", A(out, a, a + BS), I(A(win, 0, a + BS), A("of2", 16 * s, 16 * s + 16)), 255.0, None, OP.min)
         if s:
+            pool(lambda q, u, w: mv(q, A(out, a + 16 * u, a + 16 * w), I(A(win, 0, a + BS), A("of2", 16 * s + u, 16 * s + w))), 0, 16, 8, 16)
             border("y%d" % s, out, Y0)
-        dma("oy%d" % s, ("yv", slice(None), s * BS, (s + 1) * BS), (out, slice(None), a, a + BS), [(out, a, a + BS)], [], 64,
+            V("ts", A("yo", s * BS, (s + 1) * BS), A(out, a, a + BS), 255.0, None, OP.min)
+        else:
+            V("ts", A("yo", 0, BS), I(A(win, 0, a + BS), A("of2", 0, 16)), 255.0, None, OP.min)
+        dma("oy%d" % s, ("yv", slice(None), s * BS, (s + 1) * BS), ("yo", slice(None), s * BS, (s + 1) * BS), [("yo", s * BS, (s + 1) * BS)], [], 64,
             after=[sent["y%d" % s]] if s else [])
 
     def part(name, src, c0, n):
@@ -322,10 +330,9 @@ def plan():
     for s in range(4):
         iota(A("pkc", s * SLOT, s * SLOT + CAP), [[-16, CAP]], -1, -1)
     iota(A("i384", 0, HOLE), [[1, HOLE]], -HOLE)
-    iota(A("i384", HOLE, NB), [[1, NB - HOLE]], 16)
-    iota(A("nm", 0, BS + 16), [[0, 17], [1, 16]], 0)
+    early = [iota(A("i384", HOLE, NB), [[1, NB - HOLE]], 16), iota(A("nm", 0, BS + 16), [[0, 17], [1, 16]], 0)]
     for a in range(0, SIN, 512):
-        iota(A("sin", a, a + 512), [[0, 512]], 1)
+        tasks[iota(A("sin", a, a + 512), [[0, 512]], 1)]["after"] = early
         iota(A("d0", a, a + 512), [[0, 32], [-256, 16]], 191)
     for a in range(0, SLOT, 512):
         iota(A("memi", a, a + 512), [[-1, 512]], CAP - a)
@@ -334,11 +341,11 @@ def plan():
     iota(A("nb", 0, 48), [[16, 48]], Y0)
     zero("yb", 0, Y0)
     zero("memr", T4 * BS, P)
-    for a in range(OFF + H, OFF + ST, 688):
-        V("memset", A("swv", a, a + 688), 0.0)
-    for k, a in enumerate(range(OFF, OFF + ST, 688)):
-        S(A("sws", a, a + 688), A("swv", OFF + H, OFF + H + 688), AF.Copy if k else AF.Silu)
-    V("memset", A("swv", OFF, OFF + 2 * BS), 0.0)
+    Z = ST // 8
+    for k in range(PAR["zv"]):
+        V("memset", A("swv", OFF + k * Z, OFF + k * Z + Z), 0.0)
+    for k, a in enumerate(range(OFF, OFF + ST, Z)):
+        S(A("sws", a, a + Z), A("swv", OFF, OFF + Z), AF.Copy if k else AF.Silu)
     V("ts", A("pm2", 0, 1), A("pmi", 0, 1), 15, None, OP.bitwise_and)
     V("copy", pmod, A("pm2", 0, 1))
     V("ts", A("sel", 0, 144), qp, 15.0, None, OP.is_equal)
@@ -356,45 +363,37 @@ def plan():
     V("memset", A("cs", 0, 1), 0.0)
     V("copy", A("sndw", 0, 24), A("snd32", 0, 24))
     border("x", "xw", 0)
-    z = (OFF + 2 * BS, OFF + H, OFF + H, OFF + ST - 2 * BS)
-    if PAR["dz"]:
-        dma("dz", ("swv", slice(None), z[0], z[1]), ("swv", slice(None), z[2], z[3]), [("swv", z[2], z[3])], [("swv", z[0], z[1])], 600, [sent["x"]])
-    else:
-        for a in range(z[0], z[1], 560):
-            V("memset", A("swv", a, a + 560), 0.0)
+    for k, a in enumerate(range(PAR["zv"], 8, PAR["zv"])):
+        n = min(PAR["zv"], 8 - a) * Z
+        dma("dz%d" % k, ("swv", slice(None), OFF + a * Z, OFF + a * Z + n), ("swv", slice(None), OFF, OFF + n), [("swv", OFF, OFF + n)],
+            [("swv", OFF + a * Z, OFF + a * Z + n)], 400 * (k + 1), [sent["x"]] if k or not PAR["dz"] else [dx])
     load("dcd1", "cdw", BS, "cd", BS, T4 * BS, 1000, [sent["x"]])
     load("dya", "ya", Y0, "y0", 0, P, 1600, [sent["x"]])
-    load("dyb", "yb", Y0, "y0", 0, P, 2200, [sent["x"]])
     V("ts", col(5), A("tlc", 0, 1), 2.0, 1.0, OP.mult, OP.add)
     V("rec", col(6), col(5))
     for name, f in (("ndk", -XF), ("dr", 1.0), ("ndr", -1.0)):
         V("ts", mat(name), mat("idn"), col(6), f, OP.mult, OP.mult)
-    V("copy", A("swv", OFF, OFF + 2 * BS, 2), A("sdrow", 0, BS))
     V("ts", A("dsel", 0, BS), A("nm", 0, BS), pmod, 64.0, OP.is_equal, OP.mult)
     V("ts", A("dtm", 0, BS), A("nm", 15, BS + 15), pmod, -16.0, OP.is_equal, OP.mult)
     V("tt", A("dsel", 0, BS), A("dsel", 0, BS), A("dtm", 0, BS), OP.add)
     V("memset", A("bp", BS, T4 * BS), 0.0)
-    V("copy", I(A("bp", 0, P), A("sndw", 0, 24)), A("i384", 0, NB))
+    for a in range(0, 24, 8):
+        V("copy", I(A("bp", 0, P), A("sndw", a, a + 8)), A("i384", 16 * a, 16 * a + GB))
     wrap(48, "bp", BS, "psc")
     V("ts", A("bposw", 0, 48), A("psc", 0, 48), 1.0 / 16, float(HOLE), OP.mult, OP.add)
     zero("bp", 0, BS)
     zero("bp", T4 * BS, P)
-    border("y0", "ya", Y0)
 
     wrap(16, "sdrow", 0, "psm")
     V("ts", A("fw", 0, 16), A("psm", 0, 16), 0.5, None, OP.is_ge)
     WH = PAR["whole"]
-    last = [("b", awin, 0), ("o", xwin, BS)] if PAR["first3"] == "b" else [("o", xwin, BS), ("b", awin, 0)]
+    stream = [(s, xwin, BS * (s % 2), False, k) for s in WH if s < 3 for k in range(4)] + [(3, awin, BS, True, k) for k in range(4)]
     for s in range(3):
-        if s in WH:
-            places(s)
-            whole(s, xwin, BS * (s % 2), False)
+        while stream and stream[0][0] == s:
+            whole(*stream.pop(0))
         pack(s, BS * (s % 2) if s in WH else None)
-        if s == 2:
-            places(3)
-            for kind, win, c0 in last:
-                if kind == "b" or 3 in WH:
-                    whole(3, win, c0, kind == "b")
+        for k in range(min(len(stream), PAR["cut"][s])):
+            whole(*stream.pop(0))
         if s:
             flags(s)
         ranks()
@@ -407,15 +406,23 @@ def plan():
         tell(s)
         merge(2 * BS * (s + 1), BS, PAR["mo"], "psm", A("own", 0, BS))
         members(s)
+        if s == 0:
+            border("y0", "ya", Y0)
+            load("dyb", "yb", Y0, "y0", 0, P, 900, [sent["y0"]])
+    while stream:
+        whole(*stream.pop(0))
 
-    fresh(BS, "hlf", A("xw", 3 * BS, 4 * BS), "ya", 0)
+    fresh(BS, "hlf", A("xw", 3 * BS, 4 * BS), "ya", BS)
     flags(3)
     ranks()
     V("ts", A("oa", 48, 64), A("psm", 0, 16), col(4), 1024.0, OP.is_ge, OP.mult)
     V("tt", A("ob", 48, 64), A("oa", 48, 64), A("nb", 0, 16), OP.add)
     V("ts", A("of2", 48, 64), A("ob", 48, 64), -float(Y0), None, OP.add)
     settle(3, "ya", "yb")
-    pack(3, BS if 3 in WH else None)
+    spare[0] = PAR["lam"][1]
+    if 3 in WH:
+        aside(BS, "lsf", 2 * BS, "ndr", "xw", 3 * BS, xwin, "psf", BS)
+    pack(3, BS if 3 in WH else None, "psf")
     slots(3)
     members(3)
     if 3 in WH:
@@ -436,15 +443,18 @@ def plan():
     V("tt", A("ob", 0, 48), A("oa", 0, 48), A("nb", 0, 48), OP.min)
     V("copy", A("of2", 0, 48), A("ob", 0, 48))
     for s, (win, name, other) in ((2, (bwin, "yb", "ya")), (1, (awin, "ya", "yb")), (0, (bwin, "yb", "ya"))):
+        spare[0] = PAR["lam"][2 if s else 3]
         if s in WH:
             lists(s, True)
         if s:
-            move(A(other, Y0 + (s + 1) * BS, Y0 + (s + 2) * BS), A(name, Y0 + (s + 1) * BS, Y0 + (s + 2) * BS))
+            a, b = Y0 + (s + 1) * BS, Y0 + (s + 2) * BS
+            dma("dc%d" % s, (other, slice(None), a, b), (name, slice(None), a, b), [(name, a, b)], [(other, a, b)], 64, [sent["y%d" % (s + 1)]])
         match(s, win, True)
         fresh(CAP, "ihk", A("xq", s * CAP, (s + 1) * CAP), name, 0)
         settle(s, name, other)
     terms = [("ihk", "fv", 0, 2), ("ihk", "fv", 1, 2), ("ihf", "fs", 0, 2), ("ihf", "fs", 1, 2), ("ihk", "fm", 0, 1), ("ihk", "fr", 0, 1)]
-    PE([mm(A("pd4", 0, LW), mat(m), A(name, c0, step * LW, step), k == 0, k == 5) for k, (m, name, c0, step) in enumerate(terms)])
+    PE([mm(A("pd4", 0, LW), sel(0), A("sdrow", 0, LW), True, False), mm(A("pd4", 0, BS - LW), sel(1), A("sdrow", LW, BS), False, False)]
+       + [mm(A("pd4", 0, LW), mat(m), A(name, c0, step * LW, step), False, k == 5) for k, (m, name, c0, step) in enumerate(terms)])
     V("ts", A("yf1", 0, LW), A("pd4", 0, LW), 10000.0, 1.0, OP.is_ge, OP.add)
     V("tt", A("yfs", 0, LW), A("pd4", 0, LW), A("yf1", 0, LW), OP.min)
     dma("oyf", ("yf", slice(None), 0, P), ("yfs", slice(None), 0, LW), [("yfs", 0, LW)], [], 40)
@@ -491,8 +501,14 @@ def order(tasks):
         for j in before[k]:
             behind[j].append(k)
 
-    def sweep(rank, back):
-        busy, done, placed = {q: [] for q in "vstgy"}, {}, []
+    force = {}
+
+    def meets(j, w, k):
+        name = tasks[j]["ways"][w][0][0][2][0]
+        return name not in ("swv", "sws") or not tasks[j]["pool"] or any(r[0] in (name, "sof") for r in tasks[k]["rd"] | tasks[k]["wr"])
+
+    def sweep(rank, back, late):
+        busy, done, placed, start = {q: [] for q in "vstgyn"}, {}, [], {}
 
         def room(q, t, d):
             for a, b in busy[q]:
@@ -504,31 +520,45 @@ def order(tasks):
         for k in sorted(range(len(tasks)), key=lambda k: (-rank[k], -k if back else k)):
             best, lag = None, tasks[k]["lag"]
             for w, way in enumerate(tasks[k]["ways"]):
+                if force.get(k, w) != w:
+                    continue
                 steps = list(zip(way, cost[k][w]))[::-1 if back else 1]
                 q, at = steps[0][0][0][0], []
                 if back:
-                    t = max([done[j][0] + hop("-" if lag else q, done[j][1]) for j in behind[k]] + [0.0]) + lag
+                    t = max([done[j][0] + hop("-" if lag else q, done[j][1]) for j in behind[k] if meets(k, w, j)] + [0.0]) + lag
                 else:
-                    t = max([done[j][0] + hop(done[j][1], q) for j in before[k]] + [0.0])
+                    t = max([done[j][0] + hop(done[j][1], q) for j in before[k] if meets(j, done[j][2], k)] + [0.0])
                 for step, d in steps:
                     t = room(step[0][0], t + (hop(q, step[0][0]) if at else 0), d)
                     at.append(t); t += d; q = step[0][0]
-                score = t + (PAR["absd"] if len(way) > 1 else 0) + PAR["lam"] * sum(d for step, d in steps if step[0][0] == "v")
+                score = max(t, late[k] - PAR["margin"]) + (tasks[k]["spare"][1] if len(way) > 1 else 0) + tasks[k]["spare"][0] * sum(d for step, d in steps if step[0][0] == "v")
+                if steps[0][0][0][2][0] == "sws" and tasks[k]["pool"]:
+                    score += PAR["sx"]
                 if best is None or score < best[0] - 1e-9:
-                    best = (score, steps, at, t, q)
-            score, steps, at, t, q = best
-            done[k] = (t, q) if back else (t + lag, "-" if lag else q)
+                    best = (score, steps, at, t, q, w)
+            score, steps, at, t, q, w = best
+            done[k] = (t, q, w) if back else (t + lag, "-" if lag else q, w)
             for (step, d), a in zip(steps, at):
                 busy[step[0][0]] = sorted(busy[step[0][0]] + [(a, a + d)])
                 placed.append([a, k, step])
-        return [done[k][0] for k in range(len(tasks))], placed
+            start[k] = at[0]
+        span = max(d[0] for d in done.values())
+        return [done[k][0] for k in range(len(tasks))], placed, [span - start[k] for k in range(len(tasks))]
 
-    best = None
+    if PAR.get("lab"):
+        chain = PAR["lab"](tasks, sweep, chain, before, behind, force)
+    best, late = None, [0.0] * len(tasks)
     for turn in range(PAR["turns"]):
-        ends, placed = sweep(chain, False)
-        if best is None or max(ends) < best[0]:
+        ends, placed, early = sweep(chain, False, late)
+        if (best is None or max(ends) < best[0]) if PAR["turn"] is None else turn == PAR["turn"]:
             best = (max(ends), placed)
-        chain = sweep(ends, True)[0]
+        for k in range(len(tasks)):
+            ends[k] = max([ends[k]] + [ends[j] + 1e-6 for j in before[k]])
+        chain, _, late = sweep(ends, True, early)
+        if PAR.get("hook"):
+            chain = PAR["hook"](chain, before)
+        for k in range(len(tasks) - 1, -1, -1):
+            chain[k] = max([chain[k]] + [chain[j] + 1e-6 for j in behind[k]])
     span, placed = best
     placed.sort(key=lambda p: (p[0], p[1]))
     pools = {}
@@ -554,7 +584,7 @@ def order(tasks):
                 a += n
             for x in (run[3] if run else []):
                 x[2] = []
-    return [c for p in placed for c in p[2]], span
+    return [c for p in placed for c in p[2] if c[1] != "wire"], span
 
 
 def mates(a, b):
@@ -651,7 +681,7 @@ def rank_program(g, core, T, topo):
             continue
         toks = conflicts(q, reads, False) + conflicts(q, writes, True)
         if fn == "dma":
-            hold = {"dz": "x", "dcd1": "x", "dya": "x", "dyb": "x", "oy3": "y3", "oy2": "y2", "oy1": "y1"}.get(out)
+            hold = {"dz0": None if PAR["dz"] else "x", "dz1": "x", "dz2": "x", "dcd1": "x", "dya": "x", "dyb": "y0", "oy3": "y3", "oy2": "y2", "oy1": "y1", "dc2": "y3", "dc1": "y2"}.get(out)
             wait_for(q, toks + ([arrived[hold]] if hold else []))
             side = lambda x: T[x[0]][x[1], x[2]:x[3]]
             qh[q].dma_start(side(ins[0]), side(ins[1])).then_inc(T.sem[out], 16)

from concourse.bass import DstId, RemoteDMATransfer
from concourse.mybir import AluOpType as OP, ActivationFunctionType as AF

N, P, BS, T4, CAP, GB, S2 = 4, 2368, 256, 4, 160, 128, 2
NB = (N - 1) * GB
W = P + NB
ST = S2 * W
MA = 64
LOTS = [(0, MA), (MA, CAP - MA)]
OFF = 2816
FAR, FARC = 8192, 8320
SWN = OFF + FARC + ST
SIN = 1536
SLOT = 1024
XF = 1024.0
Y0 = 256
HOLE = 256
LW = 148
MAGIC = 12582912.0
PAR = dict(whole=(1, 2, 3), cb=(5, 5, 3), turn=1, gp=32, sp=16, cut=(0, 3, 9), by=["vs"] * 4, mb="swb", mo=None, dz=0, zv=4,
           lam=[(0.4, 0.3), (0.4, 0.3), (0.8, 0.2), (1, 0)], rest=0.5, turns=2, sx=0.0, margin=99, bw=[["vs"] * 5] * 3, lowa=0,
           cyc=0.9, pe=0.44, fix=0.03, sfix=0.05, gam=1.25, sig=3.6, hop=0.06, pel=0.3, net=2.9, wire=1.0, y0=1.0, dma=1.5)

B16, F32, I32, U16 = "bfloat16", "float32", "int32", "uint16"
SCRATCH = {}
for _n, _c, _d in [
        ("xw", W, B16), ("ya", Y0 + W, B16), ("yb", Y0 + W, B16), ("cdw", T4 * BS, I32), ("snd32", 24, I32), ("sndw", 24, U16),
        ("tlc", 1, B16), ("sdrow", BS, B16), ("swv", SWN, B16), ("sws", SWN, F32), ("swb", 2 * NB, B16),
        ("swo", 2 * BS, B16), ("own", BS, B16), ("sin", SIN, F32), ("come", 16 * CAP, B16), ("cw", 32 * BS, B16), ("ab", 2560, B16),
        ("ind", 7 * 512, B16), ("mn", 16 * BS, B16), ("d0", 16 * (CAP - MA), B16), ("pk", BS, F32), ("pkc", T4 * SLOT, F32),
        ("sel", 144, B16), ("qp", 144, B16), ("idf", 128, F32), ("bd", 128, B16), ("bdk", 128, B16), ("tri", 128, B16),
        ("dg", 128, B16), ("idn", 128, B16), ("dr", 128, B16), ("ndr", 128, B16), ("ndk", 128, B16), ("hlf", 128, B16),
        ("ihk", 128, B16), ("ihf", 128, F32), ("ik", 128, B16), ("pmi", 1, I32), ("pm2", 1, I32), ("col", 8, F32),
        ("nm", BS + 16, B16), ("dsel", BS, B16), ("dtm", BS, B16), ("c32", 32, B16), ("nb", 48, F32), ("i384", NB, B16),
        ("bp", P, B16), ("bposw", 48, U16), ("fw", 16, B16), ("fb", BS, B16), ("fsc", BS, B16), ("cs", 32, B16), ("tp", 16, B16),
        ("offs", 64, U16), ("of2", 64, U16), ("oa", 64, F32), ("ob", 64, F32), ("lsf", 3 * BS, U16), ("lst", 4 * CAP, U16),
        ("i32", CAP, I32), ("shf", CAP, I32), ("xq", 4 * CAP, B16), ("t1", BS, B16), ("so", CAP, F32), ("sof", CAP, U16),
        ("mt", BS, B16), ("hv", BS, I32), ("memi", SLOT, B16), ("memr", P, B16), ("yo", T4 * BS, B16),
        ("fv", 2 * LW, B16), ("fs", 2 * LW, F32), ("fr", LW, B16), ("fm", LW, B16), ("yf1", LW, F32), ("yfs", LW, B16)]:
    SCRATCH[_n] = ("sbuf", [128, _c], _d)
EX = ["x", "y0", "f0", "f1", "f2", "f3", "y3", "y2", "y1"]
for _e in EX:
    SCRATCH["msg_" + _e] = ("sbuf", [128, NB], B16)
for _s in range(4):
    SCRATCH["land%d" % _s] = ("sbuf", [128, NB + 16], B16)
PSB = ["pd0", "pd1", "pd2", "pd3", "pd4", "psc", "psm", "psf"]
for _b in PSB:
    SCRATCH[_b] = ("psum", [128, 512], F32)
DMAS = ["dx", "dsnd", "dsd", "dtl", "dcd0", "dcd1", "dya", "dyb", "dz0", "dz1", "dz2", "dc2", "dc1", "dfv", "dfs", "dfr", "dfm", "oy0", "oy1", "oy2", "oy3", "oyf"]
SEMAPHORES = ["sv", "ss", "st", "sg", "snt"] + DMAS + ["arr_" + _e for _e in EX]


def lanes(src, cores, topo):
    near = [c for c in cores if c != src and c in topo.cores_of(src)]
    far = [c for c in cores if c != src and c not in topo.cores_of(src)]
    res, used = {}, []
    for i, c in enumerate(far):
        e = topo.engines(src, c); k = len(e) // len(far)
        res[c] = e[i * k:(i + 1) * k]; used += e
    for c in near:
        e = [q for q in topo.engines(src, c) if q not in used]
        res[c] = e[:4]; used += res[c]
    return res


def A(name, c0, c1, step=1):
    return (name, c0, c1, step, None)


def I(win, off):
    return win[:4] + (off,)


def elems(a):
    return 16 * (a[4][2] - a[4][1]) if a[4] else len(range(a[1], a[2], a[3]))


def touched(call):
    if call[1] in ("dma", "send", "wire"):
        return call[4]["reads"], call[4]["writes"]
    out, ops = call[2], [x for x in list(call[3]) + list(call[4].values()) if isinstance(x, tuple)]
    return [x[:3] for x in ops] + [x[4][:3] for x in ops + [out] if x[4]], [out[:3]]


def lasts(call):
    q, fn, out, ins = call[:4]
    if fn in ("dma", "send", "wire"):
        return {"dma": 0.05, "send": 0.5, "wire": PAR["wire"]}[fn]
    n, ops = elems(out), [x for x in (out,) + tuple(ins) if isinstance(x, tuple)]
    if q == "t":
        return max(64, n) * PAR["pe"] * (4 if SCRATCH[ins[0][0]][2] == F32 else 1) / 1000
    if q == "g":
        return 0.15 + 2 * n * PAR["cyc"] / 1000
    if out[4] or (len(ops) > 1 and ops[1][4]):
        return 0.06 + n * PAR["sig" if out[4] else "gam"] / 1000
    narrow = all(SCRATCH[x[0]][2] in (B16, U16) for x in ops if elems(x) > 1)
    per = 1 if q == "s" else (1 if any(x[0] in PSB for x in ops) else 2) if fn == "tt" else 0.5 if narrow else 1
    return PAR["fix"] + (PAR["sfix"] if q == "s" else 0) + max(64, n * per) * PAR["cyc"] / 1000 + (1.3 if fn == "act" and ins[1] == AF.Silu else 0)


def plan():
    tasks, spare = [], [PAR["lam"][0]]

    def task(*ways, after=(), pool=None, lag=0.0):
        rd, wr = set(), set()
        for way in ways:
            for step in way:
                for c in step:
                    r, w = touched(c)
                    rd.update(r); wr.update(w)
        tasks.append(dict(ways=ways, rd=rd, wr=wr, after=after, pool=pool, lag=lag, spare=spare[0]))
        return len(tasks) - 1

    V = lambda fn, out, *a: task([[("v", fn, out, a, {})]])
    sc = lambda out, in_, f, **k: ("s", "act", out, (in_, f), k)
    S = lambda out, in_, f, **k: task([[sc(out, in_, f, **k)]])
    mm = lambda out, l, r, a, b: ("t", "mm", out, (l, r, a, b), {})
    PE = lambda calls: task([calls])
    iota = lambda out, pat, base, cm=0: task([[("g", "iota", out, (pat, base, cm), {})]])
    asel = lambda out, *a: task([[("g", "asel", out, (out,) + a, {})]])
    sel = lambda a: A("sel", 15 - a, 143 - a)
    mat = lambda n: A(n, 0, 128)
    col = lambda j: A("col", j, j + 1)
    mv = lambda q, out, in_: ("v", "copy", out, (in_,), {}) if q == "v" else sc(out, in_, AF.Copy)
    move = lambda out, in_: task([[mv("v", out, in_)]], [[mv("s", out, in_)]])

    def dma(sem, out, in_, reads, writes, kb, after=(), q="y"):
        return task([[(q, "dma", sem, (out, in_), dict(reads=reads, writes=writes))]], after=after, lag=PAR["dma"] + kb / 300)

    def zero(name, c0, c1):
        for a in range(c0, c1, 512):
            iota(A(name, a, min(c1, a + 512)), [[0, min(c1, a + 512) - a]], 0)

    def pool(make, m0, m1, size, most, end=None):
        key = (make, m0, most)
        for a in range(m0, m1, size):
            k = task([[make("v", m0, m1)]], [[make("s", m0, m1)]], pool=key)
            tasks[k]["ways"] = tuple([[make(q, a, min(m1, a + size))]] for q in "vs")
            tasks[k]["rest"] = PAR["rest"] * lasts(make("v", a, end or m1))

    sent = {}

    def send(e):
        land = [(landing(e, d)[0], landing(e, d)[1], landing(e, d)[1] + GB) for d in range(1, N)]
        sent[e] = task([[("g", "send", e, (), dict(reads=[("msg_" + e, 0, NB)], writes=land))], [("n", "wire", e, (), dict(reads=[], writes=[]))]],
                       lag=PAR["net"] - PAR["wire"] + {"x": 1, "y0": PAR["y0"]}.get(e, 0))

    def border(e, src, c0):
        pool(lambda q, a, b: mv(q, A("msg_" + e, 16 * a, 16 * b), I(A(src, c0, c0 + P), A("sndw", a, b))), 0, NB // 16, NB // 32, NB // 16)
        send(e)

    def wrap(c1, name, c0, ps):
        PE([mm(A(ps, 0, c1), sel(a), A(name, c0 + a, c0 + 16 * (c1 - 1) + a + 1, 16), a == 0, a == 15) for a in range(16)])

    def pieces(u, CB):
        m0, mc = LOTS[0] if 512 * u < 16 * MA else LOTS[1]
        for i in range(16):
            lo = 16 * m0 + i * mc
            a, b = max(lo, 512 * u), min(lo + mc, 512 * u + 512)
            if a < b:
                yield i, m0 + a - lo, m0 + b - lo, A("pd%d" % (u % CB), a % 512, a % 512 + b - a), a % 512 == 0, b % 512 == 0

    def near(k, slot, by="vs", after=()):
        out, ps, ab = A("ind", 512 * slot, 512 * slot + 512), A("pd%d" % k, 0, 512), A("ab", 512 * k, 512 * k + 512)
        ways = {"v": [[("v", "ts", out, (ps, MAGIC, MAGIC, OP.add, OP.is_equal), {})]],
                "s": [[sc(ab, ps, AF.Abs)], [("v", "ts", out, (ab, 0.5, None, OP.is_lt), {})]]}
        return task(*[ways[q] for q in by], after=after)

    def low(m0, m1, src, e0):
        return V("scan", A("mn", 16 * m0, 16 * m1), A("d0", 0, 16 * (m1 - m0)), A(src, e0, e0 + 16 * (m1 - m0)), 0.0, OP.max, OP.min)

    def match(s, win, back):
        c, CB = s * CAP, PAR["cb"][s] if back else 5
        for m0, mc in LOTS:
            pool(lambda q, a, b: mv(q, A("come", 16 * a, 16 * b), I(win, A("lst", c + a, c + b))), m0, m0 + mc, PAR["gp"], 256)
        for u in range(5):
            PE([mm(out, mat("ndk"), A("xq", c + a, c + b), first, False) for i, a, b, out, first, last in pieces(u, CB)])
            PE([mm(out, mat("dr"), A("come", 16 * a + i, 16 * (b - 1) + i + 1, 16), False, last) for i, a, b, out, first, last in pieces(u, CB)])
            near(u % CB, u, PAR["bw"][s][u] if back else "vs", [first] if back and u > 1 and PAR["lowa"] else ())
            m0, mc = LOTS[0] if u < 2 else LOTS[1]
            ps = "psc" if back else "psm" if u < 2 else "psf"
            PE([mm(A(ps, m0, m0 + mc), sel(i), A("ind", 16 * m0 + i * mc, 16 * m0 + (i + 1) * mc), i == 0, i == 15)
                for i in range(16) if (16 * m0 + (i + 1) * mc - 1) // 512 == u])
            if u in (1, 4):
                if back:
                    first = low(m0, m0 + mc, "come", 16 * m0)
                else:
                    targets(s, ps, m0, mc)

    def targets(s, ps, m0, mc):
        p = A(ps, m0, m0 + mc)
        V("ts", p, p, 7.5, float(FARC), OP.is_lt, OP.mult)
        V("tt", A("so", m0, m0 + mc), p, A("pkc", s * SLOT + m0, s * SLOT + m0 + mc), OP.add)
        V("ts", A("sof", m0, m0 + mc), A("so", m0, m0 + mc), float(OFF), None, OP.add)
        scatter(m0, m0 + mc)

    ring = [0, 0]

    def aside(n, lst, l0, m, xn, x0, win, ps, c0, then=None, first=0):
        for m0 in range(first, n, 64):
            mc, e0 = min(64, n - m0), 1024 * (ring[1] % 8)
            ring[1] += 1
            x, per = A(xn, x0 + m0, x0 + m0 + mc), 512 // mc
            pool(lambda q, a, b, e0=e0, m0=m0: mv(q, A("cw", e0 + 16 * a, e0 + 16 * b), I(win, A(lst, l0 + m0 + a, l0 + m0 + b))),
                 0, mc, PAR["gp"], 256)
            for i0 in range(0, 16, per):
                b, slot = (3 + ring[0] % 2, 5 + ring[0] % 2) if ps == "psf" else (ring[0] % 5, ring[0] % 5)
                ring[0] += 1
                out = lambda j: A("pd%d" % b, mc * j, mc * j + mc)
                PE([mm(out(j), mat(m), x, j == 0, False) for j in range(per)])
                PE([mm(out(j), mat("dr"), A("cw", e0 + i0 + j, e0 + i0 + j + 16 * (mc - 1) + 1, 16), False, j == per - 1) for j in range(per)])
                near(b, slot)
                PE([mm(A(ps, c0 + m0, c0 + m0 + mc), sel(i0 + j), A("ind", 512 * slot + mc * j, 512 * slot + mc * j + mc),
                       i0 + j == 0, i0 + j == 15) for j in range(per)])
            if then:
                then(m0, mc, e0)

    def whole(s, win, c0, back, k):
        if k == 0 and (s < 3 or back):
            places(s)
        aside(64 * k + 64, "lsf", (s - 1) * BS, "ndr", "xw", s * BS, win, "psc", c0,
              (lambda m0, mc, e0: low(m0, m0 + mc, "cw", e0)) if back else None, 64 * k)

    def fresh(n, m, x, win, c0):
        PE([mm(A("pd2", 0, n), mat(m), x, True, False), mm(A("pd2", 0, n), mat("hlf"), A("mn", 15, 16 * n, 16), False, True)])
        V("ts", A("hv", 0, n), A("pd2", 0, n), -0.25, None, OP.add)
        V("ts", A("mt", 0, n), A("psc", c0, c0 + n), 7.5, -0.125, OP.is_ge, OP.add)
        PE([mm(A("psm", 0, n), mat("bdk"), A("mt", 0, n), True, True)])
        V("tt", A(win, 0, n), A("psm", 0, n), A("hv", 0, n), OP.max)

    def pack(s, c0=None, ps="psc"):
        b = s * BS
        calls = [mm(A("psf", 0, BS), mat("ik"), A("xw", b, b + BS), True, c0 is None)]
        if c0 is not None:
            V("ts", A("t1", 0, BS), A(ps, c0, c0 + BS), 7.5, float(FAR), OP.is_lt, OP.mult)
            calls.append(mm(A("psf", 0, BS), mat("idn"), A("t1", 0, BS), False, True))
        PE(calls)
        V("tt", A("pk", 0, BS), A("psf", 0, BS), A("cdw", b, b + BS), OP.add)

    def flags(s):
        V("tt", A("fb", 0, BS), I(A("land%d" % (s - 1), 0, NB + 16), A("bposw", 16 * (s - 1), 16 * s)), A("own", 0, BS), OP.add)
        V("scan", A("fsc", 0, BS), A("dsel", 0, BS), A("fb", 0, BS), 0.0, OP.add, OP.min)
        V("ts", A("fw", 0, 16), A("fsc", 15, BS, 16), col(3), -15.7, OP.subtract, OP.is_gt)

    def ranks():
        f, p = A("fw", 0, 16), A("psm", 0, 16)
        V("scan", A("cs", 1, 17), A("c32", 16, 32), f, 0.0, OP.max, OP.add)
        V("tt", A("tp", 0, 16), f, A("c32", 16, 32), OP.mult)
        PE([mm(p, mat("idn"), A("c32", 0, 16), True, False), mm(p, mat("tri"), f, False, False), mm(p, mat("dg"), f, False, False)])
        PE([mm(p, mat("bd"), A("cs", 0, 16), False, False), mm(p, mat("idn"), A("tp", 0, 16), False, True)])

    def slots(s):
        V("ts", A("offs", 16 * s, 16 * s + 16), A("psm", 0, 16), col(2), None, OP.add)
        V("copy", I(A("pkc", s * SLOT, (s + 1) * SLOT), A("offs", 16 * s, 16 * s + 16)), A("pk", 0, BS))

    def lists(s, far):
        k, a, b = A("pkc", s * SLOT, s * SLOT + CAP), s * CAP, (s + 1) * CAP
        if not far:
            V("ts", A("lst", a, b), k, 0.5, -0.25, OP.mult, OP.add)
        V("copy", A("i32", 0, CAP), k)
        V("tt", A("xq", a, b), k, A("i32", 0, CAP), OP.subtract)
        if far:
            V("ts", A("shf", 0, CAP), A("i32", 0, CAP), FAR - 1, 1, OP.bitwise_and, OP.logical_shift_right)
            V("ts", A("lst", a, b), A("shf", 0, CAP), float(W - 1), None, OP.min)

    def scatter(m0, m1):
        def make(q, a, b):
            if q == "v":
                return mv("v", I(A("swv", 0, SWN), A("sof", a, b)), A("sin", 0, min(SIN, 16 * (b - a))))
            return sc(I(A("sws", 0, SWN), A("sof", a, b)), A("sin", 0, min(SIN, 16 * (b - a))), AF.Silu)
        pool(make, m0, m1, PAR["sp"], SIN // 16, CAP)

    def known(s):
        V("ts", A("sof", 0, CAP), A("pkc", s * SLOT, s * SLOT + CAP), float(OFF), None, OP.add)
        scatter(0, CAP)

    def merge(c0, n, tmp, ps, out, by="vs"):
        p = A(ps, 0, n)
        if tmp:
            a, b = A(tmp, 0, 2 * n), A("sws", OFF + c0, OFF + c0 + 2 * n)
            ways = {"v": [[mv("v", a, b)]], "s": [[mv("s", a, b)]], "g": [[("g", "asel", a, (b, [[0, 2 * n]], OP.is_gt, 0.0, 1, 0), {})]]}
            task(*[ways[q] for q in by])
        terms = [("idn", "swv", OFF + c0), ("idn", tmp, 0) if tmp else ("idf", "sws", OFF + c0)]
        for k, (m, name, a) in enumerate(terms):
            PE([mm(p, mat(m), A(name, a, a + 2 * n, 2), k == 0, False), mm(p, mat(m), A(name, a + 1, a + 2 * n, 2), False, k == 1)])
        move(out, p)

    def tell(s):
        merge(2 * P, NB, PAR["mb"], "psf", A("msg_f%d" % s, 0, NB), PAR["by"][s])
        send("f%d" % s)

    def members(s):
        S(A("memr", s * BS, (s + 1) * BS), I(A("memi", 0, SLOT), A("offs", 16 * s, 16 * s + 16)), AF.Relu, scale=64.0)

    def places(s):
        V("ts", A("lsf", (s - 1) * BS, s * BS), A("cdw", s * BS, (s + 1) * BS), 0.5, -0.25, OP.mult, OP.add)

    def settle(s, win, out):
        a = Y0 + s * BS
        if s:
            pool(lambda q, u, w: mv(q, A(out, a + 16 * u, a + 16 * w), I(A(win, 0, a + BS), A("of2", 16 * s + u, 16 * s + w))), 0, 16, 8, 16)
            border("y%d" % s, out, Y0)
            V("ts", A("yo", s * BS, (s + 1) * BS), A(out, a, a + BS), 255.0, None, OP.min)
        else:
            V("ts", A("yo", 0, BS), I(A(win, 0, a + BS), A("of2", 0, 16)), 255.0, None, OP.min)
        dma("oy%d" % s, ("yv", slice(None), s * BS, (s + 1) * BS), ("yo", slice(None), s * BS, (s + 1) * BS), [("yo", s * BS, (s + 1) * BS)], [], 64,
            after=[sent["y%d" % s]] if s else [])

    def part(name, src, c0, n):
        dma("d" + name, (name, slice(None), 0, n // 16), (src, slice(0, 128, 16), c0, c0 + n), [(src, c0, c0 + n)], [(name, 0, n // 16)], 100)

    def load(sem, name, c0, src, a, b, kb, after=(), q="y", rows=slice(None)):
        return dma(sem, (name, rows, c0, c0 + b - a), (src, slice(None), a, b), [], [(name, c0, c0 + b - a)], kb, after, q)

    xwin, awin, bwin = A("xw", 0, W), A("ya", Y0, Y0 + W), A("yb", Y0, Y0 + W)
    H, pmod, qp = ST // 2, col(0), A("qp", 0, 144)

    V("memset", A("sdrow", 0, BS), 0.0)
    load("dsnd", "snd32", 0, "snd", 0, 24, 20, q="s")
    dx = load("dx", "xw", 0, "x", 0, P, 600)
    load("dtl", "tlc", 0, "tl", 0, 1, 700)
    load("dsd", "sdrow", 0, "sd", 0, BS, 700, rows=slice(0, 128, 16))
    load("dcd0", "cdw", 0, "cd", 0, BS, 900)
    iota(A("pmi", 0, 1), [[0, 1]], 0, 1)
    iota(qp, [[0, 9], [1, 16]], 0)
    asel(qp, [[-16, 9], [0, 16]], OP.is_ge, -1.0, 0, 1)
    asel(qp, [[16, 9], [0, 16]], OP.is_ge, -1.0, 15, -1)
    iota(A("c32", 0, 16), [[32, 16]], 0)
    iota(A("c32", 16, 32), [[-32, 16]], 0)
    for s in range(4):
        iota(A("pkc", s * SLOT, s * SLOT + CAP), [[-16, CAP]], -1, -1)
    iota(A("i384", 0, HOLE), [[1, HOLE]], -HOLE)
    early = [iota(A("i384", HOLE, NB), [[1, NB - HOLE]], 16), iota(A("nm", 0, BS + 16), [[0, 17], [1, 16]], 0)]
    for a in range(0, SIN, 512):
        tasks[iota(A("sin", a, a + 512), [[0, 512]], 1)]["after"] = early
        iota(A("d0", a, a + 512), [[0, 32], [-256, 16]], 191)
    for a in range(0, SLOT, 512):
        iota(A("memi", a, a + 512), [[-1, 512]], CAP - a)
    for s in range(3):
        zero("land%d" % s, HOLE, HOLE + 16)
    iota(A("nb", 0, 48), [[16, 48]], Y0)
    zero("yb", 0, Y0)
    zero("memr", T4 * BS, P)
    Z = ST // 8
    for k in range(PAR["zv"]):
        V("memset", A("swv", OFF + k * Z, OFF + k * Z + Z), 0.0)
    for k, a in enumerate(range(OFF, OFF + ST, Z)):
        S(A("sws", a, a + Z), A("swv", OFF, OFF + Z), AF.Copy if k else AF.Silu)
    V("ts", A("pm2", 0, 1), A("pmi", 0, 1), 15, None, OP.bitwise_and)
    V("copy", pmod, A("pm2", 0, 1))
    V("ts", A("sel", 0, 144), qp, 15.0, None, OP.is_equal)
    V("ts", mat("idn"), mat("qp"), pmod, None, OP.is_equal)
    V("ts", mat("bd"), mat("qp"), 0.0, None, OP.is_ge)
    V("ts", mat("tri"), mat("qp"), pmod, None, OP.is_gt)
    V("ts", col(2), pmod, 2.0, 256.0, OP.mult, OP.add)
    V("ts", mat("dg"), mat("idn"), col(2), -1.0, OP.mult, OP.mult)
    for name, f in (("ik", 1.0 / XF), ("hlf", 0.5), ("ihk", XF / 2), ("ihf", XF / 2), ("idf", 1.0)):
        V("ts", mat(name), mat("idn"), f, None, OP.mult)
    V("ts", mat("bdk"), mat("bd"), 255.0, None, OP.mult)
    V("ts", col(4), col(2), -1.0, CAP - 0.5, OP.mult, OP.add)
    V("ts", col(3), pmod, 15.0, 16.0, OP.is_ge, OP.mult)
    V("ts", A("nb", 0, 48), A("nb", 0, 48), pmod, None, OP.add)
    V("memset", A("cs", 0, 1), 0.0)
    V("copy", A("sndw", 0, 24), A("snd32", 0, 24))
    border("x", "xw", 0)
    for k, a in enumerate(range(PAR["zv"], 8, PAR["zv"])):
        n = min(PAR["zv"], 8 - a) * Z
        dma("dz%d" % k, ("swv", slice(None), OFF + a * Z, OFF + a * Z + n), ("swv", slice(None), OFF, OFF + n), [("swv", OFF, OFF + n)],
            [("swv", OFF + a * Z, OFF + a * Z + n)], 400 * (k + 1), [sent["x"]] if k or not PAR["dz"] else [dx])
    load("dcd1", "cdw", BS, "cd", BS, T4 * BS, 1000, [sent["x"]])
    load("dya", "ya", Y0, "y0", 0, P, 1600, [sent["x"]])
    V("ts", col(5), A("tlc", 0, 1), 2.0, 1.0, OP.mult, OP.add)
    V("rec", col(6), col(5))
    for name, f in (("ndk", -XF), ("dr", 1.0), ("ndr", -1.0)):
        V("ts", mat(name), mat("idn"), col(6), f, OP.mult, OP.mult)
    V("ts", A("dsel", 0, BS), A("nm", 0, BS), pmod, 64.0, OP.is_equal, OP.mult)
    V("ts", A("dtm", 0, BS), A("nm", 15, BS + 15), pmod, -16.0, OP.is_equal, OP.mult)
    V("tt", A("dsel", 0, BS), A("dsel", 0, BS), A("dtm", 0, BS), OP.add)
    V("memset", A("bp", BS, T4 * BS), 0.0)
    for a in range(0, 24, 8):
        V("copy", I(A("bp", 0, P), A("sndw", a, a + 8)), A("i384", 16 * a, 16 * a + GB))
    wrap(48, "bp", BS, "psc")
    V("ts", A("bposw", 0, 48), A("psc", 0, 48), 1.0 / 16, float(HOLE), OP.mult, OP.add)
    zero("bp", 0, BS)
    zero("bp", T4 * BS, P)

    wrap(16, "sdrow", 0, "psm")
    V("ts", A("fw", 0, 16), A("psm", 0, 16), 0.5, None, OP.is_ge)
    WH = PAR["whole"]
    stream = [(s, xwin, BS * (s % 2), False, k) for s in WH if s < 3 for k in range(4)] + [(3, awin, BS, True, k) for k in range(4)]
    for s in range(3):
        while stream and stream[0][0] == s:
            whole(*stream.pop(0))
        pack(s, BS * (s % 2) if s in WH else None)
        for k in range(min(len(stream), PAR["cut"][s])):
            whole(*stream.pop(0))
        if s:
            flags(s)
        ranks()
        slots(s)
        if s in WH:
            known(s)
        else:
            lists(s, False)
            match(s, xwin, False)
        tell(s)
        merge(2 * BS * (s + 1), BS, PAR["mo"], "psm", A("own", 0, BS))
        members(s)
        if s == 0:
            border("y0", "ya", Y0)
            load("dyb", "yb", Y0, "y0", 0, P, 900, [sent["y0"]])
    while stream:
        whole(*stream.pop(0))

    fresh(BS, "hlf", A("xw", 3 * BS, 4 * BS), "ya", BS)
    flags(3)
    ranks()
    V("ts", A("oa", 48, 64), A("psm", 0, 16), col(4), 1024.0, OP.is_ge, OP.mult)
    V("tt", A("ob", 48, 64), A("oa", 48, 64), A("nb", 0, 16), OP.add)
    V("ts", A("of2", 48, 64), A("ob", 48, 64), -float(Y0), None, OP.add)
    settle(3, "ya", "yb")
    spare[0] = PAR["lam"][1]
    if 3 in WH:
        aside(BS, "lsf", 2 * BS, "ndr", "xw", 3 * BS, xwin, "psf", BS)
    pack(3, BS if 3 in WH else None, "psf")
    slots(3)
    members(3)
    if 3 in WH:
        known(3)
    else:
        lists(3, False)
        aside(CAP, "lst", 3 * CAP, "ndk", "xq", 3 * CAP, xwin, "psf", 0)
        targets(3, "psf", 0, CAP)
    tell(3)
    part("fv", "swv", OFF, 2 * P)
    part("fs", "sws", OFF, 2 * P)
    part("fm", "memr", 0, P)
    V("copy", I(A("bp", 0, P), A("sndw", 0, 24)), A("land3", 0, NB))
    part("fr", "bp", 0, P)
    V("ts", A("oa", 0, 48), A("offs", 0, 48), CAP - 0.5, 2048.0, OP.is_ge, OP.mult)
    V("copy", A("ob", 0, 48), A("offs", 0, 48))
    V("tt", A("oa", 0, 48), A("oa", 0, 48), A("ob", 0, 48), OP.add)
    V("tt", A("ob", 0, 48), A("oa", 0, 48), A("nb", 0, 48), OP.min)
    V("copy", A("of2", 0, 48), A("ob", 0, 48))
    for s, (win, name, other) in ((2, (bwin, "yb", "ya")), (1, (awin, "ya", "yb")), (0, (bwin, "yb", "ya"))):
        spare[0] = PAR["lam"][2 if s else 3]
        if s in WH:
            lists(s, True)
        if s:
            a, b = Y0 + (s + 1) * BS, Y0 + (s + 2) * BS
            dma("dc%d" % s, (other, slice(None), a, b), (name, slice(None), a, b), [(name, a, b)], [(other, a, b)], 64, [sent["y%d" % (s + 1)]])
        match(s, win, True)
        fresh(CAP, "ihk", A("xq", s * CAP, (s + 1) * CAP), name, 0)
        settle(s, name, other)
    terms = [("ihk", "fv", 0, 2), ("ihk", "fv", 1, 2), ("ihf", "fs", 0, 2), ("ihf", "fs", 1, 2), ("ihk", "fm", 0, 1), ("ihk", "fr", 0, 1)]
    PE([mm(A("pd4", 0, LW), sel(0), A("sdrow", 0, LW), True, False), mm(A("pd4", 0, BS - LW), sel(1), A("sdrow", LW, BS), False, False)]
       + [mm(A("pd4", 0, LW), mat(m), A(name, c0, step * LW, step), False, k == 5) for k, (m, name, c0, step) in enumerate(terms)])
    V("ts", A("yf1", 0, LW), A("pd4", 0, LW), 10000.0, 1.0, OP.is_ge, OP.add)
    V("tt", A("yfs", 0, LW), A("pd4", 0, LW), A("yf1", 0, LW), OP.min)
    dma("oyf", ("yf", slice(None), 0, P), ("yfs", slice(None), 0, LW), [("yfs", 0, LW)], [], 40)
    return tasks


def landing(e, d):
    b = (d - 1) * GB
    if e[0] == "f":
        return "land" + e[1], b + (16 if b >= HOLE and e != "f3" else 0)
    if e == "x":
        return "xw", P + b
    return ("ya" if e in ("y0", "y2") else "yb"), Y0 + P + b


def order(tasks):
    seen, before = {}, []
    for k, t in enumerate(tasks):
        deps = set(t["after"])
        for regs, w in ((t["rd"], False), (t["wr"], True)):
            for name, c0, c1 in regs:
                for a0, a1, aw, j in seen.get(name, []):
                    if (name in PSB or (a0 < c1 and c0 < a1 and (w or aw))) and not (t["pool"] and mates(tasks[j], t)):
                        deps.add(j)
        for regs, w in ((t["rd"], False), (t["wr"], True)):
            for name, c0, c1 in regs:
                old = seen.get(name, [])
                if name in PSB:
                    old = []
                elif w and not t["pool"]:
                    old = [a for a in old if not (c0 <= a[0] and a[1] <= c1)]
                seen[name] = old + [(c0, c1, w, k)]
        deps.discard(k)
        before.append(deps)
    cost = [[[sum(lasts(c) for c in step) for step in way] for way in t["ways"]] for t in tasks]
    hop = lambda a, b: 0.0 if a == b else PAR["hop"] + (PAR["pel"] if a == "t" else 0)
    chain = [0.0] * len(tasks)
    for k in range(len(tasks) - 1, -1, -1):
        chain[k] += max(sum(cost[k][0]), tasks[k].get("rest", 0)) + tasks[k]["lag"]
        for j in before[k]:
            chain[j] = max(chain[j], chain[k] + hop(tasks[j]["ways"][0][-1][0][0], tasks[k]["ways"][0][0][0][0]))
    behind = [[] for t in tasks]
    for k in range(len(tasks)):
        for j in before[k]:
            behind[j].append(k)

    force = {}

    def meets(j, w, k):
        name = tasks[j]["ways"][w][0][0][2][0]
        return name not in ("swv", "sws") or not tasks[j]["pool"] or any(r[0] in (name, "sof") for r in tasks[k]["rd"] | tasks[k]["wr"])

    def sweep(rank, back, late):
        busy, done, placed, start = {q: [] for q in "vstgyn"}, {}, [], {}

        def room(q, t, d):
            for a, b in busy[q]:
                if t + d <= a + 1e-9:
                    break
                t = max(t, b)
            return t

        for k in sorted(range(len(tasks)), key=lambda k: (-rank[k], -k if back else k)):
            best, lag = None, tasks[k]["lag"]
            for w, way in enumerate(tasks[k]["ways"]):
                if force.get(k, w) != w:
                    continue
                steps = list(zip(way, cost[k][w]))[::-1 if back else 1]
                q, at = steps[0][0][0][0], []
                if back:
                    t = max([done[j][0] + hop("-" if lag else q, done[j][1]) for j in behind[k] if meets(k, w, j)] + [0.0]) + lag
                else:
                    t = max([done[j][0] + hop(done[j][1], q) for j in before[k] if meets(j, done[j][2], k)] + [0.0])
                for step, d in steps:
                    t = room(step[0][0], t + (hop(q, step[0][0]) if at else 0), d)
                    at.append(t); t += d; q = step[0][0]
                score = max(t, late[k] - PAR["margin"]) + (tasks[k]["spare"][1] if len(way) > 1 else 0) + tasks[k]["spare"][0] * sum(d for step, d in steps if step[0][0] == "v")
                if steps[0][0][0][2][0] == "sws" and tasks[k]["pool"]:
                    score += PAR["sx"]
                if best is None or score < best[0] - 1e-9:
                    best = (score, steps, at, t, q, w)
            score, steps, at, t, q, w = best
            done[k] = (t, q, w) if back else (t + lag, "-" if lag else q, w)
            for (step, d), a in zip(steps, at):
                busy[step[0][0]] = sorted(busy[step[0][0]] + [(a, a + d)])
                placed.append([a, k, step])
            start[k] = at[0]
        span = max(d[0] for d in done.values())
        return [done[k][0] for k in range(len(tasks))], placed, [span - start[k] for k in range(len(tasks))]

    if PAR.get("lab"):
        chain = PAR["lab"](tasks, sweep, chain, before, behind, force)
    best, late = None, [0.0] * len(tasks)
    for turn in range(PAR["turns"]):
        ends, placed, early = sweep(chain, False, late)
        if (best is None or max(ends) < best[0]) if PAR["turn"] is None else turn == PAR["turn"]:
            best = (max(ends), placed)
        for k in range(len(tasks)):
            ends[k] = max([ends[k]] + [ends[j] + 1e-6 for j in before[k]])
        chain, _, late = sweep(ends, True, early)
        if PAR.get("hook"):
            chain = PAR["hook"](chain, before)
        for k in range(len(tasks) - 1, -1, -1):
            chain[k] = max([chain[k]] + [chain[j] + 1e-6 for j in behind[k]])
    span, placed = best
    placed.sort(key=lambda p: (p[0], p[1]))
    pools = {}
    for p in placed:
        if tasks[p[1]]["pool"]:
            pools.setdefault(tasks[p[1]]["pool"], []).append(p)
    for (make, m0, most), ps in pools.items():
        a = m0
        for q in "vs":
            mine = [p for p in placed if p[2] and p[2][0][0] == q]
            run = None
            for p in [p for p in ps if p[2] and p[2][0][0] == q]:
                n = elems(p[2][0][2]) // 16
                if run and mine[mine.index(p) - 1] is run[1] and a + n - run[2] <= most:
                    run[0][2] = [make(q, run[2], a + n)]
                    run[1] = p
                    run[3].append(p)
                else:
                    for x in (run[3] if run else []):
                        x[2] = []
                    p[2] = [make(q, a, a + n)]
                    run = [p, p, a, []]
                a += n
            for x in (run[3] if run else []):
                x[2] = []
    return [c for p in placed for c in p[2] if c[1] != "wire"], span


def mates(a, b):
    return a["pool"] and (a["pool"] == b["pool"] or any(r[0] == "swv" for r in a["wr"]) and any(r[0] == "swv" for r in b["wr"]))


CALLS = []


def rank_program(g, core, T, topo):
    rank = T.rank_of(core)
    if rank is None:
        return
    if not CALLS:
        CALLS.extend(order(plan())[0])
    cores = T.cores
    qh = {"v": g.vector, "s": g.scalar, "t": g.tensor, "g": g, "y": g.sync}
    qsem = {"v": "sv", "s": "ss", "t": "st", "g": "sg"}
    fns = {"copy": g.vector.tensor_copy, "tt": g.vector.tensor_tensor, "ts": g.vector.tensor_scalar, "scan": g.vector.tensor_tensor_scan,
           "memset": g.vector.memset, "rec": g.vector.reciprocal, "act": g.scalar.activation, "mm": g.tensor.matmul,
           "iota": g.iota, "asel": g.affine_select}
    cnt = {}
    know = {q: {} for q in qh}
    clocks = {}
    acc = {}

    def conflicts(q, regs, write):
        out = []
        for name, c0, c1 in regs:
            for a0, a1, w, aq, tok in acc.get(name, []):
                if name in PSB:
                    if aq != q or (q != "t" and (w or write)):
                        out.append(tok)
                elif a0 < c1 and c0 < a1 and (w or write):
                    out.append(tok)
        return out

    def wait_for(q, toks):
        best = {}
        for s, v in toks:
            best[s] = max(best.get(s, 0), v)
        for s, v in sorted(best.items(), key=lambda t: -clocks[t][1]):
            if know[q].get(s, 0) >= v:
                continue
            qh[q].wait_ge(T.sem[s], v)
            for k, x in clocks[(s, v)][0].items():
                know[q][k] = max(know[q].get(k, 0), x)

    def note(q, reads, writes, tok):
        for regs, w in ((reads, False), (writes, True)):
            for name, c0, c1 in regs:
                lst = acc.get(name, [])
                if name in PSB:
                    lst = [a for a in lst if a[3] != q or (a[2] and not w)]
                elif w:
                    lst = [a for a in lst if not (c0 <= a[0] and a[1] <= c1)]
                else:
                    lst = [a for a in lst if a[2] or a[3] != q or not (c0 <= a[0] and a[1] <= c1)]
                acc[name] = lst + [(c0, c1, w, q, tok)]

    def token(q, sem, n):
        cnt[sem] = cnt.get(sem, 0) + n
        c = dict(know[q]) if q is not None else {}
        c[sem] = cnt[sem]
        clocks[(sem, cnt[sem])] = (c, len(clocks))
        return (sem, cnt[sem])

    def ap(x):
        if not isinstance(x, tuple):
            return x
        a = T[x[0]][:, x[1]:x[2]:x[3]] if x[3] != 1 else T[x[0]][:, x[1]:x[2]]
        return a.indirect(ap(x[4])) if x[4] else a

    lan = lanes(core, cores, topo)
    coming = sum(len(lanes(c, cores, topo)[core]) for c in cores if c != core)
    arrived = {}
    for call in CALLS:
        q, fn, out, ins, kw = call
        reads, writes = touched(call)
        if fn == "send":
            wait_for("g", conflicts("g", reads, False))
            tr = []
            for d in range(1, N):
                dst = cores[(rank + d) % N] if out[0] != "f" else cores[(rank - d) % N]
                rid, pid = topo.addr(dst, core)
                name, c0 = landing(out, d)
                tr.append(RemoteDMATransfer(dst_ids=[DstId(rid=rid, pnc=pid)], dma_engine_mask=sum(1 << e for e in lan[dst]),
                                            remote_sem=T.sem["arr_" + out], src=T["msg_" + out][:, (d - 1) * GB:d * GB],
                                            dst=T[name][:, c0:c0 + GB]))
                cnt["snt"] = cnt.get("snt", 0) + len(lan[dst])
            g.remote_dma_fused(tr, local_sem=T.sem.snt)
            arrived[out] = token(None, "arr_" + out, coming)
            note("net", [], writes, arrived[out])
            continue
        toks = conflicts(q, reads, False) + conflicts(q, writes, True)
        if fn == "dma":
            hold = {"dz0": None if PAR["dz"] else "x", "dz1": "x", "dz2": "x", "dcd1": "x", "dya": "x", "dyb": "y0", "oy3": "y3", "oy2": "y2", "oy1": "y1", "dc2": "y3", "dc1": "y2"}.get(out)
            wait_for(q, toks + ([arrived[hold]] if hold else []))
            side = lambda x: T[x[0]][x[1], x[2]:x[3]]
            qh[q].dma_start(side(ins[0]), side(ins[1])).then_inc(T.sem[out], 16)
            note(q + "dma", reads, writes, token(q, out, 16))
            continue
        wait_for(q, toks)
        if fn == "iota" and SCRATCH[out[0]][2] != I32:
            kw = dict(allow_small_or_imprecise_dtypes=True)
        fns[fn](ap(out), *[ap(x) for x in ins], **{k: ap(x) for k, x in kw.items()}).then_inc(T.sem[qsem[q]], 1)
        note(q, reads, writes, token(q, qsem[q], 1))
    for sname in SEMAPHORES:
        if cnt.get(sname, 0) and know["g"].get(sname, 0) < cnt[sname]:
            g.wait_ge(T.sem[sname], cnt[sname])
